import numpy as np
import ml_dtypes


def mxq(x, axis, fmt="e4m3"):
    dtype, down = {"e4m3": (ml_dtypes.float8_e4m3fn, 7), "e5m2": (ml_dtypes.float8_e5m2, 14)}[fmt]
    v = np.moveaxis(np.asarray(x, np.float32).astype(ml_dtypes.bfloat16).astype(np.float64), axis, -1)
    blocks = v.reshape(v.shape[:-1] + (-1, 32))
    amax = np.abs(blocks).max(-1, keepdims=True)
    byte = np.maximum(np.where(amax > 0, np.frexp(amax)[1] - 1 + 127, 0) - down, 1)
    scale = np.exp2(byte - 127.0)
    codes = (blocks / scale).astype(np.float32).astype(dtype).astype(np.float64)
    return np.moveaxis((codes * scale).reshape(v.shape), -1, axis)


WIDE = False


def mx_kscale(k):
    if not WIDE:
        return np.ones(k)
    levels = np.array([24, -24, 12, -12, 0])
    if k % 512:
        return np.exp2(np.random.permutation(np.resize(levels, k // 32))).repeat(32)
    a = np.empty((k // 512, 16))
    for p in range(k // 512):
        a[p, :8] = np.random.permutation(np.resize(levels, 8))
        for g in range(8):
            far = levels[np.abs(levels - a[p, g]) >= 10]
            a[p, g + 8] = far[np.random.randint(len(far))]
    return np.exp2(a.ravel()).repeat(32)


def f64(x):
    return np.asarray(x).astype(np.float64)


def striped(idx):
    return np.tile(idx.reshape(-1, 16).T, (8, 1)).astype(np.uint16)


def unstriped(offs):
    return offs[:16].T.reshape(-1).astype(np.int64)


E2M1 = np.array([0.0, 0.5, 1.0, 1.5, 2.0, 3.0, 4.0, 6.0, -0.0, -0.5, -1.0, -1.5, -2.0, -3.0, -4.0, -6.0])


def pack_weight(w, fmt):
    k, n = w.shape
    w = f64(np.asarray(w, np.float32).astype(ml_dtypes.bfloat16)).reshape(k // 32, 32, n)
    amax = np.abs(w).max(1)
    if fmt == "e4m3":
        byte = np.frexp(amax)[1] - 1 + 127 - 7
    else:
        mant, ex = np.frexp(amax / 6.0)
        byte = np.where(mant > 0.5, ex, ex - 1) + 127
    byte = np.clip(np.where(amax > 0, byte, 1), 1, 254)
    scaled = (w * np.exp2(127.0 - byte)[:, None, :]).reshape(k, n).astype(np.float32)
    by_word = np.ascontiguousarray(scaled.reshape(k // 512, 128, 4, n).transpose(0, 1, 3, 2))
    if fmt == "e4m3":
        words = by_word.astype(ml_dtypes.float8_e4m3fn).view(np.uint8)
    else:
        c = by_word.astype(ml_dtypes.float4_e2m1fn).view(np.uint8) & 0xF
        words = (c[..., 0::2] | (c[..., 1::2] << 4)).reshape(k // 512, 128, 2 * n)
    return np.ascontiguousarray(words), np.ascontiguousarray(byte.astype(np.uint8).reshape(k // 512, 16, n))


def unpack_weight(words, scales, fmt):
    g, _, n = scales.shape
    words = np.ascontiguousarray(words).reshape(g, 128, n, -1)
    if fmt == "e4m3":
        vals = words.view(ml_dtypes.float8_e4m3fn).astype(np.float64)
    else:
        nib = np.empty((g, 128, n, 4), np.uint8)
        nib[..., 0::2] = words & 0xF
        nib[..., 1::2] = words >> 4
        vals = E2M1[nib]
    vals = vals * np.repeat(np.exp2(scales.astype(np.float64) - 127.0), 8, axis=1)[..., None]
    return vals.transpose(0, 1, 3, 2).reshape(g * 512, n)


def pack_table4(v):
    words, scales = pack_weight(v, "e2m1")
    g, t = words.shape[0] // 2, v.shape[1]
    return np.ascontiguousarray(words.reshape(g, 2, 128, t, 2).transpose(0, 2, 3, 1, 4).reshape(g, 128, t, 4)), scales


def unpack_table4(words, scales):
    g, _, t, _ = words.shape
    return unpack_weight(words.reshape(g, 128, t, 2, 2).transpose(0, 3, 1, 2, 4).reshape(2 * g, 128, 2 * t), scales, "e2m1")


def gelu(f):
    return 0.5 * f * (1.0 + np.tanh(np.sqrt(2.0 / np.pi) * (f + 0.044715 * f**3)))


K, L, R, N, T, J = 1024, 512, 1024, 1024, 4096, 2048


def setup_inputs():
    n = np.random.standard_normal
    s = mx_kscale(K)[:, None]
    s2 = mx_kscale(L)[:, None]
    u = mx_kscale(R)[:, None]
    p_tab = pack_table4(n((K, T)) * s)
    p_tab2 = pack_weight(n((L, T)) * s2, "e4m3")
    p_wb = pack_weight(n((L, R)) / np.sqrt(L) / s2, "e4m3")
    p_en = pack_weight(n((R, N)) / np.sqrt(R) / u, "e4m3")
    return {
        "tab_words": p_tab[0],
        "tab_scales": p_tab[1],
        "tab2_words": p_tab2[0],
        "tab2_scales": p_tab2[1],
        "wa": (n((K, R)) / np.sqrt(K) / s * u.T).astype(np.float32),
        "wb_words": p_wb[0],
        "wb_scales": p_wb[1],
        "en_words": p_en[0],
        "en_scales": p_en[1],
        "b": (0.3 * n(N)).astype(np.float32),
        "offs": striped(np.random.permutation(T)[:J]),
        "offs2": striped(np.random.permutation(T)[:J]),
    }


def reference(tab_words, tab_scales, tab2_words, tab2_scales, wa, wb_words, wb_scales, en_words, en_scales, b, offs, offs2):
    idx = unstriped(offs)
    idx2 = unstriped(offs2)
    tab_ = unpack_table4(tab_words, tab_scales)[:, idx]
    tab2_ = unpack_weight(tab2_words, tab2_scales, "e4m3")[:, idx2]
    wa_ = mxq(f64(wa), 0, "e4m3")
    wb_ = unpack_weight(wb_words, wb_scales, "e4m3")
    ha = wa_.T @ tab_
    hb = wb_.T @ tab2_
    h = ha * hb
    h_ = mxq(h, 0, "e4m3")
    en_ = unpack_weight(en_words, en_scales, "e4m3")
    y = en_.T @ h_
    return gelu(y + f64(b)[:, None])

@@ -1,0 +1,245 @@
+from contextlib import ExitStack
+
+import concourse.mybir as mybir
+
+K, L, R, N, T, J = 1024, 512, 1024, 1024, 4096, 2048
+FLOPS = 2 * J * (K * R + L * R + R * N)
+
+F32 = mybir.dt.float32
+BF16 = mybir.dt.bfloat16
+I32 = mybir.dt.int32
+U32 = mybir.dt.uint32
+U16 = mybir.dt.uint16
+U8 = mybir.dt.uint8
+FP8X4 = mybir.dt.float8_e4m3fn_x4
+FP4X4 = mybir.dt.float4_e2m1fn_x4
+MULT = mybir.AluOpType.mult
+GELU = mybir.ActivationFunctionType.Gelu_apprx_tanh
+
+P = 128
+PACK = 4
+PASS = P * PACK
+CHUNK = 512
+CHUNKS = J // CHUNK
+UNIT = 128
+LIST_COLS = CHUNK // 16
+SHIFT = 16
+
+
+def tile_list_kg_mul_gelu_kernel(
+    tc, tab_words, tab_scales, tab2_words, tab2_scales, wa, wb_words, wb_scales, en_words, en_scales, b, offs, offs2, out
+):
+    nc = tc.nc
+    with ExitStack() as ctx:
+        keep = ctx.enter_context(tc.tile_pool(name="keep", bufs=1))
+        ring = ctx.enter_context(tc.tile_pool(name="ring", bufs=2))
+        psum = ctx.enter_context(tc.psum_pool(name="psum", bufs=1))
+
+        def held(name, shape, dtype):
+            return keep.tile(shape, dtype, name=name, align_bytes=64)
+
+        list1 = keep.tile([P, J // 16], U16, name="list1")
+        list2 = keep.tile([P, J // 16], U16, name="list2")
+        tab_w = held("tab_w", [P, T], I32)
+        tab_s = held("tab_s", [P, T], U8)
+        tab2_w = held("tab2_w", [P, T], I32)
+        tab2_s = held("tab2_s", [P, T], U8)
+        wb_w = held("wb_w", [P, R], I32)
+        wb_s = held("wb_s", [P, R], U8)
+        en_w = held("en_w", [P, 2, N], I32)
+        en_s = held("en_s", [P, 2, N], U8)
+        bias = held("bias", [P, N // P], F32)
+        v_s0 = held("v_s0", [P, J], U8)
+        v_s1 = held("v_s1", [P, J], U8)
+        v_w = held("v_w", [P, CHUNKS, 2, 2 * CHUNK], U8)
+        v2_w = held("v2_w", [P, J], U32)
+        v2_s = held("v2_s", [P, J], U8)
+        wbp_w = held("wbp_w", [P, R], I32)
+        wbp_s = held("wbp_s", [P, R], U8)
+        wa_w = held("wa_w", [P, 2, R], U32)
+        wa_s = held("wa_s", [P, 2, R], U8)
+
+        def words(dram):
+            return dram.rearrange("p n i -> p (n i)").bitcast(I32)
+
+        def zero(plane):
+            nc.vector.memset(plane.bitcast(I32), 0)
+
+        def load_wa(a, h, c0, c1):
+            raw = keep.tile([P, PACK, c1 - c0], F32, name="wa_raw_%d_%d_%d" % (a, h, c0))
+            rows = wa[PASS * a : PASS * (a + 1), PASS * h + c0 : PASS * h + c1]
+            nc.sync.dma_start(out=raw[:], in_=rows.rearrange("(p j) c -> p j c", j=PACK))
+            return raw
+
+        zero(tab_s[:, : T // 2])
+        nc.gpsimd.memset(tab_s[:, T // 2 :].bitcast(I32), 0)
+        zero(v_s1[:])
+        zero(tab2_s[:])
+        zero(wb_s[:])
+        zero(en_s[:].rearrange("p a n -> p (a n)"))
+        nc.sync.dma_start(list1[:], offs)
+        nc.sync.dma_start(list2[:], offs2)
+        with nc.allow_non_contiguous_dma(reason="one bias value for each partition and output tile"):
+            nc.sync.dma_start(out=bias[:], in_=b.rearrange("(c p) -> p c", p=P))
+        by_row = tab_scales.rearrange("a (q r) t -> r q a t", r=4)
+        for r in range(4):
+            nc.sync.dma_start(out=tab_s[r:P:SHIFT, :].bitcast(I32), in_=by_row[r].bitcast(I32))
+        nc.sync.dma_start(out=tab_w[:], in_=words(tab_words[0]))
+        raw00 = load_wa(0, 0, 0, PASS)
+        raw10a = load_wa(1, 0, 0, PASS // 2)
+        raw10b = load_wa(1, 0, PASS // 2, PASS)
+        by_row2 = tab2_scales[0].rearrange("(q r) t -> r q t", r=4)
+        for r in range(4):
+            nc.sync.dma_start(out=tab2_s[r:P:32, :].bitcast(I32), in_=by_row2[r].bitcast(I32))
+        by_row_wb = wb_scales[0].rearrange("(q r) t -> r q t", r=4)
+        for r in range(4):
+            nc.sync.dma_start(out=wb_s[r:P:32, :].bitcast(I32), in_=by_row_wb[r].bitcast(I32))
+        raw01 = load_wa(0, 1, 0, PASS)
+        raw11 = load_wa(1, 1, 0, PASS)
+        nc.sync.dma_start(out=wb_w[:], in_=words(wb_words[0]))
+        nc.sync.dma_start(out=tab2_w[:], in_=words(tab2_words[0]))
+        by_row_en = en_scales.rearrange("a (q r) n -> r q a n", r=4)
+        for r in range(4):
+            nc.sync.dma_start(out=en_s[r:P:32, :, :].bitcast(I32), in_=by_row_en[r].bitcast(I32))
+        nc.sync.dma_start(out=en_w[:], in_=en_words.rearrange("a p n i -> p a (n i)").bitcast(I32))
+
+        def cols(c):
+            return slice(CHUNK * c, CHUNK * (c + 1))
+
+        def entries(lst, c):
+            return lst[:, LIST_COLS * c : LIST_COLS * (c + 1)]
+
+        def gather_tab(c):
+            both = ring.tile([P, CHUNK], U32, name="both", align_bytes=64)
+            nc.vector.tensor_copy(both[:], tab_w[:].bitcast(U32).indirect(entries(list1, c)))
+            nc.vector.tensor_copy(v_w[:, c, :, :].bitcast(U16), both[:].bitcast(U16).rearrange("p (j d) -> p d j", d=2))
+
+        def gather_tab2_scales(c):
+            nc.vector.tensor_copy(v2_s[:, cols(c)], tab2_s[:].indirect(entries(list2, c)))
+
+        def gather_tab2(c):
+            nc.vector.tensor_copy(v2_w[:, cols(c)], tab2_w[:].bitcast(U32).indirect(entries(list2, c)))
+
+        def round_wa(copy, grouped, raw, m0):
+            m1 = m0 + raw.shape[2] // PACK
+            copy(grouped[:, :, m0:m1, :].rearrange("p t m j -> p m j t"), raw[:].rearrange("p j (m t) -> p m j t", t=PACK))
+
+        def quantize_wa(a, h, grouped):
+            half = slice(PASS * h, PASS * (h + 1))
+            nc.vector.quantize_mx(
+                out=wa_w[:, a, half].bitcast(FP8X4), scales=wa_s[:, a, half], in_=grouped[:].rearrange("p t m j -> p (t m j)")
+            )
+
+        def new_grouped():
+            return ring.tile([P, PACK, P, PACK], BF16, name="grouped", align_bytes=64)
+
+        ha = {}
+
+        def make_ha(h, c):
+            sums = ring.tile([P, PACK, CHUNK], F32, name="ha", bufs=7, align_bytes=64)
+            for t in range(PACK):
+                m = slice(PASS * h + P * t, PASS * h + P * (t + 1))
+                bank = psum.tile([P, CHUNK], F32, name="wide_bank", bufs=5)
+                for a in range(2):
+                    nc.tensor.matmul_mx(
+                        out=bank[:],
+                        lhsT=wa_w[:, a, m].bitcast(FP8X4),
+                        lhsT_scale=wa_s[:, a, m],
+                        rhs=v_w[:, c, a, :].bitcast(FP4X4),
+                        rhs_scale=(v_s0, v_s1)[a][:, cols(c)],
+                        start=(a == 0),
+                        stop=(a == 1),
+                    )
+                nc.scalar.copy(sums[:, t, :], bank[:])
+            ha[h, c] = sums
+
+        hq = {}
+
+        def make_h(h, c):
+            rounded = ring.tile([P, CHUNK, PACK], BF16, name="rounded", bufs=3, align_bytes=64)
+            for u in range(CHUNK // UNIT):
+                q = slice(CHUNK * c + UNIT * u, CHUNK * c + UNIT * (u + 1))
+                bank = psum.tile([P, PACK, UNIT], F32, name="hb_bank", bufs=3)
+                for t in range(PACK):
+                    m = slice(PASS * h + P * t, PASS * h + P * (t + 1))
+                    nc.tensor.matmul_mx(
+                        out=bank[:, t, :],
+                        lhsT=wbp_w[:, m].bitcast(FP8X4),
+                        lhsT_scale=wbp_s[:, m],
+                        rhs=v2_w[:, q].bitcast(FP8X4),
+                        rhs_scale=v2_s[:, q],
+                        start=True,
+                        stop=True,
+                    )
+                within = slice(UNIT * u, UNIT * (u + 1))
+                nc.vector.tensor_tensor(
+                    rounded[:, within, :].rearrange("p (g i) t -> p g t i", i=2),
+                    bank[:].rearrange("p t (g i) -> p g t i", i=2),
+                    ha[h, c][:, :, within].rearrange("p t (g i) -> p g t i", i=2),
+                    MULT,
+                )
+            h_w = ring.tile([P, CHUNK], U32, name="h_w", bufs=5, align_bytes=64)
+            h_s = ring.tile([P, CHUNK], U8, name="h_s", bufs=5, align_bytes=64)
+            nc.vector.quantize_mx(out=h_w[:].bitcast(FP8X4), scales=h_s[:], in_=rounded[:].rearrange("p j t -> p (j t)"))
+            hq[h, c] = (h_w, h_s)
+
+        def make_out(c):
+            for n in range(N // P):
+                m = slice(P * n, P * (n + 1))
+                bank = psum.tile([P, CHUNK], F32, name="wide_bank", bufs=5)
+                for h in range(2):
+                    nc.tensor.matmul_mx(
+                        out=bank[:],
+                        lhsT=en_w[:, h, m].bitcast(FP8X4),
+                        lhsT_scale=en_s[:, h, m],
+                        rhs=hq[h, c][0][:].bitcast(FP8X4),
+                        rhs_scale=hq[h, c][1][:],
+                        start=(h == 0),
+                        stop=(h == 1),
+                    )
+                result = ring.tile([P, CHUNK], F32, name="result", bufs=6)
+                nc.scalar.activation(result[:], bank[:], GELU, bias=bias[:, n : n + 1])
+                nc.sync.dma_start(out=out[m, cols(c)], in_=result[:])
+
+        warm = held("warm", [P, 1], F32)
+        nc.scalar.activation(warm[:], bias[:, 0:1], GELU)
+        nc.vector.tensor_copy(v_s0[:], tab_s[:].indirect(list1[:]))
+        nc.scalar.dma_start(out=v_s1[0 : P - SHIFT, :].bitcast(I32), in_=v_s0[SHIFT:P, :].bitcast(I32))
+        gather_tab(0)
+        g00 = new_grouped()
+        round_wa(nc.scalar.copy, g00, raw00, 0)
+        g10 = new_grouped()
+        round_wa(nc.scalar.copy, g10, raw10a, 0)
+        round_wa(nc.vector.tensor_copy, g10, raw10b, P // 2)
+        quantize_wa(0, 0, g00)
+        quantize_wa(1, 0, g10)
+        g01 = new_grouped()
+        round_wa(nc.scalar.copy, g01, raw01, 0)
+        g11 = new_grouped()
+        round_wa(nc.scalar.copy, g11, raw11, 0)
+        quantize_wa(0, 1, g01)
+        quantize_wa(1, 1, g11)
+        make_ha(0, 0)
+        make_ha(1, 0)
+        gather_tab(1)
+        make_ha(0, 1)
+        make_ha(1, 1)
+        nc.vector.tensor_copy(
+            wbp_w[:].rearrange("p (h t m) -> p h m t", h=2, t=PACK), wb_w[:].rearrange("p (h m t) -> p h m t", h=2, t=PACK)
+        )
+        nc.vector.tensor_copy(
+            wbp_s[:].rearrange("p (h t m) -> p h t m", h=2, t=PACK), wb_s[:].rearrange("p (h m t) -> p h t m", h=2, t=PACK)
+        )
+        gather_tab2_scales(0)
+        gather_tab2(0)
+        for c in range(CHUNKS):
+            make_h(0, c)
+            make_h(1, c)
+            if c + 1 < CHUNKS:
+                gather_tab2_scales(c + 1)
+                gather_tab2(c + 1)
+            if c + 2 < CHUNKS:
+                gather_tab(c + 2)
+                make_ha(0, c + 2)
+                make_ha(1, c + 2)
+            make_out(c)

@@ -24,6 +24,8 @@ CHUNKS = J // CHUNK
 UNIT = 128
 LIST_COLS = CHUNK // 16
 SHIFT = 16
+BANKS = 8
+ALONE = 20
 
 
 def tile_list_kg_mul_gelu_kernel(
@@ -38,24 +40,17 @@ def tile_list_kg_mul_gelu_kernel(
         def held(name, shape, dtype):
             return keep.tile(shape, dtype, name=name, align_bytes=64)
 
+        def tenant(place, name, shape, dtype):
+            return keep.tile(shape, dtype, name=name, tag=place, align_bytes=64)
+
         list1 = keep.tile([P, J // 16], U16, name="list1")
         list2 = keep.tile([P, J // 16], U16, name="list2")
         tab_w = held("tab_w", [P, T], I32)
-        tab_s = held("tab_s", [P, T], U8)
-        tab2_w = held("tab2_w", [P, T], I32)
+        tab_s = tenant("a", "tab_s", [P, T], U8)
         tab2_s = held("tab2_s", [P, T], U8)
-        wb_w = held("wb_w", [P, R], I32)
-        wb_s = held("wb_s", [P, R], U8)
-        en_w = held("en_w", [P, 2, N], I32)
-        en_s = held("en_s", [P, 2, N], U8)
-        bias = held("bias", [P, N // P], F32)
         v_s0 = held("v_s0", [P, J], U8)
         v_s1 = held("v_s1", [P, J], U8)
         v_w = held("v_w", [P, CHUNKS, 2, 2 * CHUNK], U8)
-        v2_w = held("v2_w", [P, J], U32)
-        v2_s = held("v2_s", [P, J], U8)
-        wbp_w = held("wbp_w", [P, R], I32)
-        wbp_s = held("wbp_s", [P, R], U8)
         wa_w = held("wa_w", [P, 2, R], U32)
         wa_s = held("wa_s", [P, 2, R], U8)
 
@@ -65,43 +60,34 @@ def tile_list_kg_mul_gelu_kernel(
         def zero(plane):
             nc.vector.memset(plane.bitcast(I32), 0)
 
-        def load_wa(a, h, c0, c1):
-            raw = keep.tile([P, PACK, c1 - c0], F32, name="wa_raw_%d_%d_%d" % (a, h, c0))
-            rows = wa[PASS * a : PASS * (a + 1), PASS * h + c0 : PASS * h + c1]
-            nc.sync.dma_start(out=raw[:], in_=rows.rearrange("(p j) c -> p j c", j=PACK))
+        def wa_rows(a, h):
+            return wa[PASS * a : PASS * (a + 1), PASS * h : PASS * (h + 1)].rearrange("(p j) c -> p j c", j=PACK)
+
+        def load_wa(a, h, place):
+            raw = tenant(place, "wa_raw", [P, PACK, PASS], F32)
+            nc.sync.dma_start(out=raw[:], in_=wa_rows(a, h))
             return raw
 
-        zero(tab_s[:, : T // 2])
-        nc.gpsimd.memset(tab_s[:, T // 2 :].bitcast(I32), 0)
-        zero(v_s1[:])
+        def load_scales(plane, by_row, step):
+            for r in range(4):
+                nc.sync.dma_start(out=plane[r:P:step].bitcast(I32), in_=by_row[r].bitcast(I32))
+
+        zero(tab_s[:, : 3 * T // 4])
+        nc.gpsimd.memset(tab_s[:, 3 * T // 4 :].bitcast(I32), 0)
         zero(tab2_s[:])
-        zero(wb_s[:])
-        zero(en_s[:].rearrange("p a n -> p (a n)"))
+        zero(v_s1[:])
         nc.sync.dma_start(list1[:], offs)
         nc.sync.dma_start(list2[:], offs2)
-        with nc.allow_non_contiguous_dma(reason="one bias value for each partition and output tile"):
-            nc.sync.dma_start(out=bias[:], in_=b.rearrange("(c p) -> p c", p=P))
-        by_row = tab_scales.rearrange("a (q r) t -> r q a t", r=4)
-        for r in range(4):
-            nc.sync.dma_start(out=tab_s[r:P:SHIFT, :].bitcast(I32), in_=by_row[r].bitcast(I32))
+        raw00 = tenant("c", "wa_raw", [P, PACK, PASS], F32)
+        for c0 in (0, PASS // 2):
+            nc.sync.dma_start(out=raw00[:, 0, c0 : c0 + PASS // 2], in_=wa_rows(0, 0)[:, 0, c0 : c0 + PASS // 2])
+        load_scales(tab_s, tab_scales.rearrange("a (q r) t -> r q a t", r=4), SHIFT)
         nc.sync.dma_start(out=tab_w[:], in_=words(tab_words[0]))
-        raw00 = load_wa(0, 0, 0, PASS)
-        raw10a = load_wa(1, 0, 0, PASS // 2)
-        raw10b = load_wa(1, 0, PASS // 2, PASS)
-        by_row2 = tab2_scales[0].rearrange("(q r) t -> r q t", r=4)
-        for r in range(4):
-            nc.sync.dma_start(out=tab2_s[r:P:32, :].bitcast(I32), in_=by_row2[r].bitcast(I32))
-        by_row_wb = wb_scales[0].rearrange("(q r) t -> r q t", r=4)
-        for r in range(4):
-            nc.sync.dma_start(out=wb_s[r:P:32, :].bitcast(I32), in_=by_row_wb[r].bitcast(I32))
-        raw01 = load_wa(0, 1, 0, PASS)
-        raw11 = load_wa(1, 1, 0, PASS)
-        nc.sync.dma_start(out=wb_w[:], in_=words(wb_words[0]))
-        nc.sync.dma_start(out=tab2_w[:], in_=words(tab2_words[0]))
-        by_row_en = en_scales.rearrange("a (q r) n -> r q a n", r=4)
-        for r in range(4):
-            nc.sync.dma_start(out=en_s[r:P:32, :, :].bitcast(I32), in_=by_row_en[r].bitcast(I32))
-        nc.sync.dma_start(out=en_w[:], in_=en_words.rearrange("a p n i -> p a (n i)").bitcast(I32))
+        nc.sync.dma_start(out=raw00[:, 1:, :], in_=wa_rows(0, 0)[:, 1:, :])
+        raw10 = load_wa(1, 0, "e")
+        raw01 = load_wa(0, 1, "g")
+        raw11 = load_wa(1, 1, "b")
+        load_scales(tab2_s, tab2_scales[0].rearrange("(q r) t -> r q t", r=4), 32)
 
         def cols(c):
             return slice(CHUNK * c, CHUNK * (c + 1))
@@ -109,10 +95,9 @@ def tile_list_kg_mul_gelu_kernel(
         def entries(lst, c):
             return lst[:, LIST_COLS * c : LIST_COLS * (c + 1)]
 
-        def gather_tab(c):
-            both = ring.tile([P, CHUNK], U32, name="both", align_bytes=64)
-            nc.vector.tensor_copy(both[:], tab_w[:].bitcast(U32).indirect(entries(list1, c)))
-            nc.vector.tensor_copy(v_w[:, c, :, :].bitcast(U16), both[:].bitcast(U16).rearrange("p (j d) -> p d j", d=2))
+        def gather_tab(c, both):
+            nc.vector.tensor_copy(both, tab_w[:].bitcast(U32).indirect(entries(list1, c)))
+            nc.vector.tensor_copy(v_w[:, c, :, :].bitcast(U16), both.bitcast(U16).rearrange("p (j d) -> p d j", d=2))
 
         def gather_tab2_scales(c):
             nc.vector.tensor_copy(v2_s[:, cols(c)], tab2_s[:].indirect(entries(list2, c)))
@@ -120,9 +105,11 @@ def tile_list_kg_mul_gelu_kernel(
         def gather_tab2(c):
             nc.vector.tensor_copy(v2_w[:, cols(c)], tab2_w[:].bitcast(U32).indirect(entries(list2, c)))
 
-        def round_wa(copy, grouped, raw, m0):
-            m1 = m0 + raw.shape[2] // PACK
-            copy(grouped[:, :, m0:m1, :].rearrange("p t m j -> p m j t"), raw[:].rearrange("p j (m t) -> p m j t", t=PACK))
+        def round_wa(copy, grouped, raw, m0, m1):
+            copy(
+                grouped[:, :, m0:m1, :].rearrange("p t m j -> p m j t"),
+                raw[:, :, PACK * m0 : PACK * m1].rearrange("p j (m t) -> p m j t", t=PACK),
+            )
 
         def quantize_wa(a, h, grouped):
             half = slice(PASS * h, PASS * (h + 1))
@@ -130,116 +117,168 @@ def tile_list_kg_mul_gelu_kernel(
                 out=wa_w[:, a, half].bitcast(FP8X4), scales=wa_s[:, a, half], in_=grouped[:].rearrange("p t m j -> p (t m j)")
             )
 
-        def new_grouped():
-            return ring.tile([P, PACK, P, PACK], BF16, name="grouped", align_bytes=64)
+        def new_grouped(place):
+            return tenant(place, "grouped", [P, PACK, P, PACK], BF16)
+
+        made = []
+
+        def new_bank(shape):
+            made.append(shape)
+            return psum.tile(shape, F32, name="bank%d" % ((len(made) - 1) % BANKS))
+
+        def r_cols(h, t):
+            return slice(PASS * h + P * t, PASS * h + P * (t + 1))
+
+        def ha_pass(bank, h, c, t, a):
+            nc.tensor.matmul_mx(
+                out=bank[:],
+                lhsT=wa_w[:, a, r_cols(h, t)].bitcast(FP8X4),
+                lhsT_scale=wa_s[:, a, r_cols(h, t)],
+                rhs=v_w[:, c, a, :].bitcast(FP4X4),
+                rhs_scale=(v_s0, v_s1)[a][:, cols(c)],
+                start=(a == 0),
+                stop=(a == 1),
+            )
 
         ha = {}
 
-        def make_ha(h, c):
-            sums = ring.tile([P, PACK, CHUNK], F32, name="ha", bufs=7, align_bytes=64)
-            for t in range(PACK):
-                m = slice(PASS * h + P * t, PASS * h + P * (t + 1))
-                bank = psum.tile([P, CHUNK], F32, name="wide_bank", bufs=5)
-                for a in range(2):
-                    nc.tensor.matmul_mx(
-                        out=bank[:],
-                        lhsT=wa_w[:, a, m].bitcast(FP8X4),
-                        lhsT_scale=wa_s[:, a, m],
-                        rhs=v_w[:, c, a, :].bitcast(FP4X4),
-                        rhs_scale=(v_s0, v_s1)[a][:, cols(c)],
-                        start=(a == 0),
-                        stop=(a == 1),
-                    )
-                nc.scalar.copy(sums[:, t, :], bank[:])
-            ha[h, c] = sums
+        def make_ha(h, c, t):
+            if t == 0:
+                ha[h, c] = ring.tile([P, PACK, CHUNK], F32, name="ha", bufs=6, align_bytes=64)
+            bank = new_bank([P, CHUNK])
+            ha_pass(bank, h, c, t, 0)
+            ha_pass(bank, h, c, t, 1)
+            nc.scalar.copy(ha[h, c][:, t, :], bank[:])
 
+        rounded = {}
         hq = {}
 
-        def make_h(h, c):
-            rounded = ring.tile([P, CHUNK, PACK], BF16, name="rounded", bufs=3, align_bytes=64)
-            for u in range(CHUNK // UNIT):
-                q = slice(CHUNK * c + UNIT * u, CHUNK * c + UNIT * (u + 1))
-                bank = psum.tile([P, PACK, UNIT], F32, name="hb_bank", bufs=3)
-                for t in range(PACK):
-                    m = slice(PASS * h + P * t, PASS * h + P * (t + 1))
-                    nc.tensor.matmul_mx(
-                        out=bank[:, t, :],
-                        lhsT=wbp_w[:, m].bitcast(FP8X4),
-                        lhsT_scale=wbp_s[:, m],
-                        rhs=v2_w[:, q].bitcast(FP8X4),
-                        rhs_scale=v2_s[:, q],
-                        start=True,
-                        stop=True,
-                    )
-                within = slice(UNIT * u, UNIT * (u + 1))
-                nc.vector.tensor_tensor(
-                    rounded[:, within, :].rearrange("p (g i) t -> p g t i", i=2),
-                    bank[:].rearrange("p t (g i) -> p g t i", i=2),
-                    ha[h, c][:, :, within].rearrange("p t (g i) -> p g t i", i=2),
-                    MULT,
-                )
+        def quantize_h(h, c):
             h_w = ring.tile([P, CHUNK], U32, name="h_w", bufs=5, align_bytes=64)
             h_s = ring.tile([P, CHUNK], U8, name="h_s", bufs=5, align_bytes=64)
-            nc.vector.quantize_mx(out=h_w[:].bitcast(FP8X4), scales=h_s[:], in_=rounded[:].rearrange("p j t -> p (j t)"))
+            nc.vector.quantize_mx(out=h_w[:].bitcast(FP8X4), scales=h_s[:], in_=rounded[h, c][:].rearrange("p j t -> p (j t)"))
             hq[h, c] = (h_w, h_s)
 
-        def make_out(c):
-            for n in range(N // P):
-                m = slice(P * n, P * (n + 1))
-                bank = psum.tile([P, CHUNK], F32, name="wide_bank", bufs=5)
-                for h in range(2):
-                    nc.tensor.matmul_mx(
-                        out=bank[:],
-                        lhsT=en_w[:, h, m].bitcast(FP8X4),
-                        lhsT_scale=en_s[:, h, m],
-                        rhs=hq[h, c][0][:].bitcast(FP8X4),
-                        rhs_scale=hq[h, c][1][:],
-                        start=(h == 0),
-                        stop=(h == 1),
-                    )
-                result = ring.tile([P, CHUNK], F32, name="result", bufs=6)
-                nc.scalar.activation(result[:], bank[:], GELU, bias=bias[:, n : n + 1])
-                nc.sync.dma_start(out=out[m, cols(c)], in_=result[:])
+        def make_h(h, c, u):
+            if u == 0:
+                rounded[h, c] = ring.tile([P, CHUNK, PACK], BF16, name="rounded", bufs=3, align_bytes=64)
+            within = slice(UNIT * u, UNIT * (u + 1))
+            q = slice(CHUNK * c + UNIT * u, CHUNK * c + UNIT * (u + 1))
+            bank = new_bank([P, PACK, UNIT])
+            for t in range(PACK):
+                nc.tensor.matmul_mx(
+                    out=bank[:, t, :],
+                    lhsT=wbp[:, :R].bitcast(FP8X4)[:, r_cols(h, t)],
+                    lhsT_scale=wbp[:, R:].bitcast(U8)[:, r_cols(h, t)],
+                    rhs=v2_w[:, q].bitcast(FP8X4),
+                    rhs_scale=v2_s[:, q],
+                    start=True,
+                    stop=True,
+                )
+            nc.vector.tensor_tensor(
+                rounded[h, c][:, within, :].rearrange("p (g i) t -> p g t i", i=2),
+                bank[:].rearrange("p t (g i) -> p g t i", i=2),
+                ha[h, c][:, :, within].rearrange("p t (g i) -> p g t i", i=2),
+                MULT,
+            )
+
+        def make_out(c, n):
+            m = slice(P * n, P * (n + 1))
+            bank = new_bank([P, CHUNK])
+            for h in range(2):
+                nc.tensor.matmul_mx(
+                    out=bank[:],
+                    lhsT=en_w[:, h, m].bitcast(FP8X4),
+                    lhsT_scale=en_s[:, h, m],
+                    rhs=hq[h, c][0][:].bitcast(FP8X4),
+                    rhs_scale=hq[h, c][1][:],
+                    start=(h == 0),
+                    stop=(h == 1),
+                )
+            result = ring.tile([P, CHUNK], F32, name="result", bufs=6)
+            nc.scalar.activation(result[:], bank[:], GELU, bias=bias[:, n : n + 1])
+            nc.sync.dma_start(out=out[m, cols(c)], in_=result[:])
 
         warm = held("warm", [P, 1], F32)
-        nc.scalar.activation(warm[:], bias[:, 0:1], GELU)
+        nc.gpsimd.memset(warm[:], 0.0)
+        nc.scalar.activation(warm[:], warm[:], GELU)
+
         nc.vector.tensor_copy(v_s0[:], tab_s[:].indirect(list1[:]))
         nc.scalar.dma_start(out=v_s1[0 : P - SHIFT, :].bitcast(I32), in_=v_s0[SHIFT:P, :].bitcast(I32))
-        gather_tab(0)
-        g00 = new_grouped()
-        round_wa(nc.scalar.copy, g00, raw00, 0)
-        g10 = new_grouped()
-        round_wa(nc.scalar.copy, g10, raw10a, 0)
-        round_wa(nc.vector.tensor_copy, g10, raw10b, P // 2)
+        gather_tab(0, tenant("a", "both0", [P, CHUNK], U32)[:])
+        g00 = new_grouped("x")
+        round_wa(nc.scalar.copy, g00, raw00, 0, P // 2)
+        round_wa(nc.vector.tensor_copy, g00, raw00, P // 2, P)
         quantize_wa(0, 0, g00)
+        wb_s = tenant("a", "wb_s", [P, R], U8)
+        zero(wb_s[:])
+        load_scales(wb_s, wb_scales[0].rearrange("(q r) t -> r q t", r=4), 32)
+        wb_w = tenant("c", "wb_w", [P, R], I32)
+        nc.sync.dma_start(out=wb_w[:], in_=words(wb_words[0]))
+        both12 = tenant("x", "both12", [P, 2, CHUNK], U32)
+        gather_tab(1, both12[:, 0, :])
+        gather_tab(2, both12[:, 1, :])
+        g10 = new_grouped("y")
+        round_wa(nc.scalar.copy, g10, raw10, 0, P)
         quantize_wa(1, 0, g10)
-        g01 = new_grouped()
-        round_wa(nc.scalar.copy, g01, raw01, 0)
-        g11 = new_grouped()
-        round_wa(nc.scalar.copy, g11, raw11, 0)
+        tab2_w = tenant("e", "tab2_w", [P, T], I32)
+        nc.sync.dma_start(out=tab2_w[:], in_=words(tab2_words[0]))
+        gather_tab(3, tenant("y", "both3", [P, CHUNK], U32)[:])
+        en_s = tenant("y", "en_s", [P, 2, N], U8)
+        zero(en_s[:].rearrange("p a n -> p (a n)"))
+        load_scales(en_s, en_scales.rearrange("a (q r) n -> r q a n", r=4), 32)
+        g01 = new_grouped("z")
+        round_wa(nc.scalar.copy, g01, raw01, 0, P)
+        g11 = new_grouped("w")
+        round_wa(nc.scalar.copy, g11, raw11, 0, P)
+        en_w = tenant("g", "en_w", [P, 2, N], I32)
+        nc.sync.dma_start(out=en_w[:], in_=en_words.rearrange("a p n i -> p a (n i)").bitcast(I32))
         quantize_wa(0, 1, g01)
         quantize_wa(1, 1, g11)
-        make_ha(0, 0)
-        make_ha(1, 0)
-        gather_tab(1)
-        make_ha(0, 1)
-        make_ha(1, 1)
-        nc.vector.tensor_copy(
-            wbp_w[:].rearrange("p (h t m) -> p h m t", h=2, t=PACK), wb_w[:].rearrange("p (h m t) -> p h m t", h=2, t=PACK)
-        )
-        nc.vector.tensor_copy(
-            wbp_s[:].rearrange("p (h t m) -> p h t m", h=2, t=PACK), wb_s[:].rearrange("p (h m t) -> p h t m", h=2, t=PACK)
-        )
+
+        v2_s = tenant("z", "v2_s", [P, J], U8)
         gather_tab2_scales(0)
+        wbp = tenant("w", "wbp", [P, R + R // 4], I32)
+        nc.vector.tensor_copy(
+            wbp[:, :R].rearrange("p (h t m) -> p h m t", h=2, t=PACK), wb_w[:].rearrange("p (h m t) -> p h m t", h=2, t=PACK)
+        )
+        nc.vector.tensor_copy(
+            wbp[:, R:].bitcast(U8).rearrange("p (h t m) -> p h t m", h=2, t=PACK),
+            wb_s[:].rearrange("p (h m t) -> p h t m", h=2, t=PACK),
+        )
+        bias = tenant("a", "bias", [P, N // P], F32)
+        with nc.allow_non_contiguous_dma(reason="one bias value for each partition and output tile"):
+            nc.sync.dma_start(out=bias[:], in_=b.rearrange("(c p) -> p c", p=P))
+        v2_w = tenant("c", "v2_w", [P, J], U32)
+        gather_tab2_scales(1)
+        gather_tab2_scales(2)
         gather_tab2(0)
-        for c in range(CHUNKS):
-            make_h(0, c)
-            make_h(1, c)
-            if c + 1 < CHUNKS:
-                gather_tab2_scales(c + 1)
-                gather_tab2(c + 1)
-            if c + 2 < CHUNKS:
-                gather_tab(c + 2)
-                make_ha(0, c + 2)
-                make_ha(1, c + 2)
-            make_out(c)
+        gather_tab2_scales(3)
+        for c in range(1, CHUNKS):
+            gather_tab2(c)
+
+        first = tenant("b", "ha_first", [P, 2, PACK, CHUNK], F32)
+        opened = [(c, t, new_bank([P, CHUNK])) for c in range(2) for t in range(PACK)]
+        for c, t, bank in opened:
+            ha_pass(bank, 0, c, t, 0)
+        for c, t, bank in opened:
+            ha_pass(bank, 0, c, t, 1)
+            nc.scalar.copy(first[:, c, t, :], bank[:])
+        ha[0, 0] = first[:, 0]
+        ha[0, 1] = first[:, 1]
+
+        wide = [(make_ha, (h, c, t)) for h, c in ((1, 0), (1, 1), (0, 2), (1, 2), (0, 3), (1, 3)) for t in range(PACK)]
+        wide += [(make_out, (c, n)) for c in range(CHUNKS) for n in range(N // P)]
+        units = [(h, c, u) for c in range(CHUNKS) for h in range(2) for u in range(CHUNK // UNIT)]
+        for make, args in wide[: ALONE - BANKS]:
+            make(*args)
+        wide = wide[ALONE - BANKS :]
+        for i, (h, c, u) in enumerate(units):
+            make_h(h, c, u)
+            if u == 0 and i > 0:
+                quantize_h(*units[i - 1][:2])
+            make, args = wide[i]
+            make(*args)
+        quantize_h(*units[-1][:2])
+        for make, args in wide[len(units) :]:
+            make(*args)

@@ -47,7 +47,6 @@ def tile_list_kg_mul_gelu_kernel(
         list2 = keep.tile([P, J // 16], U16, name="list2")
         tab_w = held("tab_w", [P, T], I32)
         tab_s = tenant("a", "tab_s", [P, T], U8)
-        tab2_s = held("tab2_s", [P, T], U8)
         v_s0 = held("v_s0", [P, J], U8)
         v_s1 = held("v_s1", [P, J], U8)
         v_w = held("v_w", [P, CHUNKS, 2, 2 * CHUNK], U8)
@@ -74,20 +73,16 @@ def tile_list_kg_mul_gelu_kernel(
 
         zero(tab_s[:, : 3 * T // 4])
         nc.gpsimd.memset(tab_s[:, 3 * T // 4 :].bitcast(I32), 0)
-        zero(tab2_s[:])
         zero(v_s1[:])
         nc.sync.dma_start(list1[:], offs)
         nc.sync.dma_start(list2[:], offs2)
         raw00 = tenant("c", "wa_raw", [P, PACK, PASS], F32)
-        for c0 in (0, PASS // 2):
-            nc.sync.dma_start(out=raw00[:, 0, c0 : c0 + PASS // 2], in_=wa_rows(0, 0)[:, 0, c0 : c0 + PASS // 2])
+        nc.sync.dma_start(out=raw00[:, 0, :], in_=wa_rows(0, 0)[:, 0, :])
         load_scales(tab_s, tab_scales.rearrange("a (q r) t -> r q a t", r=4), SHIFT)
         nc.sync.dma_start(out=tab_w[:], in_=words(tab_words[0]))
         nc.sync.dma_start(out=raw00[:, 1:, :], in_=wa_rows(0, 0)[:, 1:, :])
         raw10 = load_wa(1, 0, "e")
         raw01 = load_wa(0, 1, "g")
-        raw11 = load_wa(1, 1, "b")
-        load_scales(tab2_s, tab2_scales[0].rearrange("(q r) t -> r q t", r=4), 32)
 
         def cols(c):
             return slice(CHUNK * c, CHUNK * (c + 1))
@@ -204,60 +199,68 @@ def tile_list_kg_mul_gelu_kernel(
         nc.scalar.activation(warm[:], warm[:], GELU)
 
         nc.vector.tensor_copy(v_s0[:], tab_s[:].indirect(list1[:]))
-        nc.scalar.dma_start(out=v_s1[0 : P - SHIFT, :].bitcast(I32), in_=v_s0[SHIFT:P, :].bitcast(I32))
-        gather_tab(0, tenant("a", "both0", [P, CHUNK], U32)[:])
+        nc.sync.dma_start(out=v_s1[0 : P - SHIFT, :].bitcast(I32), in_=v_s0[SHIFT:P, :].bitcast(I32))
+        raw11 = load_wa(1, 1, "a")
+        gather_tab(0, held("both0", [P, CHUNK], U32)[:])
         g00 = new_grouped("x")
         round_wa(nc.scalar.copy, g00, raw00, 0, P // 2)
         round_wa(nc.vector.tensor_copy, g00, raw00, P // 2, P)
         quantize_wa(0, 0, g00)
-        wb_s = tenant("a", "wb_s", [P, R], U8)
-        zero(wb_s[:])
-        load_scales(wb_s, wb_scales[0].rearrange("(q r) t -> r q t", r=4), 32)
-        wb_w = tenant("c", "wb_w", [P, R], I32)
-        nc.sync.dma_start(out=wb_w[:], in_=words(wb_words[0]))
+        wb = tenant("c", "wb", [P, R + R // 4], I32)
+        wb_w = wb[:, :R]
+        wb_s = wb[:, R:].bitcast(U8)
+        nc.vector.memset(wb[:, R:], 0)
+        by_row = wb_scales[0].rearrange("(q r) t -> r q t", r=4)
+        for r in range(4):
+            nc.sync.dma_start(out=wb[r:P:32, R:], in_=by_row[r].bitcast(I32))
+        nc.sync.dma_start(out=wb_w, in_=words(wb_words[0]))
         both12 = tenant("x", "both12", [P, 2, CHUNK], U32)
         gather_tab(1, both12[:, 0, :])
         gather_tab(2, both12[:, 1, :])
         g10 = new_grouped("y")
         round_wa(nc.scalar.copy, g10, raw10, 0, P)
         quantize_wa(1, 0, g10)
-        tab2_w = tenant("e", "tab2_w", [P, T], I32)
-        nc.sync.dma_start(out=tab2_w[:], in_=words(tab2_words[0]))
+        tab2_s = tenant("e", "tab2_s", [P, T], U8)
+        zero(tab2_s[:])
+        load_scales(tab2_s, tab2_scales[0].rearrange("(q r) t -> r q t", r=4), 32)
         gather_tab(3, tenant("y", "both3", [P, CHUNK], U32)[:])
-        en_s = tenant("y", "en_s", [P, 2, N], U8)
-        zero(en_s[:].rearrange("p a n -> p (a n)"))
-        load_scales(en_s, en_scales.rearrange("a (q r) n -> r q a n", r=4), 32)
+        tab2_w = tenant("y", "tab2_w", [P, T], I32)
+        nc.sync.dma_start(out=tab2_w[:], in_=words(tab2_words[0]))
         g01 = new_grouped("z")
         round_wa(nc.scalar.copy, g01, raw01, 0, P)
         g11 = new_grouped("w")
         round_wa(nc.scalar.copy, g11, raw11, 0, P)
-        en_w = tenant("g", "en_w", [P, 2, N], I32)
-        nc.sync.dma_start(out=en_w[:], in_=en_words.rearrange("a p n i -> p a (n i)").bitcast(I32))
         quantize_wa(0, 1, g01)
         quantize_wa(1, 1, g11)
+        en = tenant("z", "en", [P, 2, N + N // 4], I32)
+        en_w = en[:, :, :N]
+        en_s = en[:, :, N:].bitcast(U8)
+        nc.sync.dma_start(out=en_w, in_=en_words.rearrange("a p n i -> p a (n i)").bitcast(I32))
+        nc.vector.memset(en[:, :, N:], 0)
+        by_row = en_scales.rearrange("a (q r) n -> r q a n", r=4)
+        for r in range(4):
+            nc.sync.dma_start(out=en[r:P:32, :, N:], in_=by_row[r].bitcast(I32))
 
-        v2_s = tenant("z", "v2_s", [P, J], U8)
+        v2_s = tenant("w", "v2_s", [P, J], U8)
         gather_tab2_scales(0)
-        wbp = tenant("w", "wbp", [P, R + R // 4], I32)
+        wbp = tenant("g", "wbp", [P, R + R // 4], I32)
         nc.vector.tensor_copy(
-            wbp[:, :R].rearrange("p (h t m) -> p h m t", h=2, t=PACK), wb_w[:].rearrange("p (h m t) -> p h m t", h=2, t=PACK)
+            wbp[:, :R].rearrange("p (h t m) -> p h m t", h=2, t=PACK), wb_w.rearrange("p (h m t) -> p h m t", h=2, t=PACK)
         )
         nc.vector.tensor_copy(
             wbp[:, R:].bitcast(U8).rearrange("p (h t m) -> p h t m", h=2, t=PACK),
-            wb_s[:].rearrange("p (h m t) -> p h t m", h=2, t=PACK),
+            wb_s.rearrange("p (h m t) -> p h t m", h=2, t=PACK),
         )
-        bias = tenant("a", "bias", [P, N // P], F32)
+        v2_w = tenant("c", "v2_w", [P, J], U32)
+        for c in range(1, CHUNKS):
+            gather_tab2_scales(c)
+        bias = tenant("e", "bias", [P, N // P], F32)
         with nc.allow_non_contiguous_dma(reason="one bias value for each partition and output tile"):
             nc.sync.dma_start(out=bias[:], in_=b.rearrange("(c p) -> p c", p=P))
-        v2_w = tenant("c", "v2_w", [P, J], U32)
-        gather_tab2_scales(1)
-        gather_tab2_scales(2)
-        gather_tab2(0)
-        gather_tab2_scales(3)
-        for c in range(1, CHUNKS):
+        for c in range(CHUNKS):
             gather_tab2(c)
 
-        first = tenant("b", "ha_first", [P, 2, PACK, CHUNK], F32)
+        first = tenant("a", "ha_first", [P, 2, PACK, CHUNK], F32)
         opened = [(c, t, new_bank([P, CHUNK])) for c in range(2) for t in range(PACK)]
         for c, t, bank in opened:
             ha_pass(bank, 0, c, t, 0)

@@ -25,7 +25,7 @@ UNIT = 128
 LIST_COLS = CHUNK // 16
 SHIFT = 16
 BANKS = 8
-ALONE = 20
+ALONE = 24
 
 
 def tile_list_kg_mul_gelu_kernel(
@@ -194,10 +194,6 @@ def tile_list_kg_mul_gelu_kernel(
             nc.scalar.activation(result[:], bank[:], GELU, bias=bias[:, n : n + 1])
             nc.sync.dma_start(out=out[m, cols(c)], in_=result[:])
 
-        warm = held("warm", [P, 1], F32)
-        nc.gpsimd.memset(warm[:], 0.0)
-        nc.scalar.activation(warm[:], warm[:], GELU)
-
         nc.vector.tensor_copy(v_s0[:], tab_s[:].indirect(list1[:]))
         nc.sync.dma_start(out=v_s1[0 : P - SHIFT, :].bitcast(I32), in_=v_s0[SHIFT:P, :].bitcast(I32))
         raw11 = load_wa(1, 1, "a")
@@ -229,7 +225,7 @@ def tile_list_kg_mul_gelu_kernel(
         g01 = new_grouped("z")
         round_wa(nc.scalar.copy, g01, raw01, 0, P)
         g11 = new_grouped("w")
-        round_wa(nc.scalar.copy, g11, raw11, 0, P)
+        round_wa(nc.vector.tensor_copy, g11, raw11, 0, P)
         quantize_wa(0, 1, g01)
         quantize_wa(1, 1, g11)
         en = tenant("z", "en", [P, 2, N + N // 4], I32)
@@ -243,7 +239,7 @@ def tile_list_kg_mul_gelu_kernel(
 
         v2_s = tenant("w", "v2_s", [P, J], U8)
         gather_tab2_scales(0)
-        wbp = tenant("g", "wbp", [P, R + R // 4], I32)
+        wbp = tenant("a", "wbp", [P, R + R // 4], I32)
         nc.vector.tensor_copy(
             wbp[:, :R].rearrange("p (h t m) -> p h m t", h=2, t=PACK), wb_w.rearrange("p (h m t) -> p h m t", h=2, t=PACK)
         )
@@ -257,10 +253,10 @@ def tile_list_kg_mul_gelu_kernel(
         bias = tenant("e", "bias", [P, N // P], F32)
         with nc.allow_non_contiguous_dma(reason="one bias value for each partition and output tile"):
             nc.sync.dma_start(out=bias[:], in_=b.rearrange("(c p) -> p c", p=P))
-        for c in range(CHUNKS):
-            gather_tab2(c)
+        gather_tab2(0)
+        gather_tab2(1)
 
-        first = tenant("a", "ha_first", [P, 2, PACK, CHUNK], F32)
+        first = tenant("g", "ha_first", [P, 2, PACK, CHUNK], F32)
         opened = [(c, t, new_bank([P, CHUNK])) for c in range(2) for t in range(PACK)]
         for c, t, bank in opened:
             ha_pass(bank, 0, c, t, 0)
@@ -270,18 +266,21 @@ def tile_list_kg_mul_gelu_kernel(
         ha[0, 0] = first[:, 0]
         ha[0, 1] = first[:, 1]
 
-        wide = [(make_ha, (h, c, t)) for h, c in ((1, 0), (1, 1), (0, 2), (1, 2), (0, 3), (1, 3)) for t in range(PACK)]
+        wide = [(make_ha, (h, c, t)) for h, c in ((0, 2), (1, 0), (1, 1), (1, 2), (0, 3), (1, 3)) for t in range(PACK)]
         wide += [(make_out, (c, n)) for c in range(CHUNKS) for n in range(N // P)]
         units = [(h, c, u) for c in range(CHUNKS) for h in range(2) for u in range(CHUNK // UNIT)]
         for make, args in wide[: ALONE - BANKS]:
             make(*args)
         wide = wide[ALONE - BANKS :]
         for i, (h, c, u) in enumerate(units):
+            if (h, u) == (0, 0) and 1 <= c < CHUNKS - 1:
+                gather_tab2(c + 1)
             make_h(h, c, u)
             if u == 0 and i > 0:
                 quantize_h(*units[i - 1][:2])
-            make, args = wide[i]
-            make(*args)
+            if wide[0][0] is make_out or i % 3 != 1:
+                make, args = wide.pop(0)
+                make(*args)
         quantize_h(*units[-1][:2])
-        for make, args in wide[len(units) :]:
+        for make, args in wide:
             make(*args)

@@ -25,7 +25,15 @@ UNIT = 128
 LIST_COLS = CHUNK // 16
 SHIFT = 16
 BANKS = 8
-ALONE = 24
+ALONE = 23
+SCALES_AT = 2
+WORDS_AT = 5
+RING = 3
+FQ = 1
+FG = 1
+ODD = 1
+LEAD = 2
+WIDTHS = (256,) * 8
 
 
 def tile_list_kg_mul_gelu_kernel(
@@ -47,6 +55,7 @@ def tile_list_kg_mul_gelu_kernel(
         list2 = keep.tile([P, J // 16], U16, name="list2")
         tab_w = held("tab_w", [P, T], I32)
         tab_s = tenant("a", "tab_s", [P, T], U8)
+        tab2_s = held("tab2_s", [P, T], U8)
         v_s0 = held("v_s0", [P, J], U8)
         v_s1 = held("v_s1", [P, J], U8)
         v_w = held("v_w", [P, CHUNKS, 2, 2 * CHUNK], U8)
@@ -62,27 +71,30 @@ def tile_list_kg_mul_gelu_kernel(
         def wa_rows(a, h):
             return wa[PASS * a : PASS * (a + 1), PASS * h : PASS * (h + 1)].rearrange("(p j) c -> p j c", j=PACK)
 
-        def load_wa(a, h, place):
-            raw = tenant(place, "wa_raw", [P, PACK, PASS], F32)
-            nc.sync.dma_start(out=raw[:], in_=wa_rows(a, h))
-            return raw
-
         def load_scales(plane, by_row, step):
             for r in range(4):
                 nc.sync.dma_start(out=plane[r:P:step].bitcast(I32), in_=by_row[r].bitcast(I32))
 
         zero(tab_s[:, : 3 * T // 4])
         nc.gpsimd.memset(tab_s[:, 3 * T // 4 :].bitcast(I32), 0)
+        zero(tab2_s[:])
         zero(v_s1[:])
-        nc.sync.dma_start(list1[:], offs)
-        nc.sync.dma_start(list2[:], offs2)
+        warm = held("warm", [P, 2], F32)
+        nc.gpsimd.memset(warm[:, 0:1], 0.0)
+        nc.scalar.activation(warm[:, 1:2], warm[:, 0:1], GELU)
         raw00 = tenant("c", "wa_raw", [P, PACK, PASS], F32)
-        nc.sync.dma_start(out=raw00[:, 0, :], in_=wa_rows(0, 0)[:, 0, :])
+        raw10 = [tenant("e%d" % i, "wa_raw", [P, PACK, PASS // 2], F32) for i in range(2)]
+        nc.sync.dma_start(list1[:], offs)
+        for j in range(2):
+            nc.sync.dma_start(out=raw00[:, j, :], in_=wa_rows(0, 0)[:, j, :])
         load_scales(tab_s, tab_scales.rearrange("a (q r) t -> r q a t", r=4), SHIFT)
+        nc.sync.dma_start(out=raw00[:, 2:, :], in_=wa_rows(0, 0)[:, 2:, :])
         nc.sync.dma_start(out=tab_w[:], in_=words(tab_words[0]))
-        nc.sync.dma_start(out=raw00[:, 1:, :], in_=wa_rows(0, 0)[:, 1:, :])
-        raw10 = load_wa(1, 0, "e")
-        raw01 = load_wa(0, 1, "g")
+        for i in range(2):
+            nc.sync.dma_start(out=raw10[i][:], in_=wa_rows(1, 0)[:, :, PASS // 2 * i : PASS // 2 * (i + 1)])
+
+        nc.sync.dma_start(list2[:], offs2)
+        load_scales(tab2_s, tab2_scales[0].rearrange("(q r) t -> r q t", r=4), 32)
 
         def cols(c):
             return slice(CHUNK * c, CHUNK * (c + 1))
@@ -92,19 +104,26 @@ def tile_list_kg_mul_gelu_kernel(
 
         def gather_tab(c, both):
             nc.vector.tensor_copy(both, tab_w[:].bitcast(U32).indirect(entries(list1, c)))
-            nc.vector.tensor_copy(v_w[:, c, :, :].bitcast(U16), both.bitcast(U16).rearrange("p (j d) -> p d j", d=2))
 
-        def gather_tab2_scales(c):
-            nc.vector.tensor_copy(v2_s[:, cols(c)], tab2_s[:].indirect(entries(list2, c)))
-
-        def gather_tab2(c):
-            nc.vector.tensor_copy(v2_w[:, cols(c)], tab2_w[:].bitcast(U32).indirect(entries(list2, c)))
-
-        def round_wa(copy, grouped, raw, m0, m1):
-            copy(
-                grouped[:, :, m0:m1, :].rearrange("p t m j -> p m j t"),
-                raw[:, :, PACK * m0 : PACK * m1].rearrange("p j (m t) -> p m j t", t=PACK),
+        def part_tab(c, both, passes):
+            nc.vector.tensor_copy(
+                v_w[:, c, passes, :].bitcast(U16), both.bitcast(U16).rearrange("p (j d) -> p d j", d=2)[:, passes, :]
             )
+
+        v2_s = {}
+
+        def gather_tab2_scales(c, place):
+            v2_s[c] = tenant(place, "v2_s", [P, CHUNK], U8)
+            nc.vector.tensor_copy(v2_s[c][:], tab2_s[:].indirect(entries(list2, c)))
+
+        v2_w = {}
+
+        def gather_tab2(c, place):
+            v2_w[c] = tenant(place, "v2_w", [P, CHUNK], U32)
+            nc.vector.tensor_copy(v2_w[c][:], tab2_w[:].bitcast(U32).indirect(entries(list2, c)))
+
+        def round_wa(copy, grouped, raw):
+            copy(grouped.rearrange("p t m j -> p m j t"), raw.rearrange("p j (m t) -> p m j t", t=PACK))
 
         def quantize_wa(a, h, grouped):
             half = slice(PASS * h, PASS * (h + 1))
@@ -115,11 +134,14 @@ def tile_list_kg_mul_gelu_kernel(
         def new_grouped(place):
             return tenant(place, "grouped", [P, PACK, P, PACK], BF16)
 
-        made = []
+        banks = [psum.tile([P, CHUNK], F32, name="bank%d" % i) for i in range(BANKS)]
+        emptied = [(i, "scalar") for i in range(BANKS)]
 
-        def new_bank(shape):
-            made.append(shape)
-            return psum.tile(shape, F32, name="bank%d" % ((len(made) - 1) % BANKS))
+        def new_bank(shape, after):
+            pick = ([entry for entry in emptied if entry[1] == after] + emptied)[0]
+            emptied.remove(pick)
+            bank = banks[pick[0]][:]
+            return pick[0], bank if len(shape) == 2 else bank.rearrange("p (a b) -> p a b", a=shape[1])
 
         def r_cols(h, t):
             return slice(PASS * h + P * t, PASS * h + P * (t + 1))
@@ -139,148 +161,183 @@ def tile_list_kg_mul_gelu_kernel(
 
         def make_ha(h, c, t):
             if t == 0:
-                ha[h, c] = ring.tile([P, PACK, CHUNK], F32, name="ha", bufs=6, align_bytes=64)
-            bank = new_bank([P, CHUNK])
+                ha[h, c] = tenant("ha%d%d" % (h, c), "ha", [P, PACK, CHUNK], F32)
+            place, bank = new_bank([P, CHUNK], "vector")
             ha_pass(bank, h, c, t, 0)
             ha_pass(bank, h, c, t, 1)
             nc.scalar.copy(ha[h, c][:, t, :], bank[:])
+            emptied.append((place, "scalar"))
 
         rounded = {}
         hq = {}
 
-        def quantize_h(h, c):
-            h_w = ring.tile([P, CHUNK], U32, name="h_w", bufs=5, align_bytes=64)
-            h_s = ring.tile([P, CHUNK], U8, name="h_s", bufs=5, align_bytes=64)
-            nc.vector.quantize_mx(out=h_w[:].bitcast(FP8X4), scales=h_s[:], in_=rounded[h, c][:].rearrange("p j t -> p (j t)"))
-            hq[h, c] = (h_w, h_s)
+        def quantize_h(h, q0, width):
+            h_w = ring.tile([P, width], U32, name="h_w", bufs=5, align_bytes=64)
+            h_s = ring.tile([P, width], U8, name="h_s", bufs=5, align_bytes=64)
+            nc.vector.quantize_mx(out=h_w[:].bitcast(FP8X4), scales=h_s[:], in_=rounded[h, q0][:].rearrange("p j t -> p (j t)"))
+            hq[h, q0] = (h_w, h_s)
 
-        def make_h(h, c, u):
-            if u == 0:
-                rounded[h, c] = ring.tile([P, CHUNK, PACK], BF16, name="rounded", bufs=3, align_bytes=64)
-            within = slice(UNIT * u, UNIT * (u + 1))
-            q = slice(CHUNK * c + UNIT * u, CHUNK * c + UNIT * (u + 1))
-            bank = new_bank([P, PACK, UNIT])
+        hb = {}
+
+        def make_hb(h, q0, width, u):
+            c, at = divmod(q0 + UNIT * u, CHUNK)
+            within = slice(at, at + UNIT)
+            place, bank = new_bank([P, PACK, UNIT], "scalar")
+            hb[h, q0, u] = (place, bank)
             for t in range(PACK):
                 nc.tensor.matmul_mx(
                     out=bank[:, t, :],
-                    lhsT=wbp[:, :R].bitcast(FP8X4)[:, r_cols(h, t)],
-                    lhsT_scale=wbp[:, R:].bitcast(U8)[:, r_cols(h, t)],
-                    rhs=v2_w[:, q].bitcast(FP8X4),
-                    rhs_scale=v2_s[:, q],
+                    lhsT=wbp_w[:, r_cols(h, t)].bitcast(FP8X4),
+                    lhsT_scale=wbp_s[:, r_cols(h, t)],
+                    rhs=v2_w[c][:, within].bitcast(FP8X4),
+                    rhs_scale=v2_s[c][:, within],
                     start=True,
                     stop=True,
                 )
+
+        def make_h(h, q0, width, u):
+            if u == 0 and h == 0 and q0 % CHUNK == 0:
+                rounded[h, q0] = tenant("first%d" % (q0 // CHUNK % 2), "rounded", [P, width, PACK], BF16)
+            elif u == 0:
+                rounded[h, q0] = ring.tile([P, width, PACK], BF16, name="rounded", bufs=RING, align_bytes=64)
+            c, at = divmod(q0 + UNIT * u, CHUNK)
+            within = slice(at, at + UNIT)
+            place, bank = hb[h, q0, u]
+            emptied.append((place, "vector"))
             nc.vector.tensor_tensor(
-                rounded[h, c][:, within, :].rearrange("p (g i) t -> p g t i", i=2),
+                rounded[h, q0][:, UNIT * u : UNIT * (u + 1), :].rearrange("p (g i) t -> p g t i", i=2),
                 bank[:].rearrange("p t (g i) -> p g t i", i=2),
                 ha[h, c][:, :, within].rearrange("p t (g i) -> p g t i", i=2),
                 MULT,
             )
 
-        def make_out(c, n):
-            m = slice(P * n, P * (n + 1))
-            bank = new_bank([P, CHUNK])
-            for h in range(2):
-                nc.tensor.matmul_mx(
-                    out=bank[:],
-                    lhsT=en_w[:, h, m].bitcast(FP8X4),
-                    lhsT_scale=en_s[:, h, m],
-                    rhs=hq[h, c][0][:].bitcast(FP8X4),
-                    rhs_scale=hq[h, c][1][:],
-                    start=(h == 0),
-                    stop=(h == 1),
-                )
-            result = ring.tile([P, CHUNK], F32, name="result", bufs=6)
-            nc.scalar.activation(result[:], bank[:], GELU, bias=bias[:, n : n + 1])
-            nc.sync.dma_start(out=out[m, cols(c)], in_=result[:])
+        def make_out(q0, width, n0):
+            tiles = CHUNK // width
+            place, bank = new_bank([P, tiles, width], "vector")
+            emptied.append((place, "scalar"))
+            result = ring.tile([P, tiles, width], F32, name="result", bufs=6)
+            for i in range(tiles):
+                n = n0 + i
+                for h in range(2):
+                    nc.tensor.matmul_mx(
+                        out=bank[:, i, :],
+                        lhsT=en_w[:, h, P * n : P * (n + 1)].bitcast(FP8X4),
+                        lhsT_scale=en_s[4 * h :, P * n : P * (n + 1)],
+                        rhs=hq[h, q0][0][:].bitcast(FP8X4),
+                        rhs_scale=hq[h, q0][1][:],
+                        start=(h == 0),
+                        stop=(h == 1),
+                    )
+            for i in range(tiles):
+                nc.scalar.activation(result[:, i, :], bank[:, i, :], GELU, bias=bias[:, n0 + i : n0 + i + 1])
+            nc.sync.dma_start(
+                out=out[P * n0 : P * (n0 + tiles), q0 : q0 + width].rearrange("(i p) j -> p i j", p=P), in_=result[:]
+            )
 
         nc.vector.tensor_copy(v_s0[:], tab_s[:].indirect(list1[:]))
         nc.sync.dma_start(out=v_s1[0 : P - SHIFT, :].bitcast(I32), in_=v_s0[SHIFT:P, :].bitcast(I32))
-        raw11 = load_wa(1, 1, "a")
-        gather_tab(0, held("both0", [P, CHUNK], U32)[:])
+        late = tenant("a", "wa_late", [P, 2, PACK, PASS], F32)
+        for a in range(2):
+            nc.sync.dma_start(out=late[:, a], in_=wa_rows(a, 1))
+
         g00 = new_grouped("x")
-        round_wa(nc.scalar.copy, g00, raw00, 0, P // 2)
-        round_wa(nc.vector.tensor_copy, g00, raw00, P // 2, P)
+        round_wa(nc.scalar.copy, g00[:], raw00[:])
         quantize_wa(0, 0, g00)
         wb = tenant("c", "wb", [P, R + R // 4], I32)
         wb_w = wb[:, :R]
         wb_s = wb[:, R:].bitcast(U8)
-        nc.vector.memset(wb[:, R:], 0)
-        by_row = wb_scales[0].rearrange("(q r) t -> r q t", r=4)
-        for r in range(4):
-            nc.sync.dma_start(out=wb[r:P:32, R:], in_=by_row[r].bitcast(I32))
+        nc.gpsimd.memset(wb[:, R:], 0)
+        load_scales(wb_s, wb_scales[0].rearrange("(q r) t -> r q t", r=4), 32)
         nc.sync.dma_start(out=wb_w, in_=words(wb_words[0]))
-        both12 = tenant("x", "both12", [P, 2, CHUNK], U32)
-        gather_tab(1, both12[:, 0, :])
-        gather_tab(2, both12[:, 1, :])
-        g10 = new_grouped("y")
-        round_wa(nc.scalar.copy, g10, raw10, 0, P)
-        quantize_wa(1, 0, g10)
-        tab2_s = tenant("e", "tab2_s", [P, T], U8)
-        zero(tab2_s[:])
-        load_scales(tab2_s, tab2_scales[0].rearrange("(q r) t -> r q t", r=4), 32)
-        gather_tab(3, tenant("y", "both3", [P, CHUNK], U32)[:])
-        tab2_w = tenant("y", "tab2_w", [P, T], I32)
+        tab2_w = tenant("x", "tab2_w", [P, T], I32)
         nc.sync.dma_start(out=tab2_w[:], in_=words(tab2_words[0]))
-        g01 = new_grouped("z")
-        round_wa(nc.scalar.copy, g01, raw01, 0, P)
-        g11 = new_grouped("w")
-        round_wa(nc.vector.tensor_copy, g11, raw11, 0, P)
-        quantize_wa(0, 1, g01)
-        quantize_wa(1, 1, g11)
-        en = tenant("z", "en", [P, 2, N + N // 4], I32)
-        en_w = en[:, :, :N]
-        en_s = en[:, :, N:].bitcast(U8)
+        for c in range(2):
+            both = tenant("b", "both", [P, CHUNK], U32)
+            gather_tab(c, both[:])
+            part_tab(c, both[:], slice(0, 1))
+            part_tab(c, both[:], slice(1, 2))
+        g10 = new_grouped("y")
+        for i in range(2):
+            round_wa(nc.scalar.copy, g10[:, :, P // 2 * i : P // 2 * (i + 1), :], raw10[i][:])
+        quantize_wa(1, 0, g10)
+        en = tenant("e0", "en", [P, 2 * N + N // 4], I32)
+        en_w = en[:, : 2 * N].rearrange("p (a n) -> p a n", a=2)
+        en_s = en[:, 2 * N :].bitcast(U8)
         nc.sync.dma_start(out=en_w, in_=en_words.rearrange("a p n i -> p a (n i)").bitcast(I32))
-        nc.vector.memset(en[:, :, N:], 0)
-        by_row = en_scales.rearrange("a (q r) n -> r q a n", r=4)
-        for r in range(4):
-            nc.sync.dma_start(out=en[r:P:32, :, N:], in_=by_row[r].bitcast(I32))
-
-        v2_s = tenant("w", "v2_s", [P, J], U8)
-        gather_tab2_scales(0)
-        wbp = tenant("a", "wbp", [P, R + R // 4], I32)
-        nc.vector.tensor_copy(
-            wbp[:, :R].rearrange("p (h t m) -> p h m t", h=2, t=PACK), wb_w.rearrange("p (h m t) -> p h m t", h=2, t=PACK)
-        )
-        nc.vector.tensor_copy(
-            wbp[:, R:].bitcast(U8).rearrange("p (h t m) -> p h t m", h=2, t=PACK),
-            wb_s.rearrange("p (h m t) -> p h t m", h=2, t=PACK),
-        )
-        v2_w = tenant("c", "v2_w", [P, J], U32)
-        for c in range(1, CHUNKS):
-            gather_tab2_scales(c)
-        bias = tenant("e", "bias", [P, N // P], F32)
+        nc.gpsimd.memset(en[:, 2 * N :], 0)
+        for q in range(4):
+            nc.sync.dma_start(out=en[32 * q : 32 * q + 8, 2 * N :], in_=en_scales[:, 4 * q : 4 * q + 4, :].bitcast(I32))
+        bias = tenant("b", "bias", [P, N // P], F32)
         with nc.allow_non_contiguous_dma(reason="one bias value for each partition and output tile"):
             nc.sync.dma_start(out=bias[:], in_=b.rearrange("(c p) -> p c", p=P))
-        gather_tab2(0)
-        gather_tab2(1)
+        both2 = tenant("y", "both2", [P, CHUNK], U32)
+        gather_tab(2, both2[:])
+        part_tab(2, both2[:], slice(0, 2))
+        g01 = new_grouped("z")
+        round_wa(nc.vector.tensor_copy, g01[:], late[:, 0])
+        both3 = tenant("y", "both3", [P, CHUNK], U32)
+        gather_tab(3, both3[:])
+        quantize_wa(0, 1, g01)
+        part_tab(3, both3[:], slice(0, 2))
+        g11 = new_grouped("w")
+        round_wa(nc.vector.tensor_copy, g11[:], late[:, 1])
+        wbp_w = tenant("e1", "wbp_w", [P, R], I32)
+        wbp_s = held("wbp_s", [P, R], U8)
+        nc.vector.tensor_copy(
+            wbp_s[:].rearrange("p (h t m) -> p h t m", h=2, t=PACK), wb_s.rearrange("p (h m t) -> p h t m", h=2, t=PACK)
+        )
+        quantize_wa(1, 1, g11)
+        nc.vector.tensor_copy(
+            wbp_w[:].rearrange("p (h t m) -> p h m t", h=2, t=PACK), wb_w.rearrange("p (h m t) -> p h m t", h=2, t=PACK)
+        )
+        gather_tab2_scales(0, "w")
+        gather_tab2(0, "z")
 
-        first = tenant("g", "ha_first", [P, 2, PACK, CHUNK], F32)
-        opened = [(c, t, new_bank([P, CHUNK])) for c in range(2) for t in range(PACK)]
-        for c, t, bank in opened:
+        opened = [(c, t) + new_bank([P, CHUNK], "scalar") for c in range(2) for t in range(PACK)]
+        for c, t, place, bank in opened:
             ha_pass(bank, 0, c, t, 0)
-        for c, t, bank in opened:
+        for c, t, place, bank in opened:
+            emptied.append((place, "scalar"))
+            if t == 0:
+                ha[0, c] = tenant("ha0%d" % c, "ha", [P, PACK, CHUNK], F32)
             ha_pass(bank, 0, c, t, 1)
-            nc.scalar.copy(first[:, c, t, :], bank[:])
-        ha[0, 0] = first[:, 0]
-        ha[0, 1] = first[:, 1]
+            nc.scalar.copy(ha[0, c][:, t, :], bank[:])
 
-        wide = [(make_ha, (h, c, t)) for h, c in ((0, 2), (1, 0), (1, 1), (1, 2), (0, 3), (1, 3)) for t in range(PACK)]
-        wide += [(make_out, (c, n)) for c in range(CHUNKS) for n in range(N // P)]
-        units = [(h, c, u) for c in range(CHUNKS) for h in range(2) for u in range(CHUNK // UNIT)]
+        wide = [(make_ha, (h, c, t)) for h, c in ((0, 2), (0, 3), (1, 0), (1, 1), (1, 2), (1, 3)) for t in range(PACK)]
         for make, args in wide[: ALONE - BANKS]:
             make(*args)
         wide = wide[ALONE - BANKS :]
-        for i, (h, c, u) in enumerate(units):
-            if (h, u) == (0, 0) and 1 <= c < CHUNKS - 1:
-                gather_tab2(c + 1)
-            make_h(h, c, u)
-            if u == 0 and i > 0:
-                quantize_h(*units[i - 1][:2])
-            if wide[0][0] is make_out or i % 3 != 1:
-                make, args = wide.pop(0)
+        pieces = [(sum(WIDTHS[:i]), w) for i, w in enumerate(WIDTHS)]
+        units = [(h, q0, w, u) for q0, w in pieces for h in range(2) for u in range(w // UNIT)]
+
+        def fill(count):
+            for make, args in wide[:count]:
                 make(*args)
-        quantize_h(*units[-1][:2])
-        for make, args in wide:
-            make(*args)
+            wide[:count] = []
+
+        def scores(h, q0, w, u):
+            return [(make_out, (q0, w, n)) for n in range(0, N // P, CHUNK // w)]
+
+        for unit in units[:LEAD]:
+            make_hb(*unit)
+        for i, (h, q0, w, u) in enumerate(units):
+            c, place = divmod(i, 2 * CHUNK // UNIT)
+            make_h(h, q0, w, u)
+            if i + LEAD < len(units):
+                make_hb(*units[i + LEAD])
+            if u == 0 and i > 0:
+                fill(FQ)
+                quantize_h(*units[i - 1][:3])
+                if h == 0:
+                    wide.extend(scores(*units[i - 1]))
+            if c + 1 < CHUNKS and place == SCALES_AT:
+                gather_tab2_scales(c + 1, "first%d" % (c % 2))
+                fill(FG)
+            if c + 1 < CHUNKS and place == WORDS_AT:
+                gather_tab2(c + 1, "ha0%d" % c)
+                fill(FG)
+            if i % 2 == ODD:
+                fill(1)
+        quantize_h(*units[-1][:3])
+        wide.extend(scores(*units[-1]))
+        fill(len(wide))

@@ -24,16 +24,21 @@ CHUNKS = J // CHUNK
 UNIT = 128
 LIST_COLS = CHUNK // 16
 SHIFT = 16
+SPLIT = 2
+AHEAD = 4
+TAB2_ROW = 4
+WB_ROW = 8
 BANKS = 8
-ALONE = 23
-SCALES_AT = 2
-WORDS_AT = 5
-RING = 3
+FRESH = 1
+ALONE = 25
+SCALES_AT = 6
+WORDS_AT = 4
+RING = 2
 FQ = 1
-FG = 1
+FG = (1, 2, 2, 0)
 ODD = 1
 LEAD = 2
-WIDTHS = (256,) * 8
+WIDTHS = (512,) * 4
 
 
 def tile_list_kg_mul_gelu_kernel(
@@ -58,7 +63,7 @@ def tile_list_kg_mul_gelu_kernel(
         tab2_s = held("tab2_s", [P, T], U8)
         v_s0 = held("v_s0", [P, J], U8)
         v_s1 = held("v_s1", [P, J], U8)
-        v_w = held("v_w", [P, CHUNKS, 2, 2 * CHUNK], U8)
+        v_w = {}
         wa_w = held("wa_w", [P, 2, R], U32)
         wa_s = held("wa_s", [P, 2, R], U8)
 
@@ -71,9 +76,9 @@ def tile_list_kg_mul_gelu_kernel(
         def wa_rows(a, h):
             return wa[PASS * a : PASS * (a + 1), PASS * h : PASS * (h + 1)].rearrange("(p j) c -> p j c", j=PACK)
 
-        def load_scales(plane, by_row, step):
+        def load_scales(queue, plane, by_row, step):
             for r in range(4):
-                nc.sync.dma_start(out=plane[r:P:step].bitcast(I32), in_=by_row[r].bitcast(I32))
+                queue.dma_start(out=plane[r::step].bitcast(I32), in_=by_row[r].bitcast(I32))
 
         zero(tab_s[:, : 3 * T // 4])
         nc.gpsimd.memset(tab_s[:, 3 * T // 4 :].bitcast(I32), 0)
@@ -82,19 +87,18 @@ def tile_list_kg_mul_gelu_kernel(
         warm = held("warm", [P, 2], F32)
         nc.gpsimd.memset(warm[:, 0:1], 0.0)
         nc.scalar.activation(warm[:, 1:2], warm[:, 0:1], GELU)
-        raw00 = tenant("c", "wa_raw", [P, PACK, PASS], F32)
+        raw00 = tenant("c1", "wa_raw", [P, PACK, PASS], F32)
         raw10 = [tenant("e%d" % i, "wa_raw", [P, PACK, PASS // 2], F32) for i in range(2)]
         nc.sync.dma_start(list1[:], offs)
-        for j in range(2):
-            nc.sync.dma_start(out=raw00[:, j, :], in_=wa_rows(0, 0)[:, j, :])
-        load_scales(tab_s, tab_scales.rearrange("a (q r) t -> r q a t", r=4), SHIFT)
-        nc.sync.dma_start(out=raw00[:, 2:, :], in_=wa_rows(0, 0)[:, 2:, :])
+        nc.sync.dma_start(list2[:], offs2)
+        nc.sync.dma_start(out=raw00[:, :1, :], in_=wa_rows(0, 0)[:, :1, :])
+        load_scales(nc.sync, tab_s[:], tab_scales.rearrange("a (q r) t -> r q a t", r=4), SHIFT)
+        nc.sync.dma_start(out=raw00[:, 1:, :], in_=wa_rows(0, 0)[:, 1:, :])
         nc.sync.dma_start(out=tab_w[:], in_=words(tab_words[0]))
         for i in range(2):
             nc.sync.dma_start(out=raw10[i][:], in_=wa_rows(1, 0)[:, :, PASS // 2 * i : PASS // 2 * (i + 1)])
 
-        nc.sync.dma_start(list2[:], offs2)
-        load_scales(tab2_s, tab2_scales[0].rearrange("(q r) t -> r q t", r=4), 32)
+        load_scales(nc.gpsimd, tab2_s[TAB2_ROW:], tab2_scales[0].rearrange("(q r) t -> r q t", r=4), 32)
 
         def cols(c):
             return slice(CHUNK * c, CHUNK * (c + 1))
@@ -105,10 +109,10 @@ def tile_list_kg_mul_gelu_kernel(
         def gather_tab(c, both):
             nc.vector.tensor_copy(both, tab_w[:].bitcast(U32).indirect(entries(list1, c)))
 
-        def part_tab(c, both, passes):
-            nc.vector.tensor_copy(
-                v_w[:, c, passes, :].bitcast(U16), both.bitcast(U16).rearrange("p (j d) -> p d j", d=2)[:, passes, :]
-            )
+        def part_tab(c, both, passes, parted):
+            nc.vector.tensor_copy(parted.bitcast(U16), both.bitcast(U16).rearrange("p (j d) -> p d j", d=2)[:, passes, :])
+            for a in range(passes.start, passes.stop):
+                v_w[c, a] = parted[:, a - passes.start, :]
 
         v2_s = {}
 
@@ -137,8 +141,17 @@ def tile_list_kg_mul_gelu_kernel(
         banks = [psum.tile([P, CHUNK], F32, name="bank%d" % i) for i in range(BANKS)]
         emptied = [(i, "scalar") for i in range(BANKS)]
 
+        tied = set()
+
+        def free_for(after):
+            if after == "scalar":
+                first = [entry for entry in emptied if entry[0] not in tied]
+                return first + [entry for entry in emptied if entry[1] == after] + emptied
+            usable = [entry for entry in emptied if entry[0] in tied or not hb]
+            return [entry for entry in usable[: len(usable) - FRESH] if entry[1] == after] + usable
+
         def new_bank(shape, after):
-            pick = ([entry for entry in emptied if entry[1] == after] + emptied)[0]
+            pick = free_for(after)[0]
             emptied.remove(pick)
             bank = banks[pick[0]][:]
             return pick[0], bank if len(shape) == 2 else bank.rearrange("p (a b) -> p a b", a=shape[1])
@@ -151,13 +164,14 @@ def tile_list_kg_mul_gelu_kernel(
                 out=bank[:],
                 lhsT=wa_w[:, a, r_cols(h, t)].bitcast(FP8X4),
                 lhsT_scale=wa_s[:, a, r_cols(h, t)],
-                rhs=v_w[:, c, a, :].bitcast(FP4X4),
+                rhs=v_w[c, a].bitcast(FP4X4),
                 rhs_scale=(v_s0, v_s1)[a][:, cols(c)],
                 start=(a == 0),
                 stop=(a == 1),
             )
 
         ha = {}
+        hb = {}
 
         def make_ha(h, c, t):
             if t == 0:
@@ -177,8 +191,6 @@ def tile_list_kg_mul_gelu_kernel(
             nc.vector.quantize_mx(out=h_w[:].bitcast(FP8X4), scales=h_s[:], in_=rounded[h, q0][:].rearrange("p j t -> p (j t)"))
             hq[h, q0] = (h_w, h_s)
 
-        hb = {}
-
         def make_hb(h, q0, width, u):
             c, at = divmod(q0 + UNIT * u, CHUNK)
             within = slice(at, at + UNIT)
@@ -188,9 +200,9 @@ def tile_list_kg_mul_gelu_kernel(
                 nc.tensor.matmul_mx(
                     out=bank[:, t, :],
                     lhsT=wbp_w[:, r_cols(h, t)].bitcast(FP8X4),
-                    lhsT_scale=wbp_s[:, r_cols(h, t)],
+                    lhsT_scale=wbp_s[WB_ROW:, r_cols(h, t)],
                     rhs=v2_w[c][:, within].bitcast(FP8X4),
-                    rhs_scale=v2_s[c][:, within],
+                    rhs_scale=v2_s[c][TAB2_ROW:, within],
                     start=True,
                     stop=True,
                 )
@@ -204,10 +216,11 @@ def tile_list_kg_mul_gelu_kernel(
             within = slice(at, at + UNIT)
             place, bank = hb[h, q0, u]
             emptied.append((place, "vector"))
+            tied.add(place)
             nc.vector.tensor_tensor(
-                rounded[h, q0][:, UNIT * u : UNIT * (u + 1), :].rearrange("p (g i) t -> p g t i", i=2),
-                bank[:].rearrange("p t (g i) -> p g t i", i=2),
-                ha[h, c][:, :, within].rearrange("p t (g i) -> p g t i", i=2),
+                rounded[h, q0][:, UNIT * u : UNIT * (u + 1), :].rearrange("p (g i) t -> p g t i", i=4),
+                bank[:].rearrange("p t (g i) -> p g t i", i=4),
+                ha[h, c][:, :, within].rearrange("p t (g i) -> p g t i", i=4),
                 MULT,
             )
 
@@ -236,52 +249,59 @@ def tile_list_kg_mul_gelu_kernel(
 
         nc.vector.tensor_copy(v_s0[:], tab_s[:].indirect(list1[:]))
         nc.sync.dma_start(out=v_s1[0 : P - SHIFT, :].bitcast(I32), in_=v_s0[SHIFT:P, :].bitcast(I32))
-        late = tenant("a", "wa_late", [P, 2, PACK, PASS], F32)
-        for a in range(2):
-            nc.sync.dma_start(out=late[:, a], in_=wa_rows(a, 1))
+        raw01 = tenant("a", "wa_raw", [P, PACK, PASS], F32)
+        for i in range(SPLIT):
+            part = slice(PASS // SPLIT * i, PASS // SPLIT * (i + 1))
+            nc.sync.dma_start(out=raw01[:, :, part], in_=wa_rows(0, 1)[:, :, part])
 
+        gather_tab2_scales(0, "s0")
         g00 = new_grouped("x")
         round_wa(nc.scalar.copy, g00[:], raw00[:])
         quantize_wa(0, 0, g00)
-        wb = tenant("c", "wb", [P, R + R // 4], I32)
-        wb_w = wb[:, :R]
-        wb_s = wb[:, R:].bitcast(U8)
-        nc.gpsimd.memset(wb[:, R:], 0)
-        load_scales(wb_s, wb_scales[0].rearrange("(q r) t -> r q t", r=4), 32)
-        nc.sync.dma_start(out=wb_w, in_=words(wb_words[0]))
-        tab2_w = tenant("x", "tab2_w", [P, T], I32)
-        nc.sync.dma_start(out=tab2_w[:], in_=words(tab2_words[0]))
+        raw11 = tenant("c1", "wa_raw", [P, PACK, PASS], F32)
+        nc.sync.dma_start(out=raw11[:], in_=wa_rows(1, 1))
         for c in range(2):
             both = tenant("b", "both", [P, CHUNK], U32)
+            parted = held("v_w%d" % c, [P, 2, 2 * CHUNK], U8)
             gather_tab(c, both[:])
-            part_tab(c, both[:], slice(0, 1))
-            part_tab(c, both[:], slice(1, 2))
+            for a in range(2):
+                part_tab(c, both[:], slice(a, a + 1), parted[:, a : a + 1, :])
+        wb = tenant("x", "wb", [P, R + R // 4], I32)
+        wb_w = wb[:, :R]
+        wb_s = wb[:, R:].bitcast(U8)
+        nc.vector.memset(wb[:, R:], 0)
+        load_scales(nc.sync, wb_s[WB_ROW:], wb_scales[0].rearrange("(q r) t -> r q t", r=4), 32)
+        nc.sync.dma_start(out=wb_w, in_=words(wb_words[0]))
         g10 = new_grouped("y")
         for i in range(2):
             round_wa(nc.scalar.copy, g10[:, :, P // 2 * i : P // 2 * (i + 1), :], raw10[i][:])
         quantize_wa(1, 0, g10)
-        en = tenant("e0", "en", [P, 2 * N + N // 4], I32)
+        both2 = tenant("y", "both2", [P, CHUNK], U32)
+        gather_tab(2, both2[:])
+        part_tab(2, both2[:], slice(0, 2), held("v_w2", [P, 2, 2 * CHUNK], U8)[:])
+        tab2_w = tenant("e0", "tab2_w", [P, T], I32)
+        nc.sync.dma_start(out=tab2_w[:], in_=words(tab2_words[0]))
+        en = tenant("e1", "en", [P, 2 * N + N // 4], I32)
         en_w = en[:, : 2 * N].rearrange("p (a n) -> p a n", a=2)
         en_s = en[:, 2 * N :].bitcast(U8)
         nc.sync.dma_start(out=en_w, in_=en_words.rearrange("a p n i -> p a (n i)").bitcast(I32))
-        nc.gpsimd.memset(en[:, 2 * N :], 0)
+        nc.vector.memset(en[:, 2 * N :], 0)
         for q in range(4):
             nc.sync.dma_start(out=en[32 * q : 32 * q + 8, 2 * N :], in_=en_scales[:, 4 * q : 4 * q + 4, :].bitcast(I32))
         bias = tenant("b", "bias", [P, N // P], F32)
         with nc.allow_non_contiguous_dma(reason="one bias value for each partition and output tile"):
             nc.sync.dma_start(out=bias[:], in_=b.rearrange("(c p) -> p c", p=P))
-        both2 = tenant("y", "both2", [P, CHUNK], U32)
-        gather_tab(2, both2[:])
-        part_tab(2, both2[:], slice(0, 2))
         g01 = new_grouped("z")
-        round_wa(nc.vector.tensor_copy, g01[:], late[:, 0])
+        for i in range(SPLIT):
+            m = slice(P // SPLIT * i, P // SPLIT * (i + 1))
+            round_wa(nc.scalar.copy, g01[:, :, m, :], raw01[:, :, PASS // SPLIT * i : PASS // SPLIT * (i + 1)])
         both3 = tenant("y", "both3", [P, CHUNK], U32)
         gather_tab(3, both3[:])
         quantize_wa(0, 1, g01)
-        part_tab(3, both3[:], slice(0, 2))
+        part_tab(3, both3[:], slice(0, 2), held("v_w3", [P, 2, 2 * CHUNK], U8)[:])
         g11 = new_grouped("w")
-        round_wa(nc.vector.tensor_copy, g11[:], late[:, 1])
-        wbp_w = tenant("e1", "wbp_w", [P, R], I32)
+        round_wa(nc.vector.tensor_copy, g11[:], raw11[:])
+        wbp_w = tenant("c1", "wbp_w", [P, R], I32)
         wbp_s = held("wbp_s", [P, R], U8)
         nc.vector.tensor_copy(
             wbp_s[:].rearrange("p (h t m) -> p h t m", h=2, t=PACK), wb_s.rearrange("p (h m t) -> p h t m", h=2, t=PACK)
@@ -290,16 +310,21 @@ def tile_list_kg_mul_gelu_kernel(
         nc.vector.tensor_copy(
             wbp_w[:].rearrange("p (h t m) -> p h m t", h=2, t=PACK), wb_w.rearrange("p (h m t) -> p h m t", h=2, t=PACK)
         )
-        gather_tab2_scales(0, "w")
+        early_s = tenant("w", "early_s", [P, (AHEAD - 1) * CHUNK], U8)
+        nc.vector.tensor_copy(early_s[:], tab2_s[:].indirect(list2[:, LIST_COLS : AHEAD * LIST_COLS]))
+        for c in range(1, AHEAD):
+            v2_s[c] = early_s[:, cols(c - 1)]
         gather_tab2(0, "z")
+        gather_tab2(1, "y")
 
+        first = tenant("a", "ha_first", [P, 2, PACK, CHUNK], F32)
+        ha[0, 0] = first[:, 0]
+        ha[0, 1] = first[:, 1]
         opened = [(c, t) + new_bank([P, CHUNK], "scalar") for c in range(2) for t in range(PACK)]
         for c, t, place, bank in opened:
             ha_pass(bank, 0, c, t, 0)
         for c, t, place, bank in opened:
             emptied.append((place, "scalar"))
-            if t == 0:
-                ha[0, c] = tenant("ha0%d" % c, "ha", [P, PACK, CHUNK], F32)
             ha_pass(bank, 0, c, t, 1)
             nc.scalar.copy(ha[0, c][:, t, :], bank[:])
 
@@ -311,9 +336,10 @@ def tile_list_kg_mul_gelu_kernel(
         units = [(h, q0, w, u) for q0, w in pieces for h in range(2) for u in range(w // UNIT)]
 
         def fill(count):
-            for make, args in wide[:count]:
-                make(*args)
-            wide[:count] = []
+            for step in range(count):
+                if wide and free_for("vector"):
+                    make, args = wide.pop(0)
+                    make(*args)
 
         def scores(h, q0, w, u):
             return [(make_out, (q0, w, n)) for n in range(0, N // P, CHUNK // w)]
@@ -330,12 +356,12 @@ def tile_list_kg_mul_gelu_kernel(
                 quantize_h(*units[i - 1][:3])
                 if h == 0:
                     wide.extend(scores(*units[i - 1]))
-            if c + 1 < CHUNKS and place == SCALES_AT:
+            if AHEAD <= c + 1 < CHUNKS and place == SCALES_AT:
                 gather_tab2_scales(c + 1, "first%d" % (c % 2))
-                fill(FG)
-            if c + 1 < CHUNKS and place == WORDS_AT:
-                gather_tab2(c + 1, "ha0%d" % c)
-                fill(FG)
+            if 2 <= c + 1 < CHUNKS and place == WORDS_AT:
+                gather_tab2(c + 1, ("", "a", "ha02")[c])
+            if place in (SCALES_AT, WORDS_AT):
+                fill(FG[c])
             if i % 2 == ODD:
                 fill(1)
         quantize_h(*units[-1][:3])

@@ -84,17 +84,15 @@ def tile_list_kg_mul_gelu_kernel(
         nc.gpsimd.memset(tab_s[:, 3 * T // 4 :].bitcast(I32), 0)
         zero(tab2_s[:])
         zero(v_s1[:])
-        warm = held("warm", [P, 2], F32)
-        nc.gpsimd.memset(warm[:, 0:1], 0.0)
-        nc.scalar.activation(warm[:, 1:2], warm[:, 0:1], GELU)
-        raw00 = tenant("c1", "wa_raw", [P, PACK, PASS], F32)
+        raw00 = [tenant("c%d" % i, "wa_raw", [P, PACK, PASS // 2], F32) for i in range(2)]
         raw10 = [tenant("e%d" % i, "wa_raw", [P, PACK, PASS // 2], F32) for i in range(2)]
         nc.sync.dma_start(list1[:], offs)
         nc.sync.dma_start(list2[:], offs2)
-        nc.sync.dma_start(out=raw00[:, :1, :], in_=wa_rows(0, 0)[:, :1, :])
+        nc.sync.dma_start(out=raw00[0][:, :1, :], in_=wa_rows(0, 0)[:, :1, : PASS // 2])
         load_scales(nc.sync, tab_s[:], tab_scales.rearrange("a (q r) t -> r q a t", r=4), SHIFT)
-        nc.sync.dma_start(out=raw00[:, 1:, :], in_=wa_rows(0, 0)[:, 1:, :])
         nc.sync.dma_start(out=tab_w[:], in_=words(tab_words[0]))
+        nc.sync.dma_start(out=raw00[0][:, 1:, :], in_=wa_rows(0, 0)[:, 1:, : PASS // 2])
+        nc.sync.dma_start(out=raw00[1][:], in_=wa_rows(0, 0)[:, :, PASS // 2 :])
         for i in range(2):
             nc.sync.dma_start(out=raw10[i][:], in_=wa_rows(1, 0)[:, :, PASS // 2 * i : PASS // 2 * (i + 1)])
 
@@ -254,31 +252,34 @@ def tile_list_kg_mul_gelu_kernel(
             part = slice(PASS // SPLIT * i, PASS // SPLIT * (i + 1))
             nc.sync.dma_start(out=raw01[:, :, part], in_=wa_rows(0, 1)[:, :, part])
 
-        gather_tab2_scales(0, "s0")
-        g00 = new_grouped("x")
-        round_wa(nc.scalar.copy, g00[:], raw00[:])
-        quantize_wa(0, 0, g00)
-        raw11 = tenant("c1", "wa_raw", [P, PACK, PASS], F32)
-        nc.sync.dma_start(out=raw11[:], in_=wa_rows(1, 1))
+        both = tenant("b", "both", [P, 2, CHUNK], U32)
         for c in range(2):
-            both = tenant("b", "both", [P, CHUNK], U32)
-            parted = held("v_w%d" % c, [P, 2, 2 * CHUNK], U8)
-            gather_tab(c, both[:])
-            for a in range(2):
-                part_tab(c, both[:], slice(a, a + 1), parted[:, a : a + 1, :])
-        wb = tenant("x", "wb", [P, R + R // 4], I32)
+            gather_tab(c, both[:, c, :])
+        early = held("early", [P, 2, 2 * CHUNK], U8)
+        for c in range(2):
+            part_tab(c, both[:, c, :], slice(0, 1), early[:, c : c + 1, :])
+        g00 = new_grouped("x")
+        for i in range(2):
+            round_wa(nc.scalar.copy, g00[:, :, P // 2 * i : P // 2 * (i + 1), :], raw00[i][:])
+        quantize_wa(0, 0, g00)
+        raw11 = tenant("c0", "wa_raw", [P, PACK, PASS], F32)
+        nc.sync.dma_start(out=raw11[:], in_=wa_rows(1, 1))
+        second = held("second", [P, 2, 2 * CHUNK], U8)
+        for c in range(2):
+            part_tab(c, both[:, c, :], slice(1, 2), second[:, c : c + 1, :])
+        wb = tenant("c1", "wb", [P, R + R // 4], I32)
         wb_w = wb[:, :R]
         wb_s = wb[:, R:].bitcast(U8)
         nc.vector.memset(wb[:, R:], 0)
         load_scales(nc.sync, wb_s[WB_ROW:], wb_scales[0].rearrange("(q r) t -> r q t", r=4), 32)
         nc.sync.dma_start(out=wb_w, in_=words(wb_words[0]))
+        both2 = tenant("x", "both2", [P, CHUNK], U32)
+        gather_tab(2, both2[:])
+        part_tab(2, both2[:], slice(0, 2), held("v_w2", [P, 2, 2 * CHUNK], U8)[:])
         g10 = new_grouped("y")
         for i in range(2):
             round_wa(nc.scalar.copy, g10[:, :, P // 2 * i : P // 2 * (i + 1), :], raw10[i][:])
         quantize_wa(1, 0, g10)
-        both2 = tenant("y", "both2", [P, CHUNK], U32)
-        gather_tab(2, both2[:])
-        part_tab(2, both2[:], slice(0, 2), held("v_w2", [P, 2, 2 * CHUNK], U8)[:])
         tab2_w = tenant("e0", "tab2_w", [P, T], I32)
         nc.sync.dma_start(out=tab2_w[:], in_=words(tab2_words[0]))
         en = tenant("e1", "en", [P, 2 * N + N // 4], I32)
@@ -299,9 +300,10 @@ def tile_list_kg_mul_gelu_kernel(
         gather_tab(3, both3[:])
         quantize_wa(0, 1, g01)
         part_tab(3, both3[:], slice(0, 2), held("v_w3", [P, 2, 2 * CHUNK], U8)[:])
+        gather_tab2_scales(0, "y")
         g11 = new_grouped("w")
         round_wa(nc.vector.tensor_copy, g11[:], raw11[:])
-        wbp_w = tenant("c1", "wbp_w", [P, R], I32)
+        wbp_w = tenant("c0", "wbp_w", [P, R], I32)
         wbp_s = held("wbp_s", [P, R], U8)
         nc.vector.tensor_copy(
             wbp_s[:].rearrange("p (h t m) -> p h t m", h=2, t=PACK), wb_s.rearrange("p (h m t) -> p h t m", h=2, t=PACK)
@@ -315,7 +317,7 @@ def tile_list_kg_mul_gelu_kernel(
         for c in range(1, AHEAD):
             v2_s[c] = early_s[:, cols(c - 1)]
         gather_tab2(0, "z")
-        gather_tab2(1, "y")
+        gather_tab2(1, "x")
 
         first = tenant("a", "ha_first", [P, 2, PACK, CHUNK], F32)
         ha[0, 0] = first[:, 0]

@@ -24,7 +24,6 @@ CHUNKS = J // CHUNK
 UNIT = 128
 LIST_COLS = CHUNK // 16
 SHIFT = 16
-SPLIT = 2
 AHEAD = 4
 TAB2_ROW = 4
 WB_ROW = 8
@@ -84,19 +83,20 @@ def tile_list_kg_mul_gelu_kernel(
         nc.gpsimd.memset(tab_s[:, 3 * T // 4 :].bitcast(I32), 0)
         zero(tab2_s[:])
         zero(v_s1[:])
-        raw00 = [tenant("c%d" % i, "wa_raw", [P, PACK, PASS // 2], F32) for i in range(2)]
-        raw10 = [tenant("e%d" % i, "wa_raw", [P, PACK, PASS // 2], F32) for i in range(2)]
+        raw00 = tenant("c", "wa_raw", [P, PACK, PASS], F32)
+        raw10 = tenant("e", "wa_raw", [P, PACK, PASS], F32)
         nc.sync.dma_start(list1[:], offs)
         nc.sync.dma_start(list2[:], offs2)
-        nc.sync.dma_start(out=raw00[0][:, :1, :], in_=wa_rows(0, 0)[:, :1, : PASS // 2])
+        nc.sync.dma_start(out=raw00[:, 0, : PASS // 2], in_=wa_rows(0, 0)[:, 0, : PASS // 2])
         load_scales(nc.sync, tab_s[:], tab_scales.rearrange("a (q r) t -> r q a t", r=4), SHIFT)
         nc.sync.dma_start(out=tab_w[:], in_=words(tab_words[0]))
-        nc.sync.dma_start(out=raw00[0][:, 1:, :], in_=wa_rows(0, 0)[:, 1:, : PASS // 2])
-        nc.sync.dma_start(out=raw00[1][:], in_=wa_rows(0, 0)[:, :, PASS // 2 :])
-        for i in range(2):
-            nc.sync.dma_start(out=raw10[i][:], in_=wa_rows(1, 0)[:, :, PASS // 2 * i : PASS // 2 * (i + 1)])
+        nc.sync.dma_start(out=raw00[:, 0, PASS // 2 :], in_=wa_rows(0, 0)[:, 0, PASS // 2 :])
+        nc.sync.dma_start(out=raw00[:, 1:, :], in_=wa_rows(0, 0)[:, 1:, :])
+        nc.sync.dma_start(out=raw10[:], in_=wa_rows(1, 0))
+        raw01 = tenant("g", "wa_raw", [P, PACK, PASS], F32)
+        nc.sync.dma_start(out=raw01[:], in_=wa_rows(0, 1))
 
-        load_scales(nc.gpsimd, tab2_s[TAB2_ROW:], tab2_scales[0].rearrange("(q r) t -> r q t", r=4), 32)
+        load_scales(nc.sync, tab2_s[TAB2_ROW:], tab2_scales[0].rearrange("(q r) t -> r q t", r=4), 32)
 
         def cols(c):
             return slice(CHUNK * c, CHUNK * (c + 1))
@@ -247,10 +247,8 @@ def tile_list_kg_mul_gelu_kernel(
 
         nc.vector.tensor_copy(v_s0[:], tab_s[:].indirect(list1[:]))
         nc.sync.dma_start(out=v_s1[0 : P - SHIFT, :].bitcast(I32), in_=v_s0[SHIFT:P, :].bitcast(I32))
-        raw01 = tenant("a", "wa_raw", [P, PACK, PASS], F32)
-        for i in range(SPLIT):
-            part = slice(PASS // SPLIT * i, PASS // SPLIT * (i + 1))
-            nc.sync.dma_start(out=raw01[:, :, part], in_=wa_rows(0, 1)[:, :, part])
+        raw11 = tenant("a", "wa_raw", [P, PACK, PASS], F32)
+        nc.sync.dma_start(out=raw11[:], in_=wa_rows(1, 1))
 
         both = tenant("b", "both", [P, 2, CHUNK], U32)
         for c in range(2):
@@ -259,51 +257,45 @@ def tile_list_kg_mul_gelu_kernel(
         for c in range(2):
             part_tab(c, both[:, c, :], slice(0, 1), early[:, c : c + 1, :])
         g00 = new_grouped("x")
-        for i in range(2):
-            round_wa(nc.scalar.copy, g00[:, :, P // 2 * i : P // 2 * (i + 1), :], raw00[i][:])
+        round_wa(nc.scalar.copy, g00[:, :, : P // 2, :], raw00[:, :, : PASS // 2])
+        round_wa(nc.vector.tensor_copy, g00[:, :, P // 2 :, :], raw00[:, :, PASS // 2 :])
         quantize_wa(0, 0, g00)
-        raw11 = tenant("c0", "wa_raw", [P, PACK, PASS], F32)
-        nc.sync.dma_start(out=raw11[:], in_=wa_rows(1, 1))
-        second = held("second", [P, 2, 2 * CHUNK], U8)
-        for c in range(2):
-            part_tab(c, both[:, c, :], slice(1, 2), second[:, c : c + 1, :])
-        wb = tenant("c1", "wb", [P, R + R // 4], I32)
+        for c, place in enumerate(("second", "x")):
+            part_tab(c, both[:, c, :], slice(1, 2), tenant(place, "second", [P, 1, 2 * CHUNK], U8)[:])
+        wb = tenant("c", "wb", [P, R + R // 4], I32)
         wb_w = wb[:, :R]
         wb_s = wb[:, R:].bitcast(U8)
         nc.vector.memset(wb[:, R:], 0)
         load_scales(nc.sync, wb_s[WB_ROW:], wb_scales[0].rearrange("(q r) t -> r q t", r=4), 32)
         nc.sync.dma_start(out=wb_w, in_=words(wb_words[0]))
-        both2 = tenant("x", "both2", [P, CHUNK], U32)
+        both2 = tenant("b", "both2", [P, CHUNK], U32)
         gather_tab(2, both2[:])
         part_tab(2, both2[:], slice(0, 2), held("v_w2", [P, 2, 2 * CHUNK], U8)[:])
         g10 = new_grouped("y")
-        for i in range(2):
-            round_wa(nc.scalar.copy, g10[:, :, P // 2 * i : P // 2 * (i + 1), :], raw10[i][:])
+        round_wa(nc.scalar.copy, g10[:], raw10[:])
         quantize_wa(1, 0, g10)
-        tab2_w = tenant("e0", "tab2_w", [P, T], I32)
+        tab2_w = tenant("b", "tab2_w", [P, T], I32)
         nc.sync.dma_start(out=tab2_w[:], in_=words(tab2_words[0]))
-        en = tenant("e1", "en", [P, 2 * N + N // 4], I32)
+        en = tenant("e", "en", [P, 2 * N + N // 4], I32)
         en_w = en[:, : 2 * N].rearrange("p (a n) -> p a n", a=2)
         en_s = en[:, 2 * N :].bitcast(U8)
         nc.sync.dma_start(out=en_w, in_=en_words.rearrange("a p n i -> p a (n i)").bitcast(I32))
         nc.vector.memset(en[:, 2 * N :], 0)
         for q in range(4):
             nc.sync.dma_start(out=en[32 * q : 32 * q + 8, 2 * N :], in_=en_scales[:, 4 * q : 4 * q + 4, :].bitcast(I32))
-        bias = tenant("b", "bias", [P, N // P], F32)
-        with nc.allow_non_contiguous_dma(reason="one bias value for each partition and output tile"):
-            nc.sync.dma_start(out=bias[:], in_=b.rearrange("(c p) -> p c", p=P))
         g01 = new_grouped("z")
-        for i in range(SPLIT):
-            m = slice(P // SPLIT * i, P // SPLIT * (i + 1))
-            round_wa(nc.scalar.copy, g01[:, :, m, :], raw01[:, :, PASS // SPLIT * i : PASS // SPLIT * (i + 1)])
+        round_wa(nc.scalar.copy, g01[:], raw01[:])
         both3 = tenant("y", "both3", [P, CHUNK], U32)
         gather_tab(3, both3[:])
         quantize_wa(0, 1, g01)
+        bias = tenant("z", "bias", [P, N // P], F32)
+        with nc.allow_non_contiguous_dma(reason="one bias value for each partition and output tile"):
+            nc.sync.dma_start(out=bias[:], in_=b.rearrange("(c p) -> p c", p=P))
         part_tab(3, both3[:], slice(0, 2), held("v_w3", [P, 2, 2 * CHUNK], U8)[:])
         gather_tab2_scales(0, "y")
         g11 = new_grouped("w")
         round_wa(nc.vector.tensor_copy, g11[:], raw11[:])
-        wbp_w = tenant("c0", "wbp_w", [P, R], I32)
+        wbp_w = tenant("a", "wbp_w", [P, R], I32)
         wbp_s = held("wbp_s", [P, R], U8)
         nc.vector.tensor_copy(
             wbp_s[:].rearrange("p (h t m) -> p h t m", h=2, t=PACK), wb_s.rearrange("p (h m t) -> p h t m", h=2, t=PACK)
@@ -316,10 +308,10 @@ def tile_list_kg_mul_gelu_kernel(
         nc.vector.tensor_copy(early_s[:], tab2_s[:].indirect(list2[:, LIST_COLS : AHEAD * LIST_COLS]))
         for c in range(1, AHEAD):
             v2_s[c] = early_s[:, cols(c - 1)]
-        gather_tab2(0, "z")
-        gather_tab2(1, "x")
+        gather_tab2(0, "v0")
+        gather_tab2(1, "c")
 
-        first = tenant("a", "ha_first", [P, 2, PACK, CHUNK], F32)
+        first = tenant("g", "ha_first", [P, 2, PACK, CHUNK], F32)
         ha[0, 0] = first[:, 0]
         ha[0, 1] = first[:, 1]
         opened = [(c, t) + new_bank([P, CHUNK], "scalar") for c in range(2) for t in range(PACK)]
@@ -361,7 +353,7 @@ def tile_list_kg_mul_gelu_kernel(
             if AHEAD <= c + 1 < CHUNKS and place == SCALES_AT:
                 gather_tab2_scales(c + 1, "first%d" % (c % 2))
             if 2 <= c + 1 < CHUNKS and place == WORDS_AT:
-                gather_tab2(c + 1, ("", "a", "ha02")[c])
+                gather_tab2(c + 1, ("", "g", "ha02")[c])
             if place in (SCALES_AT, WORDS_AT):
                 fill(FG[c])
             if i % 2 == ODD:

@@ -19,25 +19,22 @@ GELU = mybir.ActivationFunctionType.Gelu_apprx_tanh
 P = 128
 PACK = 4
 PASS = P * PACK
+QUADRANT = 32
 CHUNK = 512
 CHUNKS = J // CHUNK
 UNIT = 128
+UNITS = CHUNK // UNIT
 LIST_COLS = CHUNK // 16
+BANKS = 8
 SHIFT = 16
-AHEAD = 4
 TAB2_ROW = 4
 WB_ROW = 8
-BANKS = 8
-FRESH = 1
+EN_ROWS = 4
 ALONE = 25
-SCALES_AT = 6
-WORDS_AT = 4
-RING = 2
-FQ = 1
-FG = (1, 2, 2, 0)
-ODD = 1
 LEAD = 2
-WIDTHS = (512,) * 4
+ROUNDED_TILES = 3
+H_TILES = 5
+RESULT_TILES = 6
 
 
 def tile_list_kg_mul_gelu_kernel(
@@ -55,17 +52,6 @@ def tile_list_kg_mul_gelu_kernel(
         def tenant(place, name, shape, dtype):
             return keep.tile(shape, dtype, name=name, tag=place, align_bytes=64)
 
-        list1 = keep.tile([P, J // 16], U16, name="list1")
-        list2 = keep.tile([P, J // 16], U16, name="list2")
-        tab_w = held("tab_w", [P, T], I32)
-        tab_s = tenant("a", "tab_s", [P, T], U8)
-        tab2_s = held("tab2_s", [P, T], U8)
-        v_s0 = held("v_s0", [P, J], U8)
-        v_s1 = held("v_s1", [P, J], U8)
-        v_w = {}
-        wa_w = held("wa_w", [P, 2, R], U32)
-        wa_s = held("wa_s", [P, 2, R], U8)
-
         def words(dram):
             return dram.rearrange("p n i -> p (n i)").bitcast(I32)
 
@@ -75,54 +61,67 @@ def tile_list_kg_mul_gelu_kernel(
         def wa_rows(a, h):
             return wa[PASS * a : PASS * (a + 1), PASS * h : PASS * (h + 1)].rearrange("(p j) c -> p j c", j=PACK)
 
-        def load_scales(queue, plane, by_row, step):
+        def load_wa(a, h, place):
+            raw = tenant(place, "wa_raw", [P, PACK, PASS], F32)
+            nc.sync.dma_start(out=raw[:], in_=wa_rows(a, h))
+            return raw
+
+        def load_scales(plane, by_row, step):
             for r in range(4):
-                queue.dma_start(out=plane[r::step].bitcast(I32), in_=by_row[r].bitcast(I32))
+                nc.sync.dma_start(out=plane[r::step].bitcast(I32), in_=by_row[r].bitcast(I32))
+
+        def cols(c0, c1):
+            return slice(CHUNK * c0, CHUNK * c1)
+
+        def entries(lst, c0, c1):
+            return lst[:, LIST_COLS * c0 : LIST_COLS * c1]
+
+        def r_cols(h, t):
+            return slice(PASS * h + P * t, PASS * h + P * (t + 1))
+
+        list1 = keep.tile([P, J // 16], U16, name="list1")
+        list2 = keep.tile([P, J // 16], U16, name="list2")
+        tab_w = held("tab_w", [P, T], I32)
+        tab_s = tenant("a", "tab_s", [P, T], U8)
+        tab2_s = held("tab2_s", [P, T], U8)
+        v_s0 = held("v_s0", [P, J], U8)
+        v_s1 = held("v_s1", [P, J], U8)
+        wa_w = held("wa_w", [P, 2, R], U32)
+        wa_s = held("wa_s", [P, 2, R], U8)
 
         zero(tab_s[:, : 3 * T // 4])
         nc.gpsimd.memset(tab_s[:, 3 * T // 4 :].bitcast(I32), 0)
         zero(tab2_s[:])
         zero(v_s1[:])
         raw00 = tenant("c", "wa_raw", [P, PACK, PASS], F32)
-        raw10 = tenant("e", "wa_raw", [P, PACK, PASS], F32)
         nc.sync.dma_start(list1[:], offs)
         nc.sync.dma_start(list2[:], offs2)
         nc.sync.dma_start(out=raw00[:, 0, : PASS // 2], in_=wa_rows(0, 0)[:, 0, : PASS // 2])
-        load_scales(nc.sync, tab_s[:], tab_scales.rearrange("a (q r) t -> r q a t", r=4), SHIFT)
+        load_scales(tab_s[:], tab_scales.rearrange("a (q r) t -> r q a t", r=4), SHIFT)
         nc.sync.dma_start(out=tab_w[:], in_=words(tab_words[0]))
         nc.sync.dma_start(out=raw00[:, 0, PASS // 2 :], in_=wa_rows(0, 0)[:, 0, PASS // 2 :])
         nc.sync.dma_start(out=raw00[:, 1:, :], in_=wa_rows(0, 0)[:, 1:, :])
-        nc.sync.dma_start(out=raw10[:], in_=wa_rows(1, 0))
-        raw01 = tenant("g", "wa_raw", [P, PACK, PASS], F32)
-        nc.sync.dma_start(out=raw01[:], in_=wa_rows(0, 1))
+        raw10 = load_wa(1, 0, "e")
+        raw01 = load_wa(0, 1, "g")
+        load_scales(tab2_s[TAB2_ROW:], tab2_scales[0].rearrange("(q r) t -> r q t", r=4), QUADRANT)
 
-        load_scales(nc.sync, tab2_s[TAB2_ROW:], tab2_scales[0].rearrange("(q r) t -> r q t", r=4), 32)
-
-        def cols(c):
-            return slice(CHUNK * c, CHUNK * (c + 1))
-
-        def entries(lst, c):
-            return lst[:, LIST_COLS * c : LIST_COLS * (c + 1)]
-
-        def gather_tab(c, both):
-            nc.vector.tensor_copy(both, tab_w[:].bitcast(U32).indirect(entries(list1, c)))
-
-        def part_tab(c, both, passes, parted):
-            nc.vector.tensor_copy(parted.bitcast(U16), both.bitcast(U16).rearrange("p (j d) -> p d j", d=2)[:, passes, :])
-            for a in range(passes.start, passes.stop):
-                v_w[c, a] = parted[:, a - passes.start, :]
-
-        v2_s = {}
-
-        def gather_tab2_scales(c, place):
-            v2_s[c] = tenant(place, "v2_s", [P, CHUNK], U8)
-            nc.vector.tensor_copy(v2_s[c][:], tab2_s[:].indirect(entries(list2, c)))
-
+        v_w = {}
         v2_w = {}
+
+        def gather_tab(c0, c1, both):
+            nc.vector.tensor_copy(both, tab_w[:].bitcast(U32).indirect(entries(list1, c0, c1)))
+
+        def part_tab(both, a0, a1, parted):
+            nc.vector.tensor_copy(parted.bitcast(U16), both.bitcast(U16).rearrange("p (j d) -> p d j", d=2)[:, a0:a1, :])
+
+        def gather_tab2_scales(c0, c1, place):
+            picked = tenant(place, "v2_s", [P, CHUNK * (c1 - c0)], U8)
+            nc.vector.tensor_copy(picked[:], tab2_s[:].indirect(entries(list2, c0, c1)))
+            return [picked[:, cols(c, c + 1)] for c in range(c1 - c0)]
 
         def gather_tab2(c, place):
             v2_w[c] = tenant(place, "v2_w", [P, CHUNK], U32)
-            nc.vector.tensor_copy(v2_w[c][:], tab2_w[:].bitcast(U32).indirect(entries(list2, c)))
+            nc.vector.tensor_copy(v2_w[c][:], tab2_w[:].bitcast(U32).indirect(entries(list2, c, c + 1)))
 
         def round_wa(copy, grouped, raw):
             copy(grouped.rearrange("p t m j -> p m j t"), raw.rearrange("p j (m t) -> p m j t", t=PACK))
@@ -138,65 +137,53 @@ def tile_list_kg_mul_gelu_kernel(
 
         banks = [psum.tile([P, CHUNK], F32, name="bank%d" % i) for i in range(BANKS)]
         emptied = [(i, "scalar") for i in range(BANKS)]
-
         tied = set()
+        ha = {}
+        hb = {}
+        rounded = {}
+        hq = {}
 
-        def free_for(after):
-            if after == "scalar":
-                first = [entry for entry in emptied if entry[0] not in tied]
-                return first + [entry for entry in emptied if entry[1] == after] + emptied
+        def free_for_hb():
+            untied = [entry for entry in emptied if entry[0] not in tied]
+            return untied + [entry for entry in emptied if entry[1] == "scalar"] + emptied
+
+        def free_for_wide():
             usable = [entry for entry in emptied if entry[0] in tied or not hb]
-            return [entry for entry in usable[: len(usable) - FRESH] if entry[1] == after] + usable
+            return [entry for entry in usable[:-1] if entry[1] == "vector"] + usable
 
-        def new_bank(shape, after):
-            pick = free_for(after)[0]
-            emptied.remove(pick)
-            bank = banks[pick[0]][:]
-            return pick[0], bank if len(shape) == 2 else bank.rearrange("p (a b) -> p a b", a=shape[1])
-
-        def r_cols(h, t):
-            return slice(PASS * h + P * t, PASS * h + P * (t + 1))
+        def take(free):
+            emptied.remove(free[0])
+            return free[0][0]
 
         def ha_pass(bank, h, c, t, a):
             nc.tensor.matmul_mx(
-                out=bank[:],
+                out=banks[bank][:],
                 lhsT=wa_w[:, a, r_cols(h, t)].bitcast(FP8X4),
                 lhsT_scale=wa_s[:, a, r_cols(h, t)],
                 rhs=v_w[c, a].bitcast(FP4X4),
-                rhs_scale=(v_s0, v_s1)[a][:, cols(c)],
+                rhs_scale=(v_s0, v_s1)[a][:, cols(c, c + 1)],
                 start=(a == 0),
                 stop=(a == 1),
             )
 
-        ha = {}
-        hb = {}
+        def copy_ha(bank, h, c, t):
+            nc.scalar.copy(ha[h, c][:, t, :], banks[bank][:])
+            emptied.append((bank, "scalar"))
 
         def make_ha(h, c, t):
             if t == 0:
                 ha[h, c] = tenant("ha%d%d" % (h, c), "ha", [P, PACK, CHUNK], F32)
-            place, bank = new_bank([P, CHUNK], "vector")
+            bank = take(free_for_wide())
             ha_pass(bank, h, c, t, 0)
             ha_pass(bank, h, c, t, 1)
-            nc.scalar.copy(ha[h, c][:, t, :], bank[:])
-            emptied.append((place, "scalar"))
+            copy_ha(bank, h, c, t)
 
-        rounded = {}
-        hq = {}
-
-        def quantize_h(h, q0, width):
-            h_w = ring.tile([P, width], U32, name="h_w", bufs=5, align_bytes=64)
-            h_s = ring.tile([P, width], U8, name="h_s", bufs=5, align_bytes=64)
-            nc.vector.quantize_mx(out=h_w[:].bitcast(FP8X4), scales=h_s[:], in_=rounded[h, q0][:].rearrange("p j t -> p (j t)"))
-            hq[h, q0] = (h_w, h_s)
-
-        def make_hb(h, q0, width, u):
-            c, at = divmod(q0 + UNIT * u, CHUNK)
-            within = slice(at, at + UNIT)
-            place, bank = new_bank([P, PACK, UNIT], "scalar")
-            hb[h, q0, u] = (place, bank)
+        def make_hb(c, h, u):
+            within = slice(UNIT * u, UNIT * (u + 1))
+            hb[c, h, u] = take(free_for_hb())
             for t in range(PACK):
                 nc.tensor.matmul_mx(
-                    out=bank[:, t, :],
+                    out=banks[hb[c, h, u]][:, UNIT * t : UNIT * (t + 1)],
                     lhsT=wbp_w[:, r_cols(h, t)].bitcast(FP8X4),
                     lhsT_scale=wbp_s[WB_ROW:, r_cols(h, t)],
                     rhs=v2_w[c][:, within].bitcast(FP8X4),
@@ -205,94 +192,96 @@ def tile_list_kg_mul_gelu_kernel(
                     stop=True,
                 )
 
-        def make_h(h, q0, width, u):
-            if u == 0 and h == 0 and q0 % CHUNK == 0:
-                rounded[h, q0] = tenant("first%d" % (q0 // CHUNK % 2), "rounded", [P, width, PACK], BF16)
-            elif u == 0:
-                rounded[h, q0] = ring.tile([P, width, PACK], BF16, name="rounded", bufs=RING, align_bytes=64)
-            c, at = divmod(q0 + UNIT * u, CHUNK)
-            within = slice(at, at + UNIT)
-            place, bank = hb[h, q0, u]
-            emptied.append((place, "vector"))
-            tied.add(place)
+        def make_h(c, h, u):
+            if u == 0:
+                rounded[c, h] = ring.tile([P, CHUNK, PACK], BF16, name="rounded", bufs=ROUNDED_TILES, align_bytes=64)
+            within = slice(UNIT * u, UNIT * (u + 1))
+            bank = hb[c, h, u]
             nc.vector.tensor_tensor(
-                rounded[h, q0][:, UNIT * u : UNIT * (u + 1), :].rearrange("p (g i) t -> p g t i", i=4),
-                bank[:].rearrange("p t (g i) -> p g t i", i=4),
+                rounded[c, h][:, within, :].rearrange("p (g i) t -> p g t i", i=4),
+                banks[bank][:].rearrange("p (t g i) -> p g t i", t=PACK, i=4),
                 ha[h, c][:, :, within].rearrange("p t (g i) -> p g t i", i=4),
                 MULT,
             )
+            emptied.append((bank, "vector"))
+            tied.add(bank)
 
-        def make_out(q0, width, n0):
-            tiles = CHUNK // width
-            place, bank = new_bank([P, tiles, width], "vector")
-            emptied.append((place, "scalar"))
-            result = ring.tile([P, tiles, width], F32, name="result", bufs=6)
-            for i in range(tiles):
-                n = n0 + i
-                for h in range(2):
-                    nc.tensor.matmul_mx(
-                        out=bank[:, i, :],
-                        lhsT=en_w[:, h, P * n : P * (n + 1)].bitcast(FP8X4),
-                        lhsT_scale=en_s[4 * h :, P * n : P * (n + 1)],
-                        rhs=hq[h, q0][0][:].bitcast(FP8X4),
-                        rhs_scale=hq[h, q0][1][:],
-                        start=(h == 0),
-                        stop=(h == 1),
-                    )
-            for i in range(tiles):
-                nc.scalar.activation(result[:, i, :], bank[:, i, :], GELU, bias=bias[:, n0 + i : n0 + i + 1])
-            nc.sync.dma_start(
-                out=out[P * n0 : P * (n0 + tiles), q0 : q0 + width].rearrange("(i p) j -> p i j", p=P), in_=result[:]
-            )
+        def quantize_h(c, h):
+            h_w = ring.tile([P, CHUNK], U32, name="h_w", bufs=H_TILES, align_bytes=64)
+            h_s = ring.tile([P, CHUNK], U8, name="h_s", bufs=H_TILES, align_bytes=64)
+            nc.vector.quantize_mx(out=h_w[:].bitcast(FP8X4), scales=h_s[:], in_=rounded[c, h][:].rearrange("p j t -> p (j t)"))
+            hq[c, h] = (h_w, h_s)
+
+        def make_out(c, n):
+            rows = slice(P * n, P * (n + 1))
+            bank = take(free_for_wide())
+            for h in range(2):
+                nc.tensor.matmul_mx(
+                    out=banks[bank][:],
+                    lhsT=en_w[:, h, rows].bitcast(FP8X4),
+                    lhsT_scale=en_s[EN_ROWS * h :, rows],
+                    rhs=hq[c, h][0][:].bitcast(FP8X4),
+                    rhs_scale=hq[c, h][1][:],
+                    start=(h == 0),
+                    stop=(h == 1),
+                )
+            result = ring.tile([P, CHUNK], F32, name="result", bufs=RESULT_TILES)
+            nc.scalar.activation(result[:], banks[bank][:], GELU, bias=bias[:, n : n + 1])
+            nc.sync.dma_start(out=out[rows, cols(c, c + 1)], in_=result[:])
+            emptied.append((bank, "scalar"))
 
         nc.vector.tensor_copy(v_s0[:], tab_s[:].indirect(list1[:]))
         nc.sync.dma_start(out=v_s1[0 : P - SHIFT, :].bitcast(I32), in_=v_s0[SHIFT:P, :].bitcast(I32))
-        raw11 = tenant("a", "wa_raw", [P, PACK, PASS], F32)
-        nc.sync.dma_start(out=raw11[:], in_=wa_rows(1, 1))
+        raw11 = load_wa(1, 1, "a")
 
-        both = tenant("b", "both", [P, 2, CHUNK], U32)
+        both01 = tenant("b", "both01", [P, 2, CHUNK], U32)
         for c in range(2):
-            gather_tab(c, both[:, c, :])
-        early = held("early", [P, 2, 2 * CHUNK], U8)
-        for c in range(2):
-            part_tab(c, both[:, c, :], slice(0, 1), early[:, c : c + 1, :])
+            gather_tab(c, c + 1, both01[:, c, :])
+        v_first = held("v_first", [P, 1, 2 * CHUNK], U8)
+        part_tab(both01[:, 0, :], 0, 1, v_first[:])
         g00 = new_grouped("x")
         round_wa(nc.scalar.copy, g00[:, :, : P // 2, :], raw00[:, :, : PASS // 2])
         round_wa(nc.vector.tensor_copy, g00[:, :, P // 2 :, :], raw00[:, :, PASS // 2 :])
         quantize_wa(0, 0, g00)
-        for c, place in enumerate(("second", "x")):
-            part_tab(c, both[:, c, :], slice(1, 2), tenant(place, "second", [P, 1, 2 * CHUNK], U8)[:])
+        v_next = tenant("x", "v_next", [P, 3, 2 * CHUNK], U8)
+        part_tab(both01[:, 1, :], 0, 2, v_next[:, 0:2, :])
+        part_tab(both01[:, 0, :], 1, 2, v_next[:, 2:3, :])
+        v_w.update({(0, 0): v_first[:, 0, :], (0, 1): v_next[:, 2, :], (1, 0): v_next[:, 0, :], (1, 1): v_next[:, 1, :]})
+
         wb = tenant("c", "wb", [P, R + R // 4], I32)
         wb_w = wb[:, :R]
         wb_s = wb[:, R:].bitcast(U8)
-        nc.vector.memset(wb[:, R:], 0)
-        load_scales(nc.sync, wb_s[WB_ROW:], wb_scales[0].rearrange("(q r) t -> r q t", r=4), 32)
+        zero(wb_s)
+        load_scales(wb_s[WB_ROW:], wb_scales[0].rearrange("(q r) t -> r q t", r=4), QUADRANT)
         nc.sync.dma_start(out=wb_w, in_=words(wb_words[0]))
-        both2 = tenant("b", "both2", [P, CHUNK], U32)
-        gather_tab(2, both2[:])
-        part_tab(2, both2[:], slice(0, 2), held("v_w2", [P, 2, 2 * CHUNK], U8)[:])
+
+        both23 = tenant("b", "both23", [P, 2 * CHUNK], U32)
+        gather_tab(2, 4, both23[:])
         g10 = new_grouped("y")
         round_wa(nc.scalar.copy, g10[:], raw10[:])
         quantize_wa(1, 0, g10)
-        tab2_w = tenant("b", "tab2_w", [P, T], I32)
+        tab2_w = tenant("e", "tab2_w", [P, T], I32)
         nc.sync.dma_start(out=tab2_w[:], in_=words(tab2_words[0]))
-        en = tenant("e", "en", [P, 2 * N + N // 4], I32)
+        v_last = tenant("y", "v_last", [P, 2, 4 * CHUNK], U8)
+        part_tab(both23[:], 0, 2, v_last[:])
+        for c in range(2):
+            for a in range(2):
+                v_w[2 + c, a] = v_last[:, a, 2 * CHUNK * c : 2 * CHUNK * (c + 1)]
+
+        g01 = new_grouped("z")
+        round_wa(nc.scalar.copy, g01[:], raw01[:])
+        quantize_wa(0, 1, g01)
+        en = tenant("z", "en", [P, 2 * N + N // 4], I32)
         en_w = en[:, : 2 * N].rearrange("p (a n) -> p a n", a=2)
         en_s = en[:, 2 * N :].bitcast(U8)
         nc.sync.dma_start(out=en_w, in_=en_words.rearrange("a p n i -> p a (n i)").bitcast(I32))
-        nc.vector.memset(en[:, 2 * N :], 0)
+        zero(en_s)
         for q in range(4):
-            nc.sync.dma_start(out=en[32 * q : 32 * q + 8, 2 * N :], in_=en_scales[:, 4 * q : 4 * q + 4, :].bitcast(I32))
-        g01 = new_grouped("z")
-        round_wa(nc.scalar.copy, g01[:], raw01[:])
-        both3 = tenant("y", "both3", [P, CHUNK], U32)
-        gather_tab(3, both3[:])
-        quantize_wa(0, 1, g01)
-        bias = tenant("z", "bias", [P, N // P], F32)
-        with nc.allow_non_contiguous_dma(reason="one bias value for each partition and output tile"):
-            nc.sync.dma_start(out=bias[:], in_=b.rearrange("(c p) -> p c", p=P))
-        part_tab(3, both3[:], slice(0, 2), held("v_w3", [P, 2, 2 * CHUNK], U8)[:])
-        gather_tab2_scales(0, "y")
+            nc.sync.dma_start(
+                out=en[QUADRANT * q : QUADRANT * q + 2 * EN_ROWS, 2 * N :], in_=en_scales[:, 4 * q : 4 * q + 4, :].bitcast(I32)
+            )
+        v2_s = gather_tab2_scales(0, 1, "b")
+
         g11 = new_grouped("w")
         round_wa(nc.vector.tensor_copy, g11[:], raw11[:])
         wbp_w = tenant("a", "wbp_w", [P, R], I32)
@@ -304,60 +293,51 @@ def tile_list_kg_mul_gelu_kernel(
         nc.vector.tensor_copy(
             wbp_w[:].rearrange("p (h t m) -> p h m t", h=2, t=PACK), wb_w.rearrange("p (h m t) -> p h m t", h=2, t=PACK)
         )
-        early_s = tenant("w", "early_s", [P, (AHEAD - 1) * CHUNK], U8)
-        nc.vector.tensor_copy(early_s[:], tab2_s[:].indirect(list2[:, LIST_COLS : AHEAD * LIST_COLS]))
-        for c in range(1, AHEAD):
-            v2_s[c] = early_s[:, cols(c - 1)]
-        gather_tab2(0, "v0")
-        gather_tab2(1, "c")
+        bias = tenant("c", "bias", [P, N // P], F32)
+        with nc.allow_non_contiguous_dma(reason="one bias value for each partition and output tile"):
+            nc.sync.dma_start(out=bias[:], in_=b.rearrange("(c p) -> p c", p=P))
+        v2_s.extend(gather_tab2_scales(1, CHUNKS, "w"))
+        gather_tab2(0, "v2_w0")
+        gather_tab2(1, "v2_w1")
 
-        first = tenant("g", "ha_first", [P, 2, PACK, CHUNK], F32)
-        ha[0, 0] = first[:, 0]
-        ha[0, 1] = first[:, 1]
-        opened = [(c, t) + new_bank([P, CHUNK], "scalar") for c in range(2) for t in range(PACK)]
-        for c, t, place, bank in opened:
-            ha_pass(bank, 0, c, t, 0)
-        for c, t, place, bank in opened:
-            emptied.append((place, "scalar"))
-            ha_pass(bank, 0, c, t, 1)
-            nc.scalar.copy(ha[0, c][:, t, :], bank[:])
+        ha_first = tenant("g", "ha_first", [P, 2, PACK, CHUNK], F32)
+        ha[0, 0] = ha_first[:, 0]
+        ha[0, 1] = ha_first[:, 1]
+        opened = [(take(free_for_wide()), 0, c, t) for c in range(2) for t in range(PACK)]
+        for group in opened:
+            ha_pass(*group, 0)
+        for group in opened:
+            ha_pass(*group, 1)
+            copy_ha(*group)
 
-        wide = [(make_ha, (h, c, t)) for h, c in ((0, 2), (0, 3), (1, 0), (1, 1), (1, 2), (1, 3)) for t in range(PACK)]
-        for make, args in wide[: ALONE - BANKS]:
-            make(*args)
-        wide = wide[ALONE - BANKS :]
-        pieces = [(sum(WIDTHS[:i]), w) for i, w in enumerate(WIDTHS)]
-        units = [(h, q0, w, u) for q0, w in pieces for h in range(2) for u in range(w // UNIT)]
+        wide = [(make_ha, (h, c, t)) for h in range(2) for c in range(CHUNKS) for t in range(PACK)][BANKS:]
 
         def fill(count):
             for step in range(count):
-                if wide and free_for("vector"):
+                if wide and free_for_wide():
                     make, args = wide.pop(0)
                     make(*args)
 
-        def scores(h, q0, w, u):
-            return [(make_out, (q0, w, n)) for n in range(0, N // P, CHUNK // w)]
-
+        fill(ALONE - BANKS)
+        units = [(c, h, u) for c in range(CHUNKS) for h in range(2) for u in range(UNITS)]
         for unit in units[:LEAD]:
             make_hb(*unit)
-        for i, (h, q0, w, u) in enumerate(units):
-            c, place = divmod(i, 2 * CHUNK // UNIT)
-            make_h(h, q0, w, u)
+        for i, (c, h, u) in enumerate(units):
+            gathers = 1 <= c < CHUNKS - 1
+            make_h(c, h, u)
             if i + LEAD < len(units):
                 make_hb(*units[i + LEAD])
             if u == 0 and i > 0:
-                fill(FQ)
-                quantize_h(*units[i - 1][:3])
-                if h == 0:
-                    wide.extend(scores(*units[i - 1]))
-            if AHEAD <= c + 1 < CHUNKS and place == SCALES_AT:
-                gather_tab2_scales(c + 1, "first%d" % (c % 2))
-            if 2 <= c + 1 < CHUNKS and place == WORDS_AT:
-                gather_tab2(c + 1, ("", "g", "ha02")[c])
-            if place in (SCALES_AT, WORDS_AT):
-                fill(FG[c])
-            if i % 2 == ODD:
                 fill(1)
-        quantize_h(*units[-1][:3])
-        wide.extend(scores(*units[-1]))
+                quantize_h(*units[i - 1][:2])
+                if h == 0:
+                    wide.extend([(make_out, (c - 1, n)) for n in range(N // P)])
+                elif gathers:
+                    gather_tab2(c + 1, ("g", "ha02")[c - 1])
+            if h == 1 and u % 2 == 0:
+                fill(2 if gathers else 1 if c == 0 else 0)
+            if u % 2 == 1:
+                fill(1)
+        quantize_h(CHUNKS - 1, 1)
+        wide.extend([(make_out, (CHUNKS - 1, n)) for n in range(N // P)])
         fill(len(wide))

@@ -26,7 +26,9 @@ UNIT = 128
 UNITS = CHUNK // UNIT
 LIST_COLS = CHUNK // 16
 BANKS = 8
-SHIFT = 16
+EARLY = 64
+SPLIT = 288
+ROWS_AT = 96
 TAB2_ROW = 4
 WB_ROW = 8
 EN_ROWS = 4
@@ -43,6 +45,7 @@ def tile_list_kg_mul_gelu_kernel(
     nc = tc.nc
     with ExitStack() as ctx:
         keep = ctx.enter_context(tc.tile_pool(name="keep", bufs=1))
+        head = ctx.enter_context(tc.tile_pool(name="head", bufs=1))
         ring = ctx.enter_context(tc.tile_pool(name="ring", bufs=2))
         psum = ctx.enter_context(tc.psum_pool(name="psum", bufs=1))
 
@@ -51,6 +54,9 @@ def tile_list_kg_mul_gelu_kernel(
 
         def tenant(place, name, shape, dtype):
             return keep.tile(shape, dtype, name=name, tag=place, align_bytes=64)
+
+        def placed(kib, name, shape, dtype):
+            return head.tile(shape, dtype, name=name, offset=1024 * kib, align_bytes=64)
 
         def words(dram):
             return dram.rearrange("p n i -> p (n i)").bitcast(I32)
@@ -61,8 +67,8 @@ def tile_list_kg_mul_gelu_kernel(
         def wa_rows(a, h):
             return wa[PASS * a : PASS * (a + 1), PASS * h : PASS * (h + 1)].rearrange("(p j) c -> p j c", j=PACK)
 
-        def load_wa(a, h, place):
-            raw = tenant(place, "wa_raw", [P, PACK, PASS], F32)
+        def load_wa(a, h, kib):
+            raw = placed(kib, "wa_raw%d%d" % (a, h), [P, PACK, PASS], F32)
             nc.sync.dma_start(out=raw[:], in_=wa_rows(a, h))
             return raw
 
@@ -82,28 +88,36 @@ def tile_list_kg_mul_gelu_kernel(
         list1 = keep.tile([P, J // 16], U16, name="list1")
         list2 = keep.tile([P, J // 16], U16, name="list2")
         tab_w = held("tab_w", [P, T], I32)
-        tab_s = tenant("a", "tab_s", [P, T], U8)
+        tab_s = placed(22, "tab_s", [P, T], U8)
         tab2_s = held("tab2_s", [P, T], U8)
-        v_s0 = held("v_s0", [P, J], U8)
-        v_s1 = held("v_s1", [P, J], U8)
+        v2_plane = held("v2_plane", [P, J], U8)
+        picked_s = held("picked_s", [P, J], U8)
+        v_s = [held("v_s%d" % a, [P, J], U8) for a in range(2)]
         wa_w = held("wa_w", [P, 2, R], U32)
         wa_s = held("wa_s", [P, 2, R], U8)
 
-        zero(tab_s[:, : 3 * T // 4])
-        nc.gpsimd.memset(tab_s[:, 3 * T // 4 :].bitcast(I32), 0)
+        zero(tab_s[:ROWS_AT, :])
         zero(tab2_s[:])
-        zero(v_s1[:])
-        raw00 = tenant("c", "wa_raw", [P, PACK, PASS], F32)
+        for plane in (v_s[0], v_s[1], v2_plane):
+            nc.gpsimd.memset(plane[:].bitcast(I32), 0)
+        raw00a = held("wa_raw00a", [P, PACK, EARLY], F32)
+        raw00 = placed(40, "wa_raw00", [P, PACK, PASS - EARLY], F32)
         nc.sync.dma_start(list1[:], offs)
-        nc.sync.dma_start(list2[:], offs2)
-        nc.sync.dma_start(out=raw00[:, 0, : PASS // 2], in_=wa_rows(0, 0)[:, 0, : PASS // 2])
-        load_scales(tab_s[:], tab_scales.rearrange("a (q r) t -> r q a t", r=4), SHIFT)
+        nc.sync.dma_start(out=tab_s[ROWS_AT:, :].bitcast(I32), in_=tab_scales.rearrange("a q t -> (a q) t").bitcast(I32))
+        nc.sync.dma_start(out=raw00a[:], in_=wa_rows(0, 0)[:, :, :EARLY])
         nc.sync.dma_start(out=tab_w[:], in_=words(tab_words[0]))
-        nc.sync.dma_start(out=raw00[:, 0, PASS // 2 :], in_=wa_rows(0, 0)[:, 0, PASS // 2 :])
-        nc.sync.dma_start(out=raw00[:, 1:, :], in_=wa_rows(0, 0)[:, 1:, :])
-        raw10 = load_wa(1, 0, "e")
-        raw01 = load_wa(0, 1, "g")
-        load_scales(tab2_s[TAB2_ROW:], tab2_scales[0].rearrange("(q r) t -> r q t", r=4), QUADRANT)
+        nc.sync.dma_start(list2[:], offs2)
+        nc.sync.dma_start(out=raw00[:], in_=wa_rows(0, 0)[:, :, EARLY:])
+
+        raw10 = load_wa(1, 0, 12)
+        nc.sync.dma_start(out=tab2_s[::8, :].bitcast(I32), in_=tab2_scales[0].bitcast(I32))
+
+        def move_scales(a, queue):
+            for q in range(4):
+                row = ROWS_AT + 16 * a + 4 * q
+                queue.dma_start(
+                    out=v_s[a][QUADRANT * q : QUADRANT * q + 4, :].bitcast(I32), in_=picked_s[row : row + 4, :].bitcast(I32)
+                )
 
         v_w = {}
         v2_w = {}
@@ -117,10 +131,14 @@ def tile_list_kg_mul_gelu_kernel(
         def gather_tab2_scales(c0, c1, place):
             picked = tenant(place, "v2_s", [P, CHUNK * (c1 - c0)], U8)
             nc.vector.tensor_copy(picked[:], tab2_s[:].indirect(entries(list2, c0, c1)))
-            return [picked[:, cols(c, c + 1)] for c in range(c1 - c0)]
+            for r in range(4):
+                nc.sync.dma_start(
+                    out=v2_plane[TAB2_ROW + r :: QUADRANT, cols(c0, c1)].bitcast(I32), in_=picked[8 * r :: QUADRANT, :].bitcast(I32)
+                )
+            return [v2_plane[:, cols(c, c + 1)] for c in range(c0, c1)]
 
-        def gather_tab2(c, place):
-            v2_w[c] = tenant(place, "v2_w", [P, CHUNK], U32)
+        def gather_tab2(c, picked):
+            v2_w[c] = picked
             nc.vector.tensor_copy(v2_w[c][:], tab2_w[:].bitcast(U32).indirect(entries(list2, c, c + 1)))
 
         def round_wa(copy, grouped, raw):
@@ -161,7 +179,7 @@ def tile_list_kg_mul_gelu_kernel(
                 lhsT=wa_w[:, a, r_cols(h, t)].bitcast(FP8X4),
                 lhsT_scale=wa_s[:, a, r_cols(h, t)],
                 rhs=v_w[c, a].bitcast(FP4X4),
-                rhs_scale=(v_s0, v_s1)[a][:, cols(c, c + 1)],
+                rhs_scale=v_s[a][:, cols(c, c + 1)],
                 start=(a == 0),
                 stop=(a == 1),
             )
@@ -230,9 +248,10 @@ def tile_list_kg_mul_gelu_kernel(
             nc.sync.dma_start(out=out[rows, cols(c, c + 1)], in_=result[:])
             emptied.append((bank, "scalar"))
 
-        nc.vector.tensor_copy(v_s0[:], tab_s[:].indirect(list1[:]))
-        nc.sync.dma_start(out=v_s1[0 : P - SHIFT, :].bitcast(I32), in_=v_s0[SHIFT:P, :].bitcast(I32))
-        raw11 = load_wa(1, 1, "a")
+        nc.vector.tensor_copy(picked_s[:], tab_s[:].indirect(list1[:]))
+        move_scales(0, nc.sync)
+        raw01 = load_wa(0, 1, 24)
+        move_scales(1, nc.sync)
 
         both01 = tenant("b", "both01", [P, 2, CHUNK], U32)
         for c in range(2):
@@ -240,28 +259,29 @@ def tile_list_kg_mul_gelu_kernel(
         v_first = held("v_first", [P, 1, 2 * CHUNK], U8)
         part_tab(both01[:, 0, :], 0, 1, v_first[:])
         g00 = new_grouped("x")
-        round_wa(nc.scalar.copy, g00[:, :, : P // 2, :], raw00[:, :, : PASS // 2])
-        round_wa(nc.vector.tensor_copy, g00[:, :, P // 2 :, :], raw00[:, :, PASS // 2 :])
+        round_wa(nc.scalar.copy, g00[:, :, : EARLY // PACK, :], raw00a[:])
+        round_wa(nc.scalar.copy, g00[:, :, EARLY // PACK : SPLIT // PACK, :], raw00[:, :, : SPLIT - EARLY])
+        round_wa(nc.vector.tensor_copy, g00[:, :, SPLIT // PACK :, :], raw00[:, :, SPLIT - EARLY :])
         quantize_wa(0, 0, g00)
+        raw11 = load_wa(1, 1, 44)
         v_next = tenant("x", "v_next", [P, 3, 2 * CHUNK], U8)
         part_tab(both01[:, 1, :], 0, 2, v_next[:, 0:2, :])
         part_tab(both01[:, 0, :], 1, 2, v_next[:, 2:3, :])
         v_w.update({(0, 0): v_first[:, 0, :], (0, 1): v_next[:, 2, :], (1, 0): v_next[:, 0, :], (1, 1): v_next[:, 1, :]})
-
-        wb = tenant("c", "wb", [P, R + R // 4], I32)
-        wb_w = wb[:, :R]
-        wb_s = wb[:, R:].bitcast(U8)
-        zero(wb_s)
-        load_scales(wb_s[WB_ROW:], wb_scales[0].rearrange("(q r) t -> r q t", r=4), QUADRANT)
-        nc.sync.dma_start(out=wb_w, in_=words(wb_words[0]))
 
         both23 = tenant("b", "both23", [P, 2 * CHUNK], U32)
         gather_tab(2, 4, both23[:])
         g10 = new_grouped("y")
         round_wa(nc.scalar.copy, g10[:], raw10[:])
         quantize_wa(1, 0, g10)
-        tab2_w = tenant("e", "tab2_w", [P, T], I32)
+        tab2_w = placed(0, "tab2_w", [P, T], I32)
         nc.sync.dma_start(out=tab2_w[:], in_=words(tab2_words[0]))
+        wb = placed(18, "wb", [P, R + R // 4], I32)
+        wb_w = wb[:, :R]
+        wb_s = wb[:, R:].bitcast(U8)
+        nc.sync.dma_start(out=wb_w, in_=words(wb_words[0]))
+        zero(wb_s)
+        load_scales(wb_s[WB_ROW:], wb_scales[0].rearrange("(q r) t -> r q t", r=4), QUADRANT)
         v_last = tenant("y", "v_last", [P, 2, 4 * CHUNK], U8)
         part_tab(both23[:], 0, 2, v_last[:])
         for c in range(2):
@@ -271,20 +291,11 @@ def tile_list_kg_mul_gelu_kernel(
         g01 = new_grouped("z")
         round_wa(nc.scalar.copy, g01[:], raw01[:])
         quantize_wa(0, 1, g01)
-        en = tenant("z", "en", [P, 2 * N + N // 4], I32)
-        en_w = en[:, : 2 * N].rearrange("p (a n) -> p a n", a=2)
-        en_s = en[:, 2 * N :].bitcast(U8)
-        nc.sync.dma_start(out=en_w, in_=en_words.rearrange("a p n i -> p a (n i)").bitcast(I32))
-        zero(en_s)
-        for q in range(4):
-            nc.sync.dma_start(
-                out=en[QUADRANT * q : QUADRANT * q + 2 * EN_ROWS, 2 * N :], in_=en_scales[:, 4 * q : 4 * q + 4, :].bitcast(I32)
-            )
         v2_s = gather_tab2_scales(0, 1, "b")
 
         g11 = new_grouped("w")
         round_wa(nc.vector.tensor_copy, g11[:], raw11[:])
-        wbp_w = tenant("a", "wbp_w", [P, R], I32)
+        wbp_w = held("wbp_w", [P, R], I32)
         wbp_s = held("wbp_s", [P, R], U8)
         nc.vector.tensor_copy(
             wbp_s[:].rearrange("p (h t m) -> p h t m", h=2, t=PACK), wb_s.rearrange("p (h m t) -> p h t m", h=2, t=PACK)
@@ -293,14 +304,23 @@ def tile_list_kg_mul_gelu_kernel(
         nc.vector.tensor_copy(
             wbp_w[:].rearrange("p (h t m) -> p h m t", h=2, t=PACK), wb_w.rearrange("p (h m t) -> p h m t", h=2, t=PACK)
         )
-        bias = tenant("c", "bias", [P, N // P], F32)
+        en = placed(48, "en", [P, 2 * N + N // 4], I32)
+        en_w = en[:, : 2 * N].rearrange("p (a n) -> p a n", a=2)
+        en_s = en[:, 2 * N :].bitcast(U8)
+        nc.sync.dma_start(out=en_w, in_=en_words.rearrange("a p n i -> p a (n i)").bitcast(I32))
+        zero(en_s)
+        for q in range(4):
+            nc.sync.dma_start(
+                out=en[QUADRANT * q : QUADRANT * q + 2 * EN_ROWS, 2 * N :], in_=en_scales[:, 4 * q : 4 * q + 4, :].bitcast(I32)
+            )
+        v2_s.extend(gather_tab2_scales(1, CHUNKS, "w"))
+        gather_tab2(0, tenant("v2_w0", "v2_w", [P, CHUNK], U32))
+        bias = placed(21, "bias", [P, N // P], F32)
         with nc.allow_non_contiguous_dma(reason="one bias value for each partition and output tile"):
             nc.sync.dma_start(out=bias[:], in_=b.rearrange("(c p) -> p c", p=P))
-        v2_s.extend(gather_tab2_scales(1, CHUNKS, "w"))
-        gather_tab2(0, "v2_w0")
-        gather_tab2(1, "v2_w1")
+        gather_tab2(1, placed(18, "v2_w1", [P, CHUNK], U32))
 
-        ha_first = tenant("g", "ha_first", [P, 2, PACK, CHUNK], F32)
+        ha_first = placed(24, "ha_first", [P, 2, PACK, CHUNK], F32)
         ha[0, 0] = ha_first[:, 0]
         ha[0, 1] = ha_first[:, 1]
         opened = [(take(free_for_wide()), 0, c, t) for c in range(2) for t in range(PACK)]
@@ -333,7 +353,10 @@ def tile_list_kg_mul_gelu_kernel(
                 if h == 0:
                     wide.extend([(make_out, (c - 1, n)) for n in range(N // P)])
                 elif gathers:
-                    gather_tab2(c + 1, ("g", "ha02")[c - 1])
+                    if c == 1:
+                        gather_tab2(2, placed(24, "v2_w2", [P, CHUNK], U32))
+                    else:
+                        gather_tab2(3, tenant("ha02", "v2_w", [P, CHUNK], U32))
             if h == 1 and u % 2 == 0:
                 fill(2 if gathers else 1 if c == 0 else 0)
             if u % 2 == 1:

@@ -26,13 +26,13 @@ UNIT = 128
 UNITS = CHUNK // UNIT
 LIST_COLS = CHUNK // 16
 BANKS = 8
-EARLY = 64
-SPLIT = 288
+LAST_PIECES = [(0, 2), (2, 2)]
+ROWS2_AT = 112
 ROWS_AT = 96
 TAB2_ROW = 4
 WB_ROW = 8
 EN_ROWS = 4
-ALONE = 25
+ALONE = 24
 LEAD = 2
 ROUNDED_TILES = 3
 H_TILES = 5
@@ -88,7 +88,7 @@ def tile_list_kg_mul_gelu_kernel(
         list1 = keep.tile([P, J // 16], U16, name="list1")
         list2 = keep.tile([P, J // 16], U16, name="list2")
         tab_w = held("tab_w", [P, T], I32)
-        tab_s = placed(22, "tab_s", [P, T], U8)
+        tab_s = placed(30, "tab_s", [P, T], U8)
         tab2_s = held("tab2_s", [P, T], U8)
         v2_plane = held("v2_plane", [P, J], U8)
         picked_s = held("picked_s", [P, J], U8)
@@ -97,20 +97,17 @@ def tile_list_kg_mul_gelu_kernel(
         wa_s = held("wa_s", [P, 2, R], U8)
 
         zero(tab_s[:ROWS_AT, :])
-        zero(tab2_s[:])
+        zero(tab2_s[:ROWS2_AT, :])
         for plane in (v_s[0], v_s[1], v2_plane):
             nc.gpsimd.memset(plane[:].bitcast(I32), 0)
-        raw00a = held("wa_raw00a", [P, PACK, EARLY], F32)
-        raw00 = placed(40, "wa_raw00", [P, PACK, PASS - EARLY], F32)
+        raw00 = held("wa_raw00", [P, PACK, PASS], F32)
         nc.sync.dma_start(list1[:], offs)
         nc.sync.dma_start(out=tab_s[ROWS_AT:, :].bitcast(I32), in_=tab_scales.rearrange("a q t -> (a q) t").bitcast(I32))
-        nc.sync.dma_start(out=raw00a[:], in_=wa_rows(0, 0)[:, :, :EARLY])
-        nc.sync.dma_start(out=tab_w[:], in_=words(tab_words[0]))
         nc.sync.dma_start(list2[:], offs2)
-        nc.sync.dma_start(out=raw00[:], in_=wa_rows(0, 0)[:, :, EARLY:])
-
+        nc.sync.dma_start(out=tab2_s[ROWS2_AT:, :].bitcast(I32), in_=tab2_scales[0].bitcast(I32))
+        nc.sync.dma_start(out=raw00[:], in_=wa_rows(0, 0))
+        nc.sync.dma_start(out=tab_w[:], in_=words(tab_words[0]))
         raw10 = load_wa(1, 0, 12)
-        nc.sync.dma_start(out=tab2_s[::8, :].bitcast(I32), in_=tab2_scales[0].bitcast(I32))
 
         def move_scales(a, queue):
             for q in range(4):
@@ -131,9 +128,11 @@ def tile_list_kg_mul_gelu_kernel(
         def gather_tab2_scales(c0, c1, place):
             picked = tenant(place, "v2_s", [P, CHUNK * (c1 - c0)], U8)
             nc.vector.tensor_copy(picked[:], tab2_s[:].indirect(entries(list2, c0, c1)))
-            for r in range(4):
+            for q in range(4):
+                row = QUADRANT * q + TAB2_ROW
                 nc.sync.dma_start(
-                    out=v2_plane[TAB2_ROW + r :: QUADRANT, cols(c0, c1)].bitcast(I32), in_=picked[8 * r :: QUADRANT, :].bitcast(I32)
+                    out=v2_plane[row : row + 4, cols(c0, c1)].bitcast(I32),
+                    in_=picked[ROWS2_AT + 4 * q : ROWS2_AT + 4 * q + 4, :].bitcast(I32),
                 )
             return [v2_plane[:, cols(c, c + 1)] for c in range(c0, c1)]
 
@@ -196,6 +195,9 @@ def tile_list_kg_mul_gelu_kernel(
             ha_pass(bank, h, c, t, 1)
             copy_ha(bank, h, c, t)
 
+        def piece_of(c, u):
+            return [piece for piece in (LAST_PIECES if c == CHUNKS - 1 else [(0, UNITS)]) if piece[0] <= u][-1]
+
         def make_hb(c, h, u):
             within = slice(UNIT * u, UNIT * (u + 1))
             hb[c, h, u] = take(free_for_hb())
@@ -211,12 +213,13 @@ def tile_list_kg_mul_gelu_kernel(
                 )
 
         def make_h(c, h, u):
-            if u == 0:
-                rounded[c, h] = ring.tile([P, CHUNK, PACK], BF16, name="rounded", bufs=ROUNDED_TILES, align_bytes=64)
+            first, count = piece_of(c, u)
+            if u == first:
+                rounded[c, h, first] = ring.tile([P, UNIT * count, PACK], BF16, name="rounded", bufs=ROUNDED_TILES, align_bytes=64)
             within = slice(UNIT * u, UNIT * (u + 1))
             bank = hb[c, h, u]
             nc.vector.tensor_tensor(
-                rounded[c, h][:, within, :].rearrange("p (g i) t -> p g t i", i=4),
+                rounded[c, h, first][:, UNIT * (u - first) : UNIT * (u - first + 1), :].rearrange("p (g i) t -> p g t i", i=4),
                 banks[bank][:].rearrange("p (t g i) -> p g t i", t=PACK, i=4),
                 ha[h, c][:, :, within].rearrange("p t (g i) -> p g t i", i=4),
                 MULT,
@@ -224,56 +227,69 @@ def tile_list_kg_mul_gelu_kernel(
             emptied.append((bank, "vector"))
             tied.add(bank)
 
-        def quantize_h(c, h):
-            h_w = ring.tile([P, CHUNK], U32, name="h_w", bufs=H_TILES, align_bytes=64)
-            h_s = ring.tile([P, CHUNK], U8, name="h_s", bufs=H_TILES, align_bytes=64)
-            nc.vector.quantize_mx(out=h_w[:].bitcast(FP8X4), scales=h_s[:], in_=rounded[c, h][:].rearrange("p j t -> p (j t)"))
-            hq[c, h] = (h_w, h_s)
+        def quantize_h(c, h, u):
+            first, count = piece_of(c, u)
+            h_w = ring.tile([P, UNIT * count], U32, name="h_w", bufs=H_TILES, align_bytes=64)
+            h_s = ring.tile([P, UNIT * count], U8, name="h_s", bufs=H_TILES, align_bytes=64)
+            nc.vector.quantize_mx(
+                out=h_w[:].bitcast(FP8X4), scales=h_s[:], in_=rounded[c, h, first][:].rearrange("p j t -> p (j t)")
+            )
+            hq[c, h, first] = (h_w, h_s)
 
-        def make_out(c, n):
-            rows = slice(P * n, P * (n + 1))
+        def make_out(c, first, n0):
+            width = UNIT * piece_of(c, first)[1]
+            tiles = CHUNK // width
             bank = take(free_for_wide())
-            for h in range(2):
-                nc.tensor.matmul_mx(
-                    out=banks[bank][:],
-                    lhsT=en_w[:, h, rows].bitcast(FP8X4),
-                    lhsT_scale=en_s[EN_ROWS * h :, rows],
-                    rhs=hq[c, h][0][:].bitcast(FP8X4),
-                    rhs_scale=hq[c, h][1][:],
-                    start=(h == 0),
-                    stop=(h == 1),
+            result = ring.tile([P, tiles, width], F32, name="result", bufs=RESULT_TILES)
+            for i in range(tiles):
+                for h in range(2):
+                    nc.tensor.matmul_mx(
+                        out=banks[bank][:, width * i : width * (i + 1)],
+                        lhsT=en_w[:, h, P * (n0 + i) : P * (n0 + i + 1)].bitcast(FP8X4),
+                        lhsT_scale=en_s[EN_ROWS * h :, P * (n0 + i) : P * (n0 + i + 1)],
+                        rhs=hq[c, h, first][0][:].bitcast(FP8X4),
+                        rhs_scale=hq[c, h, first][1][:],
+                        start=(h == 0),
+                        stop=(h == 1),
+                    )
+            for i in range(tiles):
+                nc.scalar.activation(
+                    result[:, i, :], banks[bank][:, width * i : width * (i + 1)], GELU, bias=bias[:, n0 + i : n0 + i + 1]
                 )
-            result = ring.tile([P, CHUNK], F32, name="result", bufs=RESULT_TILES)
-            nc.scalar.activation(result[:], banks[bank][:], GELU, bias=bias[:, n : n + 1])
-            nc.sync.dma_start(out=out[rows, cols(c, c + 1)], in_=result[:])
+            start = CHUNK * c + UNIT * first
+            rows = out[P * n0 : P * (n0 + tiles), start : start + width]
+            nc.sync.dma_start(out=rows.rearrange("(i p) j -> p i j", p=P), in_=result[:])
             emptied.append((bank, "scalar"))
+
+        def out_banks(c, first):
+            return [(make_out, (c, first, n0)) for n0 in range(0, N // P, UNITS // piece_of(c, first)[1])]
 
         nc.vector.tensor_copy(picked_s[:], tab_s[:].indirect(list1[:]))
         move_scales(0, nc.sync)
-        raw01 = load_wa(0, 1, 24)
+        raw01 = load_wa(0, 1, 32)
         move_scales(1, nc.sync)
-
-        both01 = tenant("b", "both01", [P, 2, CHUNK], U32)
-        for c in range(2):
-            gather_tab(c, c + 1, both01[:, c, :])
-        v_first = held("v_first", [P, 1, 2 * CHUNK], U8)
-        part_tab(both01[:, 0, :], 0, 1, v_first[:])
+        raw11 = load_wa(1, 1, 24)
+        v2_s = gather_tab2_scales(0, 1, "s2")
         g00 = new_grouped("x")
-        round_wa(nc.scalar.copy, g00[:, :, : EARLY // PACK, :], raw00a[:])
-        round_wa(nc.scalar.copy, g00[:, :, EARLY // PACK : SPLIT // PACK, :], raw00[:, :, : SPLIT - EARLY])
-        round_wa(nc.vector.tensor_copy, g00[:, :, SPLIT // PACK :, :], raw00[:, :, SPLIT - EARLY :])
+        round_wa(nc.scalar.copy, g00[:], raw00[:])
         quantize_wa(0, 0, g00)
-        raw11 = load_wa(1, 1, 44)
-        v_next = tenant("x", "v_next", [P, 3, 2 * CHUNK], U8)
-        part_tab(both01[:, 1, :], 0, 2, v_next[:, 0:2, :])
-        part_tab(both01[:, 0, :], 1, 2, v_next[:, 2:3, :])
-        v_w.update({(0, 0): v_first[:, 0, :], (0, 1): v_next[:, 2, :], (1, 0): v_next[:, 0, :], (1, 1): v_next[:, 1, :]})
 
-        both23 = tenant("b", "both23", [P, 2 * CHUNK], U32)
-        gather_tab(2, 4, both23[:])
+        both0 = placed(48, "both0", [P, 2 * CHUNK], U32)
+        parted = [held("parted%d" % c, [P, 2, 2 * CHUNK], U8) for c in range(3)]
+        gather_tab(0, 1, both0[:, :CHUNK])
+        part_tab(both0[:, :CHUNK], 0, 2, parted[0][:])
+        both1 = placed(48, "both1", [P, CHUNK], U32)
+        both2 = placed(50, "both2", [P, CHUNK], U32)
+        gather_tab(1, 2, both1[:])
+        gather_tab(2, 3, both2[:])
+        part_tab(both1[:], 0, 2, parted[1][:])
         g10 = new_grouped("y")
         round_wa(nc.scalar.copy, g10[:], raw10[:])
         quantize_wa(1, 0, g10)
+        part_tab(both2[:], 0, 2, parted[2][:])
+        for c in range(3):
+            for a in range(2):
+                v_w[c, a] = parted[c][:, a, :]
         tab2_w = placed(0, "tab2_w", [P, T], I32)
         nc.sync.dma_start(out=tab2_w[:], in_=words(tab2_words[0]))
         wb = placed(18, "wb", [P, R + R // 4], I32)
@@ -282,16 +298,16 @@ def tile_list_kg_mul_gelu_kernel(
         nc.sync.dma_start(out=wb_w, in_=words(wb_words[0]))
         zero(wb_s)
         load_scales(wb_s[WB_ROW:], wb_scales[0].rearrange("(q r) t -> r q t", r=4), QUADRANT)
-        v_last = tenant("y", "v_last", [P, 2, 4 * CHUNK], U8)
-        part_tab(both23[:], 0, 2, v_last[:])
-        for c in range(2):
-            for a in range(2):
-                v_w[2 + c, a] = v_last[:, a, 2 * CHUNK * c : 2 * CHUNK * (c + 1)]
+        both3 = tenant("y", "both3", [P, CHUNK], U32)
+        gather_tab(3, 4, both3[:])
+        v_last = held("v_last", [P, 2, 2 * CHUNK], U8)
+        part_tab(both3[:], 0, 2, v_last[:])
+        for a in range(2):
+            v_w[3, a] = v_last[:, a, :]
 
         g01 = new_grouped("z")
         round_wa(nc.scalar.copy, g01[:], raw01[:])
         quantize_wa(0, 1, g01)
-        v2_s = gather_tab2_scales(0, 1, "b")
 
         g11 = new_grouped("w")
         round_wa(nc.vector.tensor_copy, g11[:], raw11[:])
@@ -304,7 +320,7 @@ def tile_list_kg_mul_gelu_kernel(
         nc.vector.tensor_copy(
             wbp_w[:].rearrange("p (h t m) -> p h m t", h=2, t=PACK), wb_w.rearrange("p (h m t) -> p h m t", h=2, t=PACK)
         )
-        en = placed(48, "en", [P, 2 * N + N // 4], I32)
+        en = placed(23, "en", [P, 2 * N + N // 4], I32)
         en_w = en[:, : 2 * N].rearrange("p (a n) -> p a n", a=2)
         en_s = en[:, 2 * N :].bitcast(U8)
         nc.sync.dma_start(out=en_w, in_=en_words.rearrange("a p n i -> p a (n i)").bitcast(I32))
@@ -320,7 +336,7 @@ def tile_list_kg_mul_gelu_kernel(
             nc.sync.dma_start(out=bias[:], in_=b.rearrange("(c p) -> p c", p=P))
         gather_tab2(1, placed(18, "v2_w1", [P, CHUNK], U32))
 
-        ha_first = placed(24, "ha_first", [P, 2, PACK, CHUNK], F32)
+        ha_first = placed(32, "ha_first", [P, 2, PACK, CHUNK], F32)
         ha[0, 0] = ha_first[:, 0]
         ha[0, 1] = ha_first[:, 1]
         opened = [(take(free_for_wide()), 0, c, t) for c in range(2) for t in range(PACK)]
@@ -339,7 +355,8 @@ def tile_list_kg_mul_gelu_kernel(
                     make(*args)
 
         fill(ALONE - BANKS)
-        units = [(c, h, u) for c in range(CHUNKS) for h in range(2) for u in range(UNITS)]
+        units = [(c, h, u) for c in range(CHUNKS - 1) for h in range(2) for u in range(UNITS)]
+        units.extend([(CHUNKS - 1, h, u) for first, count in LAST_PIECES for h in range(2) for u in range(first, first + count)])
         for unit in units[:LEAD]:
             make_hb(*unit)
         for i, (c, h, u) in enumerate(units):
@@ -347,20 +364,19 @@ def tile_list_kg_mul_gelu_kernel(
             make_h(c, h, u)
             if i + LEAD < len(units):
                 make_hb(*units[i + LEAD])
-            if u == 0 and i > 0:
+            if u == piece_of(c, u)[0] and i > 0:
                 fill(1)
-                quantize_h(*units[i - 1][:2])
+                quantize_h(*units[i - 1])
                 if h == 0:
-                    wide.extend([(make_out, (c - 1, n)) for n in range(N // P)])
-                elif gathers:
-                    if c == 1:
-                        gather_tab2(2, placed(24, "v2_w2", [P, CHUNK], U32))
-                    else:
-                        gather_tab2(3, tenant("ha02", "v2_w", [P, CHUNK], U32))
+                    wide.extend(out_banks(units[i - 1][0], piece_of(units[i - 1][0], units[i - 1][2])[0]))
+                elif c == 1:
+                    gather_tab2(2, placed(32, "v2_w2", [P, CHUNK], U32))
+                elif c == 2:
+                    gather_tab2(3, tenant("ha02", "v2_w", [P, CHUNK], U32))
             if h == 1 and u % 2 == 0:
-                fill(2 if gathers else 1 if c == 0 else 0)
+                fill(2 if gathers else 1)
             if u % 2 == 1:
                 fill(1)
-        quantize_h(CHUNKS - 1, 1)
-        wide.extend([(make_out, (CHUNKS - 1, n)) for n in range(N // P)])
+        quantize_h(*units[-1])
+        wide.extend(out_banks(CHUNKS - 1, LAST_PIECES[-1][0]))
         fill(len(wide))

@@ -26,13 +26,13 @@ UNIT = 128
 UNITS = CHUNK // UNIT
 LIST_COLS = CHUNK // 16
 BANKS = 8
-LAST_PIECES = [(0, 2), (2, 2)]
+LAST_PIECES = [(0, 4)]
 ROWS2_AT = 112
 ROWS_AT = 96
-TAB2_ROW = 4
-WB_ROW = 8
+TAB2_ROW = 0
+WB_ROW = 4
 EN_ROWS = 4
-ALONE = 24
+ALONE = 26
 LEAD = 2
 ROUNDED_TILES = 3
 H_TILES = 5
@@ -85,6 +85,10 @@ def tile_list_kg_mul_gelu_kernel(
         def r_cols(h, t):
             return slice(PASS * h + P * t, PASS * h + P * (t + 1))
 
+        warm_in = held("warm_in", [P, 1], F32)
+        warm_out = held("warm_out", [P, 1], F32)
+        nc.gpsimd.memset(warm_in[:], 0.0)
+        nc.scalar.activation(warm_out[:], warm_in[:], GELU)
         list1 = keep.tile([P, J // 16], U16, name="list1")
         list2 = keep.tile([P, J // 16], U16, name="list2")
         tab_w = held("tab_w", [P, T], I32)
@@ -110,11 +114,9 @@ def tile_list_kg_mul_gelu_kernel(
         raw10 = load_wa(1, 0, 12)
 
         def move_scales(a, queue):
-            for q in range(4):
-                row = ROWS_AT + 16 * a + 4 * q
-                queue.dma_start(
-                    out=v_s[a][QUADRANT * q : QUADRANT * q + 4, :].bitcast(I32), in_=picked_s[row : row + 4, :].bitcast(I32)
-                )
+            for r in range(4):
+                row = ROWS_AT + 16 * a + r
+                queue.dma_start(out=v_s[a][r::QUADRANT, :].bitcast(I32), in_=picked_s[row : row + 13 : 4, :].bitcast(I32))
 
         v_w = {}
         v2_w = {}
@@ -128,11 +130,10 @@ def tile_list_kg_mul_gelu_kernel(
         def gather_tab2_scales(c0, c1, place):
             picked = tenant(place, "v2_s", [P, CHUNK * (c1 - c0)], U8)
             nc.vector.tensor_copy(picked[:], tab2_s[:].indirect(entries(list2, c0, c1)))
-            for q in range(4):
-                row = QUADRANT * q + TAB2_ROW
+            for r in range(4):
                 nc.sync.dma_start(
-                    out=v2_plane[row : row + 4, cols(c0, c1)].bitcast(I32),
-                    in_=picked[ROWS2_AT + 4 * q : ROWS2_AT + 4 * q + 4, :].bitcast(I32),
+                    out=v2_plane[TAB2_ROW + r :: QUADRANT, cols(c0, c1)].bitcast(I32),
+                    in_=picked[ROWS2_AT + r :: 4, :].bitcast(I32),
                 )
             return [v2_plane[:, cols(c, c + 1)] for c in range(c0, c1)]
 
@@ -205,7 +206,7 @@ def tile_list_kg_mul_gelu_kernel(
                 nc.tensor.matmul_mx(
                     out=banks[hb[c, h, u]][:, UNIT * t : UNIT * (t + 1)],
                     lhsT=wbp_w[:, r_cols(h, t)].bitcast(FP8X4),
-                    lhsT_scale=wbp_s[WB_ROW:, r_cols(h, t)],
+                    lhsT_scale=wbp_s[WB_ROW + 4 * h :, r_cols(0, t)],
                     rhs=v2_w[c][:, within].bitcast(FP8X4),
                     rhs_scale=v2_s[c][TAB2_ROW:, within],
                     start=True,
@@ -290,14 +291,18 @@ def tile_list_kg_mul_gelu_kernel(
         for c in range(3):
             for a in range(2):
                 v_w[c, a] = parted[c][:, a, :]
-        tab2_w = placed(0, "tab2_w", [P, T], I32)
-        nc.sync.dma_start(out=tab2_w[:], in_=words(tab2_words[0]))
-        wb = placed(18, "wb", [P, R + R // 4], I32)
+        wb = placed(18, "wb", [P, R + PASS // 4], I32)
         wb_w = wb[:, :R]
         wb_s = wb[:, R:].bitcast(U8)
         nc.sync.dma_start(out=wb_w, in_=words(wb_words[0]))
+        tab2_w = placed(0, "tab2_w", [P, T], I32)
+        nc.sync.dma_start(out=tab2_w[:], in_=words(tab2_words[0]))
         zero(wb_s)
-        load_scales(wb_s[WB_ROW:], wb_scales[0].rearrange("(q r) t -> r q t", r=4), QUADRANT)
+        for q in range(4):
+            row = QUADRANT * q + WB_ROW
+            nc.sync.dma_start(
+                out=wb[row : row + 8, R:], in_=wb_scales[0, 4 * q : 4 * q + 4, :].rearrange("r (h c) -> h r c", h=2).bitcast(I32)
+            )
         both3 = tenant("y", "both3", [P, CHUNK], U32)
         gather_tab(3, 4, both3[:])
         v_last = held("v_last", [P, 2, 2 * CHUNK], U8)
@@ -312,10 +317,8 @@ def tile_list_kg_mul_gelu_kernel(
         g11 = new_grouped("w")
         round_wa(nc.vector.tensor_copy, g11[:], raw11[:])
         wbp_w = held("wbp_w", [P, R], I32)
-        wbp_s = held("wbp_s", [P, R], U8)
-        nc.vector.tensor_copy(
-            wbp_s[:].rearrange("p (h t m) -> p h t m", h=2, t=PACK), wb_s.rearrange("p (h m t) -> p h t m", h=2, t=PACK)
-        )
+        wbp_s = held("wbp_s", [P, PASS], U8)
+        nc.vector.tensor_copy(wbp_s[:].rearrange("p (t m) -> p t m", t=PACK), wb_s.rearrange("p (m t) -> p t m", t=PACK))
         quantize_wa(1, 1, g11)
         nc.vector.tensor_copy(
             wbp_w[:].rearrange("p (h t m) -> p h m t", h=2, t=PACK), wb_w.rearrange("p (h m t) -> p h m t", h=2, t=PACK)

@@ -142,7 +142,7 @@ def tile_list_kg_mul_gelu_kernel(
             nc.vector.tensor_copy(v2_w[c][:], tab2_w[:].bitcast(U32).indirect(entries(list2, c, c + 1)))
 
         def round_wa(copy, grouped, raw):
-            copy(grouped.rearrange("p t m j -> p m j t"), raw.rearrange("p j (m t) -> p m j t", t=PACK))
+            copy(grouped.rearrange("p (u v) m j -> p u m j v", v=2), raw.rearrange("p j (m u v) -> p u m j v", u=2, v=2))
 
         def quantize_wa(a, h, grouped):
             half = slice(PASS * h, PASS * (h + 1))

@@ -270,7 +270,7 @@ def tile_list_kg_mul_gelu_kernel(
         raw01 = load_wa(0, 1, 32)
         move_scales(1, nc.sync)
         raw11 = load_wa(1, 1, 24)
-        v2_s = gather_tab2_scales(0, 1, "s2")
+        v2_s = gather_tab2_scales(0, 2, "s2")
         g00 = new_grouped("x")
         round_wa(nc.scalar.copy, g00[:], raw00[:])
         quantize_wa(0, 0, g00)
@@ -311,7 +311,7 @@ def tile_list_kg_mul_gelu_kernel(
             v_w[3, a] = v_last[:, a, :]
 
         g01 = new_grouped("z")
-        round_wa(nc.scalar.copy, g01[:], raw01[:])
+        round_wa(nc.vector.tensor_copy, g01[:], raw01[:])
         quantize_wa(0, 1, g01)
 
         g11 = new_grouped("w")
@@ -332,14 +332,14 @@ def tile_list_kg_mul_gelu_kernel(
             nc.sync.dma_start(
                 out=en[QUADRANT * q : QUADRANT * q + 2 * EN_ROWS, 2 * N :], in_=en_scales[:, 4 * q : 4 * q + 4, :].bitcast(I32)
             )
-        v2_s.extend(gather_tab2_scales(1, CHUNKS, "w"))
+        v2_s.extend(gather_tab2_scales(2, CHUNKS, "w"))
         gather_tab2(0, tenant("v2_w0", "v2_w", [P, CHUNK], U32))
         bias = placed(21, "bias", [P, N // P], F32)
         with nc.allow_non_contiguous_dma(reason="one bias value for each partition and output tile"):
             nc.sync.dma_start(out=bias[:], in_=b.rearrange("(c p) -> p c", p=P))
         gather_tab2(1, placed(18, "v2_w1", [P, CHUNK], U32))
 
-        ha_first = placed(32, "ha_first", [P, 2, PACK, CHUNK], F32)
+        ha_first = held("ha_first", [P, 2, PACK, CHUNK], F32)
         ha[0, 0] = ha_first[:, 0]
         ha[0, 1] = ha_first[:, 1]
         opened = [(take(free_for_wide()), 0, c, t) for c in range(2) for t in range(PACK)]
@@ -373,7 +373,7 @@ def tile_list_kg_mul_gelu_kernel(
                 if h == 0:
                     wide.extend(out_banks(units[i - 1][0], piece_of(units[i - 1][0], units[i - 1][2])[0]))
                 elif c == 1:
-                    gather_tab2(2, placed(32, "v2_w2", [P, CHUNK], U32))
+                    gather_tab2(2, tenant("ha_first", "v2_w2", [P, CHUNK], U32))
                 elif c == 2:
                     gather_tab2(3, tenant("ha02", "v2_w", [P, CHUNK], U32))
             if h == 1 and u % 2 == 0:

@@ -27,12 +27,12 @@ UNITS = CHUNK // UNIT
 LIST_COLS = CHUNK // 16
 BANKS = 8
 LAST_PIECES = [(0, 4)]
-ROWS2_AT = 112
+ROWS2_AT = 32
 ROWS_AT = 96
 TAB2_ROW = 0
 WB_ROW = 4
 EN_ROWS = 4
-ALONE = 26
+ALONE = 23
 LEAD = 2
 ROUNDED_TILES = 3
 H_TILES = 5
@@ -92,31 +92,34 @@ def tile_list_kg_mul_gelu_kernel(
         list1 = keep.tile([P, J // 16], U16, name="list1")
         list2 = keep.tile([P, J // 16], U16, name="list2")
         tab_w = held("tab_w", [P, T], I32)
-        tab_s = placed(30, "tab_s", [P, T], U8)
+        tab_s = held("tab_s", [P, T], U8)
         tab2_s = held("tab2_s", [P, T], U8)
         v2_plane = held("v2_plane", [P, J], U8)
         picked_s = held("picked_s", [P, J], U8)
-        v_s = [held("v_s%d" % a, [P, J], U8) for a in range(2)]
+        v_planes = held("v_planes", [P, 2 * J], U8)
+        v_s = [v_planes[:, J * a : J * (a + 1)] for a in range(2)]
         wa_w = held("wa_w", [P, 2, R], U32)
         wa_s = held("wa_s", [P, 2, R], U8)
 
         zero(tab_s[:ROWS_AT, :])
-        zero(tab2_s[:ROWS2_AT, :])
-        for plane in (v_s[0], v_s[1], v2_plane):
+        zero(tab2_s[:])
+        for plane in (v_planes, v2_plane):
             nc.gpsimd.memset(plane[:].bitcast(I32), 0)
         raw00 = held("wa_raw00", [P, PACK, PASS], F32)
         nc.sync.dma_start(list1[:], offs)
-        nc.sync.dma_start(out=tab_s[ROWS_AT:, :].bitcast(I32), in_=tab_scales.rearrange("a q t -> (a q) t").bitcast(I32))
-        nc.sync.dma_start(list2[:], offs2)
-        nc.sync.dma_start(out=tab2_s[ROWS2_AT:, :].bitcast(I32), in_=tab2_scales[0].bitcast(I32))
-        nc.sync.dma_start(out=raw00[:], in_=wa_rows(0, 0))
+        nc.sync.dma_start(out=tab_s[ROWS_AT:, :].bitcast(I32), in_=tab_scales.rearrange("a q t -> q a t").bitcast(I32))
         nc.sync.dma_start(out=tab_w[:], in_=words(tab_words[0]))
+        nc.sync.dma_start(out=raw00[:], in_=wa_rows(0, 0))
         raw10 = load_wa(1, 0, 12)
+        nc.sync.dma_start(list2[:], offs2)
+        nc.sync.dma_start(out=tab2_s[ROWS2_AT : ROWS2_AT + 64 : 4, :].bitcast(I32), in_=tab2_scales[0].bitcast(I32))
 
-        def move_scales(a, queue):
-            for r in range(4):
-                row = ROWS_AT + 16 * a + r
-                queue.dma_start(out=v_s[a][r::QUADRANT, :].bitcast(I32), in_=picked_s[row : row + 13 : 4, :].bitcast(I32))
+        def move_scales():
+            for q in range(4):
+                row = ROWS_AT + 8 * q
+                nc.scalar.dma_start(
+                    out=v_planes[QUADRANT * q : QUADRANT * q + 4, :].bitcast(I32), in_=picked_s[row : row + 8, :].bitcast(I32)
+                )
 
         v_w = {}
         v2_w = {}
@@ -127,15 +130,13 @@ def tile_list_kg_mul_gelu_kernel(
         def part_tab(both, a0, a1, parted):
             nc.vector.tensor_copy(parted.bitcast(U16), both.bitcast(U16).rearrange("p (j d) -> p d j", d=2)[:, a0:a1, :])
 
-        def gather_tab2_scales(c0, c1, place):
-            picked = tenant(place, "v2_s", [P, CHUNK * (c1 - c0)], U8)
+        def gather_tab2_scales(c0, c1, picked):
             nc.vector.tensor_copy(picked[:], tab2_s[:].indirect(entries(list2, c0, c1)))
             for r in range(4):
                 nc.sync.dma_start(
                     out=v2_plane[TAB2_ROW + r :: QUADRANT, cols(c0, c1)].bitcast(I32),
-                    in_=picked[ROWS2_AT + r :: 4, :].bitcast(I32),
+                    in_=picked[ROWS2_AT + 4 * r : ROWS2_AT + 64 : 16, :].bitcast(I32),
                 )
-            return [v2_plane[:, cols(c, c + 1)] for c in range(c0, c1)]
 
         def gather_tab2(c, picked):
             v2_w[c] = picked
@@ -150,8 +151,19 @@ def tile_list_kg_mul_gelu_kernel(
                 out=wa_w[:, a, half].bitcast(FP8X4), scales=wa_s[:, a, half], in_=grouped[:].rearrange("p t m j -> p (t m j)")
             )
 
-        def new_grouped(place):
-            return tenant(place, "grouped", [P, PACK, P, PACK], BF16)
+        def round_pair(a, u, raw):
+            if (a, u) == (0, 0):
+                grouped = placed(50, "pair00", [P, 2, P, PACK], BF16)
+            else:
+                grouped = tenant("pair%d%d" % (a, u), "grouped", [P, 2, P, PACK], BF16)
+            nc.scalar.copy(grouped[:].rearrange("p v m j -> p m j v"), raw.rearrange("p j (m u v) -> p u m j v", u=2, v=2)[:, u])
+            return grouped
+
+        def quantize_pair(a, u, grouped):
+            pair = slice(2 * P * u, 2 * P * (u + 1))
+            nc.vector.quantize_mx(
+                out=wa_w[:, a, pair].bitcast(FP8X4), scales=wa_s[:, a, pair], in_=grouped[:].rearrange("p v m j -> p (v m j)")
+            )
 
         banks = [psum.tile([P, CHUNK], F32, name="bank%d" % i) for i in range(BANKS)]
         emptied = [(i, "scalar") for i in range(BANKS)]
@@ -208,7 +220,7 @@ def tile_list_kg_mul_gelu_kernel(
                     lhsT=wbp_w[:, r_cols(h, t)].bitcast(FP8X4),
                     lhsT_scale=wbp_s[WB_ROW + 4 * h :, r_cols(0, t)],
                     rhs=v2_w[c][:, within].bitcast(FP8X4),
-                    rhs_scale=v2_s[c][TAB2_ROW:, within],
+                    rhs_scale=v2_plane[TAB2_ROW:, CHUNK * c + UNIT * u : CHUNK * c + UNIT * (u + 1)],
                     start=True,
                     stop=True,
                 )
@@ -266,31 +278,31 @@ def tile_list_kg_mul_gelu_kernel(
             return [(make_out, (c, first, n0)) for n0 in range(0, N // P, UNITS // piece_of(c, first)[1])]
 
         nc.vector.tensor_copy(picked_s[:], tab_s[:].indirect(list1[:]))
-        move_scales(0, nc.sync)
+        move_scales()
+        pairs = [[round_pair(a, u, raw[:]) for u in range(2)] for a, raw in enumerate((raw00, raw10))]
+        parted = {c: held("parted%d" % c, [P, 2, 2 * CHUNK], U8) for c in (0, 2, 3)}
+        both = [placed(kib, "both%d" % c, [P, CHUNK], U32) for c, kib in enumerate((31, 53))]
+        for c in range(2):
+            gather_tab(c, c + 1, both[c][:])
+        part_tab(both[0][:], 0, 2, parted[0][:])
         raw01 = load_wa(0, 1, 32)
-        move_scales(1, nc.sync)
         raw11 = load_wa(1, 1, 24)
-        v2_s = gather_tab2_scales(0, 2, "s2")
-        g00 = new_grouped("x")
-        round_wa(nc.scalar.copy, g00[:], raw00[:])
-        quantize_wa(0, 0, g00)
-
-        both0 = placed(48, "both0", [P, 2 * CHUNK], U32)
-        parted = [held("parted%d" % c, [P, 2, 2 * CHUNK], U8) for c in range(3)]
-        gather_tab(0, 1, both0[:, :CHUNK])
-        part_tab(both0[:, :CHUNK], 0, 2, parted[0][:])
-        both1 = placed(48, "both1", [P, CHUNK], U32)
-        both2 = placed(50, "both2", [P, CHUNK], U32)
-        gather_tab(1, 2, both1[:])
-        gather_tab(2, 3, both2[:])
-        part_tab(both1[:], 0, 2, parted[1][:])
-        g10 = new_grouped("y")
-        round_wa(nc.scalar.copy, g10[:], raw10[:])
-        quantize_wa(1, 0, g10)
-        part_tab(both2[:], 0, 2, parted[2][:])
-        for c in range(3):
+        quantize_pair(0, 0, pairs[0][0])
+        parted[1] = placed(49, "parted1", [P, 2, 2 * CHUNK], U8)
+        part_tab(both[1][:], 0, 2, parted[1][:])
+        for c in range(CHUNKS):
             for a in range(2):
                 v_w[c, a] = parted[c][:, a, :]
+        both2 = placed(51, "both2", [P, CHUNK], U32)
+        gather_tab(2, 3, both2[:])
+        quantize_pair(0, 1, pairs[0][1])
+        quantize_pair(1, 0, pairs[1][0])
+        part_tab(both2[:], 0, 2, parted[2][:])
+        quantize_pair(1, 1, pairs[1][1])
+        both3 = tenant("pair10", "both3", [P, CHUNK], U32)
+        gather_tab(3, 4, both3[:])
+        part_tab(both3[:], 0, 2, parted[3][:])
+
         wb = placed(18, "wb", [P, R + PASS // 4], I32)
         wb_w = wb[:, :R]
         wb_s = wb[:, R:].bitcast(U8)
@@ -303,36 +315,29 @@ def tile_list_kg_mul_gelu_kernel(
             nc.sync.dma_start(
                 out=wb[row : row + 8, R:], in_=wb_scales[0, 4 * q : 4 * q + 4, :].rearrange("r (h c) -> h r c", h=2).bitcast(I32)
             )
-        both3 = tenant("y", "both3", [P, CHUNK], U32)
-        gather_tab(3, 4, both3[:])
-        v_last = held("v_last", [P, 2, 2 * CHUNK], U8)
-        part_tab(both3[:], 0, 2, v_last[:])
-        for a in range(2):
-            v_w[3, a] = v_last[:, a, :]
 
-        g01 = new_grouped("z")
+        g01 = held("g01", [P, PACK, P, PACK], BF16)
         round_wa(nc.vector.tensor_copy, g01[:], raw01[:])
-        quantize_wa(0, 1, g01)
-
-        g11 = new_grouped("w")
+        g11 = placed(40, "g11", [P, PACK, P, PACK], BF16)
         round_wa(nc.vector.tensor_copy, g11[:], raw11[:])
+        quantize_wa(0, 1, g01)
+        quantize_wa(1, 1, g11)
+        gather_tab2_scales(0, 2, placed(40, "v2_s01", [P, 2 * CHUNK], U8))
         wbp_w = held("wbp_w", [P, R], I32)
         wbp_s = held("wbp_s", [P, PASS], U8)
         nc.vector.tensor_copy(wbp_s[:].rearrange("p (t m) -> p t m", t=PACK), wb_s.rearrange("p (m t) -> p t m", t=PACK))
-        quantize_wa(1, 1, g11)
         nc.vector.tensor_copy(
             wbp_w[:].rearrange("p (h t m) -> p h m t", h=2, t=PACK), wb_w.rearrange("p (h m t) -> p h m t", h=2, t=PACK)
         )
-        en = placed(23, "en", [P, 2 * N + N // 4], I32)
+        en = placed(40, "en", [P, 2 * N + N // 4], I32)
         en_w = en[:, : 2 * N].rearrange("p (a n) -> p a n", a=2)
         en_s = en[:, 2 * N :].bitcast(U8)
         nc.sync.dma_start(out=en_w, in_=en_words.rearrange("a p n i -> p a (n i)").bitcast(I32))
-        zero(en_s)
+        nc.gpsimd.memset(en_s.bitcast(I32), 0)
         for q in range(4):
             nc.sync.dma_start(
                 out=en[QUADRANT * q : QUADRANT * q + 2 * EN_ROWS, 2 * N :], in_=en_scales[:, 4 * q : 4 * q + 4, :].bitcast(I32)
             )
-        v2_s.extend(gather_tab2_scales(2, CHUNKS, "w"))
         gather_tab2(0, tenant("v2_w0", "v2_w", [P, CHUNK], U32))
         bias = placed(21, "bias", [P, N // P], F32)
         with nc.allow_non_contiguous_dma(reason="one bias value for each partition and output tile"):
@@ -342,7 +347,7 @@ def tile_list_kg_mul_gelu_kernel(
         ha_first = held("ha_first", [P, 2, PACK, CHUNK], F32)
         ha[0, 0] = ha_first[:, 0]
         ha[0, 1] = ha_first[:, 1]
-        opened = [(take(free_for_wide()), 0, c, t) for c in range(2) for t in range(PACK)]
+        opened = [(take(free_for_wide()), 0, c, 2 * u + v) for u in range(2) for c in range(2) for v in range(2)]
         for group in opened:
             ha_pass(*group, 0)
         for group in opened:
@@ -370,6 +375,8 @@ def tile_list_kg_mul_gelu_kernel(
             if u == piece_of(c, u)[0] and i > 0:
                 fill(1)
                 quantize_h(*units[i - 1])
+                if h == 0 and c == 1:
+                    gather_tab2_scales(2, CHUNKS, tenant("ha10", "v2_s23", [P, 2 * CHUNK], U8))
                 if h == 0:
                     wide.extend(out_banks(units[i - 1][0], piece_of(units[i - 1][0], units[i - 1][2])[0]))
                 elif c == 1:

@@ -32,7 +32,8 @@ ROWS_AT = 96
 TAB2_ROW = 0
 WB_ROW = 4
 EN_ROWS = 4
-ALONE = 23
+ALONE = 24
+WARM_PASSES = 4
 LEAD = 2
 ROUNDED_TILES = 3
 H_TILES = 5
@@ -56,7 +57,7 @@ def tile_list_kg_mul_gelu_kernel(
             return keep.tile(shape, dtype, name=name, tag=place, align_bytes=64)
 
         def placed(kib, name, shape, dtype):
-            return head.tile(shape, dtype, name=name, offset=1024 * kib, align_bytes=64)
+            return head.tile(shape, dtype, name=name, offset=int(1024 * kib), align_bytes=64)
 
         def words(dram):
             return dram.rearrange("p n i -> p (n i)").bitcast(I32)
@@ -106,6 +107,11 @@ def tile_list_kg_mul_gelu_kernel(
         for plane in (v_planes, v2_plane):
             nc.gpsimd.memset(plane[:].bitcast(I32), 0)
         raw00 = held("wa_raw00", [P, PACK, PASS], F32)
+        zeros = held("zeros", [P, PASS], BF16)
+        zeros_w = held("zeros_w", [P, P], U32)
+        zeros_s = held("zeros_s", [P, P], U8)
+        nc.gpsimd.memset(zeros[:], 0.0)
+        nc.vector.quantize_mx(out=zeros_w[:].bitcast(FP8X4), scales=zeros_s[:], in_=zeros[:])
         nc.sync.dma_start(list1[:], offs)
         nc.sync.dma_start(out=tab_s[ROWS_AT:, :].bitcast(I32), in_=tab_scales.rearrange("a q t -> q a t").bitcast(I32))
         nc.sync.dma_start(out=tab_w[:], in_=words(tab_words[0]))
@@ -152,8 +158,8 @@ def tile_list_kg_mul_gelu_kernel(
             )
 
         def round_pair(a, u, raw):
-            if (a, u) == (0, 0):
-                grouped = placed(50, "pair00", [P, 2, P, PACK], BF16)
+            if a == u:
+                grouped = placed(55 - 9 * a, "pair%d%d" % (a, u), [P, 2, P, PACK], BF16)
             else:
                 grouped = tenant("pair%d%d" % (a, u), "grouped", [P, 2, P, PACK], BF16)
             nc.scalar.copy(grouped[:].rearrange("p v m j -> p m j v"), raw.rearrange("p j (m u v) -> p u m j v", u=2, v=2)[:, u])
@@ -281,19 +287,29 @@ def tile_list_kg_mul_gelu_kernel(
         move_scales()
         pairs = [[round_pair(a, u, raw[:]) for u in range(2)] for a, raw in enumerate((raw00, raw10))]
         parted = {c: held("parted%d" % c, [P, 2, 2 * CHUNK], U8) for c in (0, 2, 3)}
-        both = [placed(kib, "both%d" % c, [P, CHUNK], U32) for c, kib in enumerate((31, 53))]
+        both = [placed(kib, "both%d" % c, [P, CHUNK], U32) for c, kib in enumerate((31, 58))]
         for c in range(2):
             gather_tab(c, c + 1, both[c][:])
+        for step in range(WARM_PASSES):
+            nc.tensor.matmul_mx(
+                out=banks[BANKS - 1][:],
+                lhsT=zeros_w[:].bitcast(FP8X4),
+                lhsT_scale=zeros_s[:],
+                rhs=both[0][:].bitcast(U8)[:, : 2 * CHUNK].bitcast(FP4X4),
+                rhs_scale=picked_s[:, :CHUNK],
+                start=True,
+                stop=True,
+            )
         part_tab(both[0][:], 0, 2, parted[0][:])
         raw01 = load_wa(0, 1, 32)
         raw11 = load_wa(1, 1, 24)
         quantize_pair(0, 0, pairs[0][0])
-        parted[1] = placed(49, "parted1", [P, 2, 2 * CHUNK], U8)
+        parted[1] = placed(54, "parted1", [P, 2, 2 * CHUNK], U8)
         part_tab(both[1][:], 0, 2, parted[1][:])
         for c in range(CHUNKS):
             for a in range(2):
                 v_w[c, a] = parted[c][:, a, :]
-        both2 = placed(51, "both2", [P, CHUNK], U32)
+        both2 = placed(56, "both2", [P, CHUNK], U32)
         gather_tab(2, 3, both2[:])
         quantize_pair(0, 1, pairs[0][1])
         quantize_pair(1, 0, pairs[1][0])
@@ -316,19 +332,23 @@ def tile_list_kg_mul_gelu_kernel(
                 out=wb[row : row + 8, R:], in_=wb_scales[0, 4 * q : 4 * q + 4, :].rearrange("r (h c) -> h r c", h=2).bitcast(I32)
             )
 
+        gather_tab2_scales(0, 1, placed(47, "v2_s0", [P, CHUNK], U8))
         g01 = held("g01", [P, PACK, P, PACK], BF16)
         round_wa(nc.vector.tensor_copy, g01[:], raw01[:])
-        g11 = placed(40, "g11", [P, PACK, P, PACK], BF16)
+        g11 = placed(48.5, "g11", [P, PACK, P, PACK], BF16)
         round_wa(nc.vector.tensor_copy, g11[:], raw11[:])
         quantize_wa(0, 1, g01)
         quantize_wa(1, 1, g11)
-        gather_tab2_scales(0, 2, placed(40, "v2_s01", [P, 2 * CHUNK], U8))
-        wbp_w = held("wbp_w", [P, R], I32)
-        wbp_s = held("wbp_s", [P, PASS], U8)
-        nc.vector.tensor_copy(wbp_s[:].rearrange("p (t m) -> p t m", t=PACK), wb_s.rearrange("p (m t) -> p t m", t=PACK))
-        nc.vector.tensor_copy(
-            wbp_w[:].rearrange("p (h t m) -> p h m t", h=2, t=PACK), wb_w.rearrange("p (h m t) -> p h m t", h=2, t=PACK)
-        )
+        gather_tab2(0, tenant("v2_w0", "v2_w", [P, CHUNK], U32))
+        gather_tab2_scales(1, 2, placed(48.5, "v2_s1", [P, CHUNK], U8))
+        wbp_w = placed(49.5, "wbp_w", [P, R], I32)
+        wbp_s = placed(49, "wbp_s", [P, PASS], U8)
+        nc.gpsimd.tensor_copy(wbp_s[:].rearrange("p (t m) -> p t m", t=PACK), wb_s.rearrange("p (m t) -> p t m", t=PACK))
+        for h in range(2):
+            half = slice(PASS * h, PASS * (h + 1))
+            nc.gpsimd.tensor_copy(
+                wbp_w[:, half].rearrange("p (t m) -> p t m", t=PACK), wb_w[:, half].rearrange("p (m t) -> p t m", t=PACK)
+            )
         en = placed(40, "en", [P, 2 * N + N // 4], I32)
         en_w = en[:, : 2 * N].rearrange("p (a n) -> p a n", a=2)
         en_s = en[:, 2 * N :].bitcast(U8)
@@ -338,11 +358,10 @@ def tile_list_kg_mul_gelu_kernel(
             nc.sync.dma_start(
                 out=en[QUADRANT * q : QUADRANT * q + 2 * EN_ROWS, 2 * N :], in_=en_scales[:, 4 * q : 4 * q + 4, :].bitcast(I32)
             )
-        gather_tab2(0, tenant("v2_w0", "v2_w", [P, CHUNK], U32))
         bias = placed(21, "bias", [P, N // P], F32)
         with nc.allow_non_contiguous_dma(reason="one bias value for each partition and output tile"):
             nc.sync.dma_start(out=bias[:], in_=b.rearrange("(c p) -> p c", p=P))
-        gather_tab2(1, placed(18, "v2_w1", [P, CHUNK], U32))
+        gather_tab2(1, held("v2_w1", [P, CHUNK], U32))
 
         ha_first = held("ha_first", [P, 2, PACK, CHUNK], F32)
         ha[0, 0] = ha_first[:, 0]

@@ -32,7 +32,7 @@ ROWS_AT = 96
 TAB2_ROW = 0
 WB_ROW = 4
 EN_ROWS = 4
-ALONE = 24
+ALONE = 26
 WARM_PASSES = 4
 LEAD = 2
 ROUNDED_TILES = 3
@@ -86,6 +86,8 @@ def tile_list_kg_mul_gelu_kernel(
         def r_cols(h, t):
             return slice(PASS * h + P * t, PASS * h + P * (t + 1))
 
+        zeros = held("zeros", [P, PASS], BF16)
+        nc.gpsimd.memset(zeros[:], 0.0)
         warm_in = held("warm_in", [P, 1], F32)
         warm_out = held("warm_out", [P, 1], F32)
         nc.gpsimd.memset(warm_in[:], 0.0)
@@ -107,18 +109,17 @@ def tile_list_kg_mul_gelu_kernel(
         for plane in (v_planes, v2_plane):
             nc.gpsimd.memset(plane[:].bitcast(I32), 0)
         raw00 = held("wa_raw00", [P, PACK, PASS], F32)
-        zeros = held("zeros", [P, PASS], BF16)
         zeros_w = held("zeros_w", [P, P], U32)
         zeros_s = held("zeros_s", [P, P], U8)
-        nc.gpsimd.memset(zeros[:], 0.0)
         nc.vector.quantize_mx(out=zeros_w[:].bitcast(FP8X4), scales=zeros_s[:], in_=zeros[:])
         nc.sync.dma_start(list1[:], offs)
         nc.sync.dma_start(out=tab_s[ROWS_AT:, :].bitcast(I32), in_=tab_scales.rearrange("a q t -> q a t").bitcast(I32))
         nc.sync.dma_start(out=tab_w[:], in_=words(tab_words[0]))
         nc.sync.dma_start(out=raw00[:], in_=wa_rows(0, 0))
-        raw10 = load_wa(1, 0, 12)
+        raw10 = load_wa(1, 0, 0)
         nc.sync.dma_start(list2[:], offs2)
         nc.sync.dma_start(out=tab2_s[ROWS2_AT : ROWS2_AT + 64 : 4, :].bitcast(I32), in_=tab2_scales[0].bitcast(I32))
+        raw01 = load_wa(0, 1, 8)
 
         def move_scales():
             for q in range(4):
@@ -159,7 +160,7 @@ def tile_list_kg_mul_gelu_kernel(
 
         def round_pair(a, u, raw):
             if a == u:
-                grouped = placed(55 - 9 * a, "pair%d%d" % (a, u), [P, 2, P, PACK], BF16)
+                grouped = placed(49 - 3 * a, "pair%d%d" % (a, u), [P, 2, P, PACK], BF16)
             else:
                 grouped = tenant("pair%d%d" % (a, u), "grouped", [P, 2, P, PACK], BF16)
             nc.scalar.copy(grouped[:].rearrange("p v m j -> p m j v"), raw.rearrange("p j (m u v) -> p u m j v", u=2, v=2)[:, u])
@@ -287,7 +288,7 @@ def tile_list_kg_mul_gelu_kernel(
         move_scales()
         pairs = [[round_pair(a, u, raw[:]) for u in range(2)] for a, raw in enumerate((raw00, raw10))]
         parted = {c: held("parted%d" % c, [P, 2, 2 * CHUNK], U8) for c in (0, 2, 3)}
-        both = [placed(kib, "both%d" % c, [P, CHUNK], U32) for c, kib in enumerate((31, 58))]
+        both = [placed(kib, "both%d" % c, [P, CHUNK], U32) for c, kib in enumerate((23, 44))]
         for c in range(2):
             gather_tab(c, c + 1, both[c][:])
         for step in range(WARM_PASSES):
@@ -301,15 +302,14 @@ def tile_list_kg_mul_gelu_kernel(
                 stop=True,
             )
         part_tab(both[0][:], 0, 2, parted[0][:])
-        raw01 = load_wa(0, 1, 32)
-        raw11 = load_wa(1, 1, 24)
+        raw11 = load_wa(1, 1, 16)
         quantize_pair(0, 0, pairs[0][0])
-        parted[1] = placed(54, "parted1", [P, 2, 2 * CHUNK], U8)
+        parted[1] = placed(48, "parted1", [P, 2, 2 * CHUNK], U8)
         part_tab(both[1][:], 0, 2, parted[1][:])
         for c in range(CHUNKS):
             for a in range(2):
                 v_w[c, a] = parted[c][:, a, :]
-        both2 = placed(56, "both2", [P, CHUNK], U32)
+        both2 = placed(50, "both2", [P, CHUNK], U32)
         gather_tab(2, 3, both2[:])
         quantize_pair(0, 1, pairs[0][1])
         quantize_pair(1, 0, pairs[1][0])
@@ -319,37 +319,35 @@ def tile_list_kg_mul_gelu_kernel(
         gather_tab(3, 4, both3[:])
         part_tab(both3[:], 0, 2, parted[3][:])
 
-        wb = placed(18, "wb", [P, R + PASS // 4], I32)
+        wb = placed(24, "wb", [P, R + PASS // 4], I32)
         wb_w = wb[:, :R]
         wb_s = wb[:, R:].bitcast(U8)
         nc.sync.dma_start(out=wb_w, in_=words(wb_words[0]))
-        tab2_w = placed(0, "tab2_w", [P, T], I32)
-        nc.sync.dma_start(out=tab2_w[:], in_=words(tab2_words[0]))
         zero(wb_s)
         for q in range(4):
             row = QUADRANT * q + WB_ROW
             nc.sync.dma_start(
                 out=wb[row : row + 8, R:], in_=wb_scales[0, 4 * q : 4 * q + 4, :].rearrange("r (h c) -> h r c", h=2).bitcast(I32)
             )
+        tab2_w = placed(29, "tab2_w", [P, T], I32)
+        nc.sync.dma_start(out=tab2_w[:], in_=words(tab2_words[0]))
 
         gather_tab2_scales(0, 1, placed(47, "v2_s0", [P, CHUNK], U8))
         g01 = held("g01", [P, PACK, P, PACK], BF16)
         round_wa(nc.vector.tensor_copy, g01[:], raw01[:])
-        g11 = placed(48.5, "g11", [P, PACK, P, PACK], BF16)
+        g11 = placed(8, "g11", [P, PACK, P, PACK], BF16)
         round_wa(nc.vector.tensor_copy, g11[:], raw11[:])
         quantize_wa(0, 1, g01)
         quantize_wa(1, 1, g11)
+        wbp_w = held("wbp_w", [P, R], I32)
+        wbp_s = held("wbp_s", [P, PASS], U8)
+        nc.vector.tensor_copy(wbp_s[:].rearrange("p (t m) -> p t m", t=PACK), wb_s.rearrange("p (m t) -> p t m", t=PACK))
+        nc.vector.tensor_copy(
+            wbp_w[:].rearrange("p (h t m) -> p h m t", h=2, t=PACK), wb_w.rearrange("p (h m t) -> p h m t", h=2, t=PACK)
+        )
+        gather_tab2_scales(1, 3, placed(8, "v2_s12", [P, 2 * CHUNK], U8))
         gather_tab2(0, tenant("v2_w0", "v2_w", [P, CHUNK], U32))
-        gather_tab2_scales(1, 2, placed(48.5, "v2_s1", [P, CHUNK], U8))
-        wbp_w = placed(49.5, "wbp_w", [P, R], I32)
-        wbp_s = placed(49, "wbp_s", [P, PASS], U8)
-        nc.gpsimd.tensor_copy(wbp_s[:].rearrange("p (t m) -> p t m", t=PACK), wb_s.rearrange("p (m t) -> p t m", t=PACK))
-        for h in range(2):
-            half = slice(PASS * h, PASS * (h + 1))
-            nc.gpsimd.tensor_copy(
-                wbp_w[:, half].rearrange("p (t m) -> p t m", t=PACK), wb_w[:, half].rearrange("p (m t) -> p t m", t=PACK)
-            )
-        en = placed(40, "en", [P, 2 * N + N // 4], I32)
+        en = placed(0, "en", [P, 2 * N + N // 4], I32)
         en_w = en[:, : 2 * N].rearrange("p (a n) -> p a n", a=2)
         en_s = en[:, 2 * N :].bitcast(U8)
         nc.sync.dma_start(out=en_w, in_=en_words.rearrange("a p n i -> p a (n i)").bitcast(I32))
@@ -358,7 +356,7 @@ def tile_list_kg_mul_gelu_kernel(
             nc.sync.dma_start(
                 out=en[QUADRANT * q : QUADRANT * q + 2 * EN_ROWS, 2 * N :], in_=en_scales[:, 4 * q : 4 * q + 4, :].bitcast(I32)
             )
-        bias = placed(21, "bias", [P, N // P], F32)
+        bias = placed(27, "bias", [P, N // P], F32)
         with nc.allow_non_contiguous_dma(reason="one bias value for each partition and output tile"):
             nc.sync.dma_start(out=bias[:], in_=b.rearrange("(c p) -> p c", p=P))
         gather_tab2(1, held("v2_w1", [P, CHUNK], U32))
@@ -395,7 +393,7 @@ def tile_list_kg_mul_gelu_kernel(
                 fill(1)
                 quantize_h(*units[i - 1])
                 if h == 0 and c == 1:
-                    gather_tab2_scales(2, CHUNKS, tenant("ha10", "v2_s23", [P, 2 * CHUNK], U8))
+                    gather_tab2_scales(3, CHUNKS, tenant("ha10", "v2_s3", [P, CHUNK], U8))
                 if h == 0:
                     wide.extend(out_banks(units[i - 1][0], piece_of(units[i - 1][0], units[i - 1][2])[0]))
                 elif c == 1:

@@ -32,12 +32,12 @@ ROWS_AT = 96
 TAB2_ROW = 0
 WB_ROW = 4
 EN_ROWS = 4
-ALONE = 26
-WARM_PASSES = 4
+ALONE = 23
+WARM_PASSES = 5
 LEAD = 2
 ROUNDED_TILES = 3
 H_TILES = 5
-RESULT_TILES = 6
+RESULT_TILES = 8
 
 
 def tile_list_kg_mul_gelu_kernel(
@@ -95,7 +95,7 @@ def tile_list_kg_mul_gelu_kernel(
         list1 = keep.tile([P, J // 16], U16, name="list1")
         list2 = keep.tile([P, J // 16], U16, name="list2")
         tab_w = held("tab_w", [P, T], I32)
-        tab_s = held("tab_s", [P, T], U8)
+        tab_s = placed(37, "tab_s", [P, T], U8)
         tab2_s = held("tab2_s", [P, T], U8)
         v2_plane = held("v2_plane", [P, J], U8)
         picked_s = held("picked_s", [P, J], U8)
@@ -108,23 +108,21 @@ def tile_list_kg_mul_gelu_kernel(
         zero(tab2_s[:])
         for plane in (v_planes, v2_plane):
             nc.gpsimd.memset(plane[:].bitcast(I32), 0)
-        raw00 = held("wa_raw00", [P, PACK, PASS], F32)
         zeros_w = held("zeros_w", [P, P], U32)
         zeros_s = held("zeros_s", [P, P], U8)
         nc.vector.quantize_mx(out=zeros_w[:].bitcast(FP8X4), scales=zeros_s[:], in_=zeros[:])
         nc.sync.dma_start(list1[:], offs)
         nc.sync.dma_start(out=tab_s[ROWS_AT:, :].bitcast(I32), in_=tab_scales.rearrange("a q t -> q a t").bitcast(I32))
         nc.sync.dma_start(out=tab_w[:], in_=words(tab_words[0]))
-        nc.sync.dma_start(out=raw00[:], in_=wa_rows(0, 0))
-        raw10 = load_wa(1, 0, 0)
+        raw00 = load_wa(0, 0, 14)
+        raw10 = load_wa(1, 0, 23)
         nc.sync.dma_start(list2[:], offs2)
         nc.sync.dma_start(out=tab2_s[ROWS2_AT : ROWS2_AT + 64 : 4, :].bitcast(I32), in_=tab2_scales[0].bitcast(I32))
-        raw01 = load_wa(0, 1, 8)
 
         def move_scales():
             for q in range(4):
                 row = ROWS_AT + 8 * q
-                nc.scalar.dma_start(
+                nc.sync.dma_start(
                     out=v_planes[QUADRANT * q : QUADRANT * q + 4, :].bitcast(I32), in_=picked_s[row : row + 8, :].bitcast(I32)
                 )
 
@@ -159,10 +157,7 @@ def tile_list_kg_mul_gelu_kernel(
             )
 
         def round_pair(a, u, raw):
-            if a == u:
-                grouped = placed(49 - 3 * a, "pair%d%d" % (a, u), [P, 2, P, PACK], BF16)
-            else:
-                grouped = tenant("pair%d%d" % (a, u), "grouped", [P, 2, P, PACK], BF16)
+            grouped = held("pair%d%d" % (a, u), [P, 2, P, PACK], BF16)
             nc.scalar.copy(grouped[:].rearrange("p v m j -> p m j v"), raw.rearrange("p j (m u v) -> p u m j v", u=2, v=2)[:, u])
             return grouped
 
@@ -286,9 +281,12 @@ def tile_list_kg_mul_gelu_kernel(
 
         nc.vector.tensor_copy(picked_s[:], tab_s[:].indirect(list1[:]))
         move_scales()
+        raw01 = [placed(kib, "wa_raw01%d" % w, [P, PACK, PASS // 2], F32) for w, kib in enumerate((40, 34))]
+        for w in range(2):
+            nc.sync.dma_start(out=raw01[w][:], in_=wa_rows(0, 1)[:, :, PASS // 2 * w : PASS // 2 * (w + 1)])
         pairs = [[round_pair(a, u, raw[:]) for u in range(2)] for a, raw in enumerate((raw00, raw10))]
-        parted = {c: held("parted%d" % c, [P, 2, 2 * CHUNK], U8) for c in (0, 2, 3)}
-        both = [placed(kib, "both%d" % c, [P, CHUNK], U32) for c, kib in enumerate((23, 44))]
+        parted = [held("parted%d" % c, [P, 2, 2 * CHUNK], U8) for c in range(CHUNKS)]
+        both = [placed(66, "both0", [P, CHUNK], U32), held("both1", [P, CHUNK], U32)]
         for c in range(2):
             gather_tab(c, c + 1, both[c][:])
         for step in range(WARM_PASSES):
@@ -302,52 +300,54 @@ def tile_list_kg_mul_gelu_kernel(
                 stop=True,
             )
         part_tab(both[0][:], 0, 2, parted[0][:])
-        raw11 = load_wa(1, 1, 16)
-        quantize_pair(0, 0, pairs[0][0])
-        parted[1] = placed(48, "parted1", [P, 2, 2 * CHUNK], U8)
+        raw11 = load_wa(1, 1, 59)
         part_tab(both[1][:], 0, 2, parted[1][:])
+        quantize_pair(0, 0, pairs[0][0])
+        quantize_pair(0, 1, pairs[0][1])
         for c in range(CHUNKS):
             for a in range(2):
                 v_w[c, a] = parted[c][:, a, :]
-        both2 = placed(50, "both2", [P, CHUNK], U32)
+        both2 = placed(16, "both2", [P, CHUNK], U32)
         gather_tab(2, 3, both2[:])
-        quantize_pair(0, 1, pairs[0][1])
         quantize_pair(1, 0, pairs[1][0])
         part_tab(both2[:], 0, 2, parted[2][:])
         quantize_pair(1, 1, pairs[1][1])
-        both3 = tenant("pair10", "both3", [P, CHUNK], U32)
-        gather_tab(3, 4, both3[:])
-        part_tab(both3[:], 0, 2, parted[3][:])
-
-        wb = placed(24, "wb", [P, R + PASS // 4], I32)
+        wb = placed(18, "wb", [P, R + PASS // 4], I32)
         wb_w = wb[:, :R]
         wb_s = wb[:, R:].bitcast(U8)
         nc.sync.dma_start(out=wb_w, in_=words(wb_words[0]))
-        zero(wb_s)
+        nc.gpsimd.memset(wb_s.bitcast(I32), 0)
         for q in range(4):
             row = QUADRANT * q + WB_ROW
             nc.sync.dma_start(
                 out=wb[row : row + 8, R:], in_=wb_scales[0, 4 * q : 4 * q + 4, :].rearrange("r (h c) -> h r c", h=2).bitcast(I32)
             )
-        tab2_w = placed(29, "tab2_w", [P, T], I32)
+        tab2_w = placed(0, "tab2_w", [P, T], I32)
         nc.sync.dma_start(out=tab2_w[:], in_=words(tab2_words[0]))
 
-        gather_tab2_scales(0, 1, placed(47, "v2_s0", [P, CHUNK], U8))
+        both3 = placed(23, "both3", [P, CHUNK], U32)
+        gather_tab(3, 4, both3[:])
+        gather_tab2_scales(0, 1, placed(30.5, "v2_s0", [P, CHUNK], U8))
+        part_tab(both3[:], 0, 2, parted[3][:])
+
         g01 = held("g01", [P, PACK, P, PACK], BF16)
-        round_wa(nc.vector.tensor_copy, g01[:], raw01[:])
-        g11 = placed(8, "g11", [P, PACK, P, PACK], BF16)
+        for w, copy in enumerate((nc.scalar.copy, nc.vector.tensor_copy)):
+            round_wa(copy, g01[:, :, P // 2 * w : P // 2 * (w + 1), :], raw01[w][:])
+        g11 = placed(25, "g11", [P, PACK, P, PACK], BF16)
         round_wa(nc.vector.tensor_copy, g11[:], raw11[:])
         quantize_wa(0, 1, g01)
         quantize_wa(1, 1, g11)
-        wbp_w = held("wbp_w", [P, R], I32)
-        wbp_s = held("wbp_s", [P, PASS], U8)
-        nc.vector.tensor_copy(wbp_s[:].rearrange("p (t m) -> p t m", t=PACK), wb_s.rearrange("p (m t) -> p t m", t=PACK))
-        nc.vector.tensor_copy(
-            wbp_w[:].rearrange("p (h t m) -> p h m t", h=2, t=PACK), wb_w.rearrange("p (h m t) -> p h m t", h=2, t=PACK)
-        )
-        gather_tab2_scales(1, 3, placed(8, "v2_s12", [P, 2 * CHUNK], U8))
+        wbp_w = placed(26.5, "wbp_w", [P, R], I32)
+        wbp_s = placed(26, "wbp_s", [P, PASS], U8)
+        nc.gpsimd.tensor_copy(wbp_s[:].rearrange("p (t m) -> p t m", t=PACK), wb_s.rearrange("p (m t) -> p t m", t=PACK))
+        for h in range(2):
+            half = slice(PASS * h, PASS * (h + 1))
+            nc.gpsimd.tensor_copy(
+                wbp_w[:, half].rearrange("p (t m) -> p t m", t=PACK), wb_w[:, half].rearrange("p (m t) -> p t m", t=PACK)
+            )
         gather_tab2(0, tenant("v2_w0", "v2_w", [P, CHUNK], U32))
-        en = placed(0, "en", [P, 2 * N + N // 4], I32)
+        gather_tab2_scales(1, 3, placed(25, "v2_s12", [P, 2 * CHUNK], U8))
+        en = placed(17, "en", [P, 2 * N + N // 4], I32)
         en_w = en[:, : 2 * N].rearrange("p (a n) -> p a n", a=2)
         en_s = en[:, 2 * N :].bitcast(U8)
         nc.sync.dma_start(out=en_w, in_=en_words.rearrange("a p n i -> p a (n i)").bitcast(I32))
@@ -356,12 +356,12 @@ def tile_list_kg_mul_gelu_kernel(
             nc.sync.dma_start(
                 out=en[QUADRANT * q : QUADRANT * q + 2 * EN_ROWS, 2 * N :], in_=en_scales[:, 4 * q : 4 * q + 4, :].bitcast(I32)
             )
-        bias = placed(27, "bias", [P, N // P], F32)
+        bias = placed(30.5, "bias", [P, N // P], F32)
         with nc.allow_non_contiguous_dma(reason="one bias value for each partition and output tile"):
             nc.sync.dma_start(out=bias[:], in_=b.rearrange("(c p) -> p c", p=P))
         gather_tab2(1, held("v2_w1", [P, CHUNK], U32))
 
-        ha_first = held("ha_first", [P, 2, PACK, CHUNK], F32)
+        ha_first = placed(43, "ha_first", [P, 2, PACK, CHUNK], F32)
         ha[0, 0] = ha_first[:, 0]
         ha[0, 1] = ha_first[:, 1]
         opened = [(take(free_for_wide()), 0, c, 2 * u + v) for u in range(2) for c in range(2) for v in range(2)]
@@ -397,7 +397,7 @@ def tile_list_kg_mul_gelu_kernel(
                 if h == 0:
                     wide.extend(out_banks(units[i - 1][0], piece_of(units[i - 1][0], units[i - 1][2])[0]))
                 elif c == 1:
-                    gather_tab2(2, tenant("ha_first", "v2_w2", [P, CHUNK], U32))
+                    gather_tab2(2, placed(51, "v2_w2", [P, CHUNK], U32))
                 elif c == 2:
                     gather_tab2(3, tenant("ha02", "v2_w", [P, CHUNK], U32))
             if h == 1 and u % 2 == 0:

@@ -26,18 +26,27 @@ UNIT = 128
 UNITS = CHUNK // UNIT
 LIST_COLS = CHUNK // 16
 BANKS = 8
-LAST_PIECES = [(0, 4)]
-ROWS2_AT = 32
-ROWS_AT = 96
-TAB2_ROW = 0
+TAB_ROWS_AT = 96
+TAB2_ROWS_AT = 32
 WB_ROW = 4
-EN_ROWS = 4
+EN_ROW = 4
 ALONE = 23
-WARM_PASSES = 5
 LEAD = 2
 ROUNDED_TILES = 3
 H_TILES = 5
 RESULT_TILES = 8
+
+PLACES = {
+    "wa00": 14, "tab2_w": 0, "both2": 16, "wb": 18,
+    "wa10": 23, "both3": 23, "picked2_0": 30.5,
+    "bias": 30.5,
+    "tab_s": 37, "wa01_0": 40, "wa01_1": 34,
+    "ha_first": 43,
+    "both0": 66, "wa11": 59,
+    "grouped11": 25, "picked2_1": 25, "wb_sorted_s": 26, "wb_sorted_w": 26.5,
+    "en": 17,
+    "v2_w2": 51,
+}
 
 
 def tile_list_kg_mul_gelu_kernel(
@@ -53,29 +62,20 @@ def tile_list_kg_mul_gelu_kernel(
         def held(name, shape, dtype):
             return keep.tile(shape, dtype, name=name, align_bytes=64)
 
-        def tenant(place, name, shape, dtype):
-            return keep.tile(shape, dtype, name=name, tag=place, align_bytes=64)
+        def tenant(tag, name, shape, dtype):
+            return keep.tile(shape, dtype, name=name, tag=tag, align_bytes=64)
 
-        def placed(kib, name, shape, dtype):
-            return head.tile(shape, dtype, name=name, offset=int(1024 * kib), align_bytes=64)
+        def placed(name, shape, dtype):
+            return head.tile(shape, dtype, name=name, offset=int(1024 * PLACES[name]), align_bytes=64)
 
         def words(dram):
             return dram.rearrange("p n i -> p (n i)").bitcast(I32)
 
-        def zero(plane):
-            nc.vector.memset(plane.bitcast(I32), 0)
-
-        def wa_rows(a, h):
-            return wa[PASS * a : PASS * (a + 1), PASS * h : PASS * (h + 1)].rearrange("(p j) c -> p j c", j=PACK)
-
-        def load_wa(a, h, kib):
-            raw = placed(kib, "wa_raw%d%d" % (a, h), [P, PACK, PASS], F32)
-            nc.sync.dma_start(out=raw[:], in_=wa_rows(a, h))
+        def load_wa(name, a, h, c0, c1):
+            raw = placed(name, [P, PACK, c1 - c0], F32)
+            rows = wa[PASS * a : PASS * (a + 1), PASS * h + c0 : PASS * h + c1]
+            nc.sync.dma_start(out=raw[:], in_=rows.rearrange("(p j) c -> p j c", j=PACK))
             return raw
-
-        def load_scales(plane, by_row, step):
-            for r in range(4):
-                nc.sync.dma_start(out=plane[r::step].bitcast(I32), in_=by_row[r].bitcast(I32))
 
         def cols(c0, c1):
             return slice(CHUNK * c0, CHUNK * c1)
@@ -86,85 +86,65 @@ def tile_list_kg_mul_gelu_kernel(
         def r_cols(h, t):
             return slice(PASS * h + P * t, PASS * h + P * (t + 1))
 
-        zeros = held("zeros", [P, PASS], BF16)
-        nc.gpsimd.memset(zeros[:], 0.0)
-        warm_in = held("warm_in", [P, 1], F32)
-        warm_out = held("warm_out", [P, 1], F32)
-        nc.gpsimd.memset(warm_in[:], 0.0)
-        nc.scalar.activation(warm_out[:], warm_in[:], GELU)
         list1 = keep.tile([P, J // 16], U16, name="list1")
         list2 = keep.tile([P, J // 16], U16, name="list2")
         tab_w = held("tab_w", [P, T], I32)
-        tab_s = placed(37, "tab_s", [P, T], U8)
+        tab_s = placed("tab_s", [P, T], U8)
         tab2_s = held("tab2_s", [P, T], U8)
         v2_plane = held("v2_plane", [P, J], U8)
         picked_s = held("picked_s", [P, J], U8)
         v_planes = held("v_planes", [P, 2 * J], U8)
-        v_s = [v_planes[:, J * a : J * (a + 1)] for a in range(2)]
         wa_w = held("wa_w", [P, 2, R], U32)
         wa_s = held("wa_s", [P, 2, R], U8)
 
-        zero(tab_s[:ROWS_AT, :])
-        zero(tab2_s[:])
+        nc.vector.memset(tab_s[:TAB_ROWS_AT, :].bitcast(I32), 0)
+        nc.vector.memset(tab2_s[:].bitcast(I32), 0)
         for plane in (v_planes, v2_plane):
             nc.gpsimd.memset(plane[:].bitcast(I32), 0)
-        zeros_w = held("zeros_w", [P, P], U32)
-        zeros_s = held("zeros_s", [P, P], U8)
-        nc.vector.quantize_mx(out=zeros_w[:].bitcast(FP8X4), scales=zeros_s[:], in_=zeros[:])
         nc.sync.dma_start(list1[:], offs)
-        nc.sync.dma_start(out=tab_s[ROWS_AT:, :].bitcast(I32), in_=tab_scales.rearrange("a q t -> q a t").bitcast(I32))
+        nc.sync.dma_start(out=tab_s[TAB_ROWS_AT:, :].bitcast(I32), in_=tab_scales.rearrange("a q t -> q a t").bitcast(I32))
         nc.sync.dma_start(out=tab_w[:], in_=words(tab_words[0]))
-        raw00 = load_wa(0, 0, 14)
-        raw10 = load_wa(1, 0, 23)
+        raw00 = load_wa("wa00", 0, 0, 0, PASS)
+        raw10 = load_wa("wa10", 1, 0, 0, PASS)
         nc.sync.dma_start(list2[:], offs2)
-        nc.sync.dma_start(out=tab2_s[ROWS2_AT : ROWS2_AT + 64 : 4, :].bitcast(I32), in_=tab2_scales[0].bitcast(I32))
-
-        def move_scales():
-            for q in range(4):
-                row = ROWS_AT + 8 * q
-                nc.sync.dma_start(
-                    out=v_planes[QUADRANT * q : QUADRANT * q + 4, :].bitcast(I32), in_=picked_s[row : row + 8, :].bitcast(I32)
-                )
+        nc.sync.dma_start(out=tab2_s[TAB2_ROWS_AT : TAB2_ROWS_AT + 64 : 4, :].bitcast(I32), in_=tab2_scales[0].bitcast(I32))
 
         v_w = {}
         v2_w = {}
 
-        def gather_tab(c0, c1, both):
-            nc.vector.tensor_copy(both, tab_w[:].bitcast(U32).indirect(entries(list1, c0, c1)))
+        def gather_tab(c, both):
+            nc.vector.tensor_copy(both[:], tab_w[:].bitcast(U32).indirect(entries(list1, c, c + 1)))
+            return both
 
-        def part_tab(both, a0, a1, parted):
-            nc.vector.tensor_copy(parted.bitcast(U16), both.bitcast(U16).rearrange("p (j d) -> p d j", d=2)[:, a0:a1, :])
+        def part_tab(c, both, parted):
+            nc.vector.tensor_copy(parted[:].bitcast(U16), both[:].bitcast(U16).rearrange("p (j d) -> p d j", d=2))
+            for a in range(2):
+                v_w[c, a] = parted[:, a, :]
 
         def gather_tab2_scales(c0, c1, picked):
             nc.vector.tensor_copy(picked[:], tab2_s[:].indirect(entries(list2, c0, c1)))
-            for r in range(4):
+            for s in range(4):
                 nc.sync.dma_start(
-                    out=v2_plane[TAB2_ROW + r :: QUADRANT, cols(c0, c1)].bitcast(I32),
-                    in_=picked[ROWS2_AT + 4 * r : ROWS2_AT + 64 : 16, :].bitcast(I32),
+                    out=v2_plane[s::QUADRANT, cols(c0, c1)].bitcast(I32),
+                    in_=picked[TAB2_ROWS_AT + 4 * s : TAB2_ROWS_AT + 64 : 16, :].bitcast(I32),
                 )
 
         def gather_tab2(c, picked):
             v2_w[c] = picked
-            nc.vector.tensor_copy(v2_w[c][:], tab2_w[:].bitcast(U32).indirect(entries(list2, c, c + 1)))
+            nc.vector.tensor_copy(picked[:], tab2_w[:].bitcast(U32).indirect(entries(list2, c, c + 1)))
 
         def round_wa(copy, grouped, raw):
             copy(grouped.rearrange("p (u v) m j -> p u m j v", v=2), raw.rearrange("p j (m u v) -> p u m j v", u=2, v=2))
-
-        def quantize_wa(a, h, grouped):
-            half = slice(PASS * h, PASS * (h + 1))
-            nc.vector.quantize_mx(
-                out=wa_w[:, a, half].bitcast(FP8X4), scales=wa_s[:, a, half], in_=grouped[:].rearrange("p t m j -> p (t m j)")
-            )
 
         def round_pair(a, u, raw):
             grouped = held("pair%d%d" % (a, u), [P, 2, P, PACK], BF16)
             nc.scalar.copy(grouped[:].rearrange("p v m j -> p m j v"), raw.rearrange("p j (m u v) -> p u m j v", u=2, v=2)[:, u])
             return grouped
 
-        def quantize_pair(a, u, grouped):
-            pair = slice(2 * P * u, 2 * P * (u + 1))
+        def quantize_wa(a, r0, grouped):
+            span = slice(r0, r0 + P * grouped.shape[1])
             nc.vector.quantize_mx(
-                out=wa_w[:, a, pair].bitcast(FP8X4), scales=wa_s[:, a, pair], in_=grouped[:].rearrange("p v m j -> p (v m j)")
+                out=wa_w[:, a, span].bitcast(FP8X4), scales=wa_s[:, a, span], in_=grouped[:].rearrange("p t m j -> p (t m j)")
             )
 
         banks = [psum.tile([P, CHUNK], F32, name="bank%d" % i) for i in range(BANKS)]
@@ -193,7 +173,7 @@ def tile_list_kg_mul_gelu_kernel(
                 lhsT=wa_w[:, a, r_cols(h, t)].bitcast(FP8X4),
                 lhsT_scale=wa_s[:, a, r_cols(h, t)],
                 rhs=v_w[c, a].bitcast(FP4X4),
-                rhs_scale=v_s[a][:, cols(c, c + 1)],
+                rhs_scale=v_planes[:, J * a + CHUNK * c : J * a + CHUNK * (c + 1)],
                 start=(a == 0),
                 stop=(a == 1),
             )
@@ -210,31 +190,26 @@ def tile_list_kg_mul_gelu_kernel(
             ha_pass(bank, h, c, t, 1)
             copy_ha(bank, h, c, t)
 
-        def piece_of(c, u):
-            return [piece for piece in (LAST_PIECES if c == CHUNKS - 1 else [(0, UNITS)]) if piece[0] <= u][-1]
-
         def make_hb(c, h, u):
-            within = slice(UNIT * u, UNIT * (u + 1))
             hb[c, h, u] = take(free_for_hb())
             for t in range(PACK):
                 nc.tensor.matmul_mx(
                     out=banks[hb[c, h, u]][:, UNIT * t : UNIT * (t + 1)],
-                    lhsT=wbp_w[:, r_cols(h, t)].bitcast(FP8X4),
-                    lhsT_scale=wbp_s[WB_ROW + 4 * h :, r_cols(0, t)],
-                    rhs=v2_w[c][:, within].bitcast(FP8X4),
-                    rhs_scale=v2_plane[TAB2_ROW:, CHUNK * c + UNIT * u : CHUNK * c + UNIT * (u + 1)],
+                    lhsT=wb_sorted_w[:, r_cols(h, t)].bitcast(FP8X4),
+                    lhsT_scale=wb_sorted_s[WB_ROW + 4 * h :, r_cols(0, t)],
+                    rhs=v2_w[c][:, UNIT * u : UNIT * (u + 1)].bitcast(FP8X4),
+                    rhs_scale=v2_plane[:, CHUNK * c + UNIT * u : CHUNK * c + UNIT * (u + 1)],
                     start=True,
                     stop=True,
                 )
 
         def make_h(c, h, u):
-            first, count = piece_of(c, u)
-            if u == first:
-                rounded[c, h, first] = ring.tile([P, UNIT * count, PACK], BF16, name="rounded", bufs=ROUNDED_TILES, align_bytes=64)
+            if u == 0:
+                rounded[c, h] = ring.tile([P, CHUNK, PACK], BF16, name="rounded", bufs=ROUNDED_TILES, align_bytes=64)
             within = slice(UNIT * u, UNIT * (u + 1))
             bank = hb[c, h, u]
             nc.vector.tensor_tensor(
-                rounded[c, h, first][:, UNIT * (u - first) : UNIT * (u - first + 1), :].rearrange("p (g i) t -> p g t i", i=4),
+                rounded[c, h][:, within, :].rearrange("p (g i) t -> p g t i", i=4),
                 banks[bank][:].rearrange("p (t g i) -> p g t i", t=PACK, i=4),
                 ha[h, c][:, :, within].rearrange("p t (g i) -> p g t i", i=4),
                 MULT,
@@ -242,77 +217,55 @@ def tile_list_kg_mul_gelu_kernel(
             emptied.append((bank, "vector"))
             tied.add(bank)
 
-        def quantize_h(c, h, u):
-            first, count = piece_of(c, u)
-            h_w = ring.tile([P, UNIT * count], U32, name="h_w", bufs=H_TILES, align_bytes=64)
-            h_s = ring.tile([P, UNIT * count], U8, name="h_s", bufs=H_TILES, align_bytes=64)
-            nc.vector.quantize_mx(
-                out=h_w[:].bitcast(FP8X4), scales=h_s[:], in_=rounded[c, h, first][:].rearrange("p j t -> p (j t)")
-            )
-            hq[c, h, first] = (h_w, h_s)
+        def quantize_h(c, h):
+            h_w = ring.tile([P, CHUNK], U32, name="h_w", bufs=H_TILES, align_bytes=64)
+            h_s = ring.tile([P, CHUNK], U8, name="h_s", bufs=H_TILES, align_bytes=64)
+            nc.vector.quantize_mx(out=h_w[:].bitcast(FP8X4), scales=h_s[:], in_=rounded[c, h][:].rearrange("p j t -> p (j t)"))
+            hq[c, h] = (h_w, h_s)
 
-        def make_out(c, first, n0):
-            width = UNIT * piece_of(c, first)[1]
-            tiles = CHUNK // width
+        def make_out(c, n):
             bank = take(free_for_wide())
-            result = ring.tile([P, tiles, width], F32, name="result", bufs=RESULT_TILES)
-            for i in range(tiles):
-                for h in range(2):
-                    nc.tensor.matmul_mx(
-                        out=banks[bank][:, width * i : width * (i + 1)],
-                        lhsT=en_w[:, h, P * (n0 + i) : P * (n0 + i + 1)].bitcast(FP8X4),
-                        lhsT_scale=en_s[EN_ROWS * h :, P * (n0 + i) : P * (n0 + i + 1)],
-                        rhs=hq[c, h, first][0][:].bitcast(FP8X4),
-                        rhs_scale=hq[c, h, first][1][:],
-                        start=(h == 0),
-                        stop=(h == 1),
-                    )
-            for i in range(tiles):
-                nc.scalar.activation(
-                    result[:, i, :], banks[bank][:, width * i : width * (i + 1)], GELU, bias=bias[:, n0 + i : n0 + i + 1]
+            result = ring.tile([P, CHUNK], F32, name="result", bufs=RESULT_TILES)
+            for h in range(2):
+                nc.tensor.matmul_mx(
+                    out=banks[bank][:],
+                    lhsT=en_w[:, h, P * n : P * (n + 1)].bitcast(FP8X4),
+                    lhsT_scale=en_s[EN_ROW * h :, P * n : P * (n + 1)],
+                    rhs=hq[c, h][0][:].bitcast(FP8X4),
+                    rhs_scale=hq[c, h][1][:],
+                    start=(h == 0),
+                    stop=(h == 1),
                 )
-            start = CHUNK * c + UNIT * first
-            rows = out[P * n0 : P * (n0 + tiles), start : start + width]
-            nc.sync.dma_start(out=rows.rearrange("(i p) j -> p i j", p=P), in_=result[:])
+            nc.scalar.activation(result[:], banks[bank][:], GELU, bias=bias[:, n : n + 1])
+            nc.sync.dma_start(out=out[P * n : P * (n + 1), cols(c, c + 1)], in_=result[:])
             emptied.append((bank, "scalar"))
 
-        def out_banks(c, first):
-            return [(make_out, (c, first, n0)) for n0 in range(0, N // P, UNITS // piece_of(c, first)[1])]
+        def out_banks(c):
+            return [(make_out, (c, n)) for n in range(N // P)]
 
         nc.vector.tensor_copy(picked_s[:], tab_s[:].indirect(list1[:]))
-        move_scales()
-        raw01 = [placed(kib, "wa_raw01%d" % w, [P, PACK, PASS // 2], F32) for w, kib in enumerate((40, 34))]
-        for w in range(2):
-            nc.sync.dma_start(out=raw01[w][:], in_=wa_rows(0, 1)[:, :, PASS // 2 * w : PASS // 2 * (w + 1)])
+        for q in range(4):
+            row = TAB_ROWS_AT + 8 * q
+            nc.sync.dma_start(
+                out=v_planes[QUADRANT * q : QUADRANT * q + 4, :].bitcast(I32), in_=picked_s[row : row + 8, :].bitcast(I32)
+            )
+        raw01 = [load_wa("wa01_%d" % w, 0, 1, PASS // 2 * w, PASS // 2 * (w + 1)) for w in range(2)]
+
         pairs = [[round_pair(a, u, raw[:]) for u in range(2)] for a, raw in enumerate((raw00, raw10))]
         parted = [held("parted%d" % c, [P, 2, 2 * CHUNK], U8) for c in range(CHUNKS)]
-        both = [placed(66, "both0", [P, CHUNK], U32), held("both1", [P, CHUNK], U32)]
-        for c in range(2):
-            gather_tab(c, c + 1, both[c][:])
-        for step in range(WARM_PASSES):
-            nc.tensor.matmul_mx(
-                out=banks[BANKS - 1][:],
-                lhsT=zeros_w[:].bitcast(FP8X4),
-                lhsT_scale=zeros_s[:],
-                rhs=both[0][:].bitcast(U8)[:, : 2 * CHUNK].bitcast(FP4X4),
-                rhs_scale=picked_s[:, :CHUNK],
-                start=True,
-                stop=True,
-            )
-        part_tab(both[0][:], 0, 2, parted[0][:])
-        raw11 = load_wa(1, 1, 59)
-        part_tab(both[1][:], 0, 2, parted[1][:])
-        quantize_pair(0, 0, pairs[0][0])
-        quantize_pair(0, 1, pairs[0][1])
-        for c in range(CHUNKS):
-            for a in range(2):
-                v_w[c, a] = parted[c][:, a, :]
-        both2 = placed(16, "both2", [P, CHUNK], U32)
-        gather_tab(2, 3, both2[:])
-        quantize_pair(1, 0, pairs[1][0])
-        part_tab(both2[:], 0, 2, parted[2][:])
-        quantize_pair(1, 1, pairs[1][1])
-        wb = placed(18, "wb", [P, R + PASS // 4], I32)
+        both0 = gather_tab(0, placed("both0", [P, CHUNK], U32))
+        both1 = gather_tab(1, held("both1", [P, CHUNK], U32))
+        part_tab(0, both0, parted[0])
+        raw11 = load_wa("wa11", 1, 1, 0, PASS)
+        part_tab(1, both1, parted[1])
+        quantize_wa(0, 0, pairs[0][0])
+        quantize_wa(0, 2 * P, pairs[0][1])
+        both2 = gather_tab(2, placed("both2", [P, CHUNK], U32))
+        quantize_wa(1, 0, pairs[1][0])
+        part_tab(2, both2, parted[2])
+        quantize_wa(1, 2 * P, pairs[1][1])
+
+        wb = placed("wb", [P, R + PASS // 4], I32)
         wb_w = wb[:, :R]
         wb_s = wb[:, R:].bitcast(U8)
         nc.sync.dma_start(out=wb_w, in_=words(wb_words[0]))
@@ -320,48 +273,49 @@ def tile_list_kg_mul_gelu_kernel(
         for q in range(4):
             row = QUADRANT * q + WB_ROW
             nc.sync.dma_start(
-                out=wb[row : row + 8, R:], in_=wb_scales[0, 4 * q : 4 * q + 4, :].rearrange("r (h c) -> h r c", h=2).bitcast(I32)
+                out=wb[row : row + 8, R:], in_=wb_scales[0, 4 * q : 4 * q + 4, :].rearrange("s (h c) -> h s c", h=2).bitcast(I32)
             )
-        tab2_w = placed(0, "tab2_w", [P, T], I32)
+        tab2_w = placed("tab2_w", [P, T], I32)
         nc.sync.dma_start(out=tab2_w[:], in_=words(tab2_words[0]))
 
-        both3 = placed(23, "both3", [P, CHUNK], U32)
-        gather_tab(3, 4, both3[:])
-        gather_tab2_scales(0, 1, placed(30.5, "v2_s0", [P, CHUNK], U8))
-        part_tab(both3[:], 0, 2, parted[3][:])
+        both3 = gather_tab(3, placed("both3", [P, CHUNK], U32))
+        gather_tab2_scales(0, 1, placed("picked2_0", [P, CHUNK], U8))
+        part_tab(3, both3, parted[3])
 
-        g01 = held("g01", [P, PACK, P, PACK], BF16)
+        grouped01 = held("grouped01", [P, PACK, P, PACK], BF16)
         for w, copy in enumerate((nc.scalar.copy, nc.vector.tensor_copy)):
-            round_wa(copy, g01[:, :, P // 2 * w : P // 2 * (w + 1), :], raw01[w][:])
-        g11 = placed(25, "g11", [P, PACK, P, PACK], BF16)
-        round_wa(nc.vector.tensor_copy, g11[:], raw11[:])
-        quantize_wa(0, 1, g01)
-        quantize_wa(1, 1, g11)
-        wbp_w = placed(26.5, "wbp_w", [P, R], I32)
-        wbp_s = placed(26, "wbp_s", [P, PASS], U8)
-        nc.gpsimd.tensor_copy(wbp_s[:].rearrange("p (t m) -> p t m", t=PACK), wb_s.rearrange("p (m t) -> p t m", t=PACK))
+            round_wa(copy, grouped01[:, :, P // 2 * w : P // 2 * (w + 1), :], raw01[w][:])
+        grouped11 = placed("grouped11", [P, PACK, P, PACK], BF16)
+        round_wa(nc.vector.tensor_copy, grouped11[:], raw11[:])
+        quantize_wa(0, PASS, grouped01)
+        quantize_wa(1, PASS, grouped11)
+
+        wb_sorted_w = placed("wb_sorted_w", [P, R], I32)
+        wb_sorted_s = placed("wb_sorted_s", [P, PASS], U8)
+        nc.gpsimd.tensor_copy(wb_sorted_s[:].rearrange("p (t m) -> p t m", t=PACK), wb_s.rearrange("p (m t) -> p t m", t=PACK))
         for h in range(2):
             half = slice(PASS * h, PASS * (h + 1))
             nc.gpsimd.tensor_copy(
-                wbp_w[:, half].rearrange("p (t m) -> p t m", t=PACK), wb_w[:, half].rearrange("p (m t) -> p t m", t=PACK)
+                wb_sorted_w[:, half].rearrange("p (t m) -> p t m", t=PACK), wb_w[:, half].rearrange("p (m t) -> p t m", t=PACK)
             )
-        gather_tab2(0, tenant("v2_w0", "v2_w", [P, CHUNK], U32))
-        gather_tab2_scales(1, 3, placed(25, "v2_s12", [P, 2 * CHUNK], U8))
-        en = placed(17, "en", [P, 2 * N + N // 4], I32)
+        gather_tab2(0, held("v2_w0", [P, CHUNK], U32))
+        gather_tab2_scales(1, 3, placed("picked2_1", [P, 2 * CHUNK], U8))
+
+        en = placed("en", [P, 2 * N + N // 4], I32)
         en_w = en[:, : 2 * N].rearrange("p (a n) -> p a n", a=2)
         en_s = en[:, 2 * N :].bitcast(U8)
         nc.sync.dma_start(out=en_w, in_=en_words.rearrange("a p n i -> p a (n i)").bitcast(I32))
         nc.gpsimd.memset(en_s.bitcast(I32), 0)
         for q in range(4):
             nc.sync.dma_start(
-                out=en[QUADRANT * q : QUADRANT * q + 2 * EN_ROWS, 2 * N :], in_=en_scales[:, 4 * q : 4 * q + 4, :].bitcast(I32)
+                out=en[QUADRANT * q : QUADRANT * q + 2 * EN_ROW, 2 * N :], in_=en_scales[:, 4 * q : 4 * q + 4, :].bitcast(I32)
             )
-        bias = placed(30.5, "bias", [P, N // P], F32)
+        bias = placed("bias", [P, N // P], F32)
         with nc.allow_non_contiguous_dma(reason="one bias value for each partition and output tile"):
             nc.sync.dma_start(out=bias[:], in_=b.rearrange("(c p) -> p c", p=P))
         gather_tab2(1, held("v2_w1", [P, CHUNK], U32))
 
-        ha_first = placed(43, "ha_first", [P, 2, PACK, CHUNK], F32)
+        ha_first = placed("ha_first", [P, 2, PACK, CHUNK], F32)
         ha[0, 0] = ha_first[:, 0]
         ha[0, 1] = ha_first[:, 1]
         opened = [(take(free_for_wide()), 0, c, 2 * u + v) for u in range(2) for c in range(2) for v in range(2)]
@@ -380,8 +334,7 @@ def tile_list_kg_mul_gelu_kernel(
                     make(*args)
 
         fill(ALONE - BANKS)
-        units = [(c, h, u) for c in range(CHUNKS - 1) for h in range(2) for u in range(UNITS)]
-        units.extend([(CHUNKS - 1, h, u) for first, count in LAST_PIECES for h in range(2) for u in range(first, first + count)])
+        units = [(c, h, u) for c in range(CHUNKS) for h in range(2) for u in range(UNITS)]
         for unit in units[:LEAD]:
             make_hb(*unit)
         for i, (c, h, u) in enumerate(units):
@@ -389,21 +342,21 @@ def tile_list_kg_mul_gelu_kernel(
             make_h(c, h, u)
             if i + LEAD < len(units):
                 make_hb(*units[i + LEAD])
-            if u == piece_of(c, u)[0] and i > 0:
+            if u == 0 and i > 0:
                 fill(1)
-                quantize_h(*units[i - 1])
+                quantize_h(*units[i - 1][:2])
                 if h == 0 and c == 1:
-                    gather_tab2_scales(3, CHUNKS, tenant("ha10", "v2_s3", [P, CHUNK], U8))
+                    gather_tab2_scales(3, CHUNKS, tenant("ha10", "picked2_3", [P, CHUNK], U8))
                 if h == 0:
-                    wide.extend(out_banks(units[i - 1][0], piece_of(units[i - 1][0], units[i - 1][2])[0]))
+                    wide.extend(out_banks(c - 1))
                 elif c == 1:
-                    gather_tab2(2, placed(51, "v2_w2", [P, CHUNK], U32))
+                    gather_tab2(2, placed("v2_w2", [P, CHUNK], U32))
                 elif c == 2:
-                    gather_tab2(3, tenant("ha02", "v2_w", [P, CHUNK], U32))
+                    gather_tab2(3, tenant("ha02", "v2_w3", [P, CHUNK], U32))
             if h == 1 and u % 2 == 0:
                 fill(2 if gathers else 1)
             if u % 2 == 1:
                 fill(1)
-        quantize_h(*units[-1])
-        wide.extend(out_banks(CHUNKS - 1, LAST_PIECES[-1][0]))
+        quantize_h(CHUNKS - 1, 1)
+        wide.extend(out_banks(CHUNKS - 1))
         fill(len(wide))

@@ -14,6 +14,7 @@ U8 = mybir.dt.uint8
 FP8X4 = mybir.dt.float8_e4m3fn_x4
 FP4X4 = mybir.dt.float4_e2m1fn_x4
 MULT = mybir.AluOpType.mult
+ADD = mybir.AluOpType.add
 GELU = mybir.ActivationFunctionType.Gelu_apprx_tanh
 
 P = 128
@@ -22,30 +23,30 @@ PASS = P * PACK
 QUADRANT = 32
 CHUNK = 512
 CHUNKS = J // CHUNK
+BLOCK = 256
 UNIT = 128
 UNITS = CHUNK // UNIT
-LIST_COLS = CHUNK // 16
 BANKS = 8
 TAB_ROWS_AT = 96
 TAB2_ROWS_AT = 32
 WB_ROW = 4
 EN_ROW = 4
-ALONE = 23
 LEAD = 2
-ROUNDED_TILES = 3
-H_TILES = 5
+RUNS = ((0, 2), (2, 3), (3, 4))
+ALONE = 24
+DELAY = 1
+EXTRA = (1, 2)
+SHARED_FROM = 1
+H_TILES = 6
 RESULT_TILES = 8
 
 PLACES = {
-    "wa00": 14, "tab2_w": 0, "both2": 16, "wb": 18,
-    "wa10": 23, "both3": 23, "picked2_0": 30.5,
-    "bias": 30.5,
-    "tab_s": 37, "wa01_0": 40, "wa01_1": 34,
-    "ha_first": 43,
-    "both0": 66, "wa11": 59,
-    "grouped11": 25, "picked2_1": 25, "wb_sorted_s": 26, "wb_sorted_w": 26.5,
-    "en": 17,
-    "v2_w2": 51,
+    "tab_w": 0, "result": 0,
+    "wa00": 16, "wa11": 16,
+    "wa10": 24, "tab_s": 32, "picked2_0": 17.5, "parted3": 16, "both3": 18, "picked3": 20, "picked2_1": 21, "rounded": 26,
+    "pair00": 38, "both2": 38,
+    "pair10": 40,
+    "grouped11": 43, "wb_sorted_w": 39.5, "wb_sorted_s": 44,
 }
 
 
@@ -65,15 +66,14 @@ def tile_list_kg_mul_gelu_kernel(
         def tenant(tag, name, shape, dtype):
             return keep.tile(shape, dtype, name=name, tag=tag, align_bytes=64)
 
-        def placed(name, shape, dtype):
-            return head.tile(shape, dtype, name=name, offset=int(1024 * PLACES[name]), align_bytes=64)
+        def placed(name, shape, dtype, bufs=1):
+            return head.tile(shape, dtype, name=name, offset=int(1024 * PLACES[name]), align_bytes=64, bufs=bufs)
 
         def words(dram):
             return dram.rearrange("p n i -> p (n i)").bitcast(I32)
 
-        def load_wa(name, a, h, c0, c1):
-            raw = placed(name, [P, PACK, c1 - c0], F32)
-            rows = wa[PASS * a : PASS * (a + 1), PASS * h + c0 : PASS * h + c1]
+        def load_wa(raw, a, h):
+            rows = wa[PASS * a : PASS * (a + 1), PASS * h : PASS * (h + 1)]
             nc.sync.dma_start(out=raw[:], in_=rows.rearrange("(p j) c -> p j c", j=PACK))
             return raw
 
@@ -81,45 +81,56 @@ def tile_list_kg_mul_gelu_kernel(
             return slice(CHUNK * c0, CHUNK * c1)
 
         def entries(lst, c0, c1):
-            return lst[:, LIST_COLS * c0 : LIST_COLS * c1]
-
-        def r_cols(h, t):
-            return slice(PASS * h + P * t, PASS * h + P * (t + 1))
+            return lst[:, CHUNK // 16 * c0 : CHUNK // 16 * c1]
 
         list1 = keep.tile([P, J // 16], U16, name="list1")
         list2 = keep.tile([P, J // 16], U16, name="list2")
-        tab_w = held("tab_w", [P, T], I32)
+        tab_w = placed("tab_w", [P, T], I32)
         tab_s = placed("tab_s", [P, T], U8)
         tab2_s = held("tab2_s", [P, T], U8)
+        tab2_w = held("tab2_w", [P, T], I32)
         v2_plane = held("v2_plane", [P, J], U8)
-        picked_s = held("picked_s", [P, J], U8)
-        v_planes = held("v_planes", [P, 2 * J], U8)
-        wa_w = held("wa_w", [P, 2, R], U32)
-        wa_s = held("wa_s", [P, 2, R], U8)
+        v_planes = [held("v_planes%d" % g, [P, 2, CHUNK * (c1 - c0)], U8) for g, (c0, c1) in enumerate(RUNS)]
+        wb = held("wb", [P, R + PASS // 4], I32)
+        en = held("en", [P, 2 * N + N // 4], I32)
+        wb_w = wb[:, :R]
+        wb_s = wb[:, R:].bitcast(U8)
+        en_w = en[:, : 2 * N].rearrange("p (a n) -> p a n", a=2)
+        en_s = en[:, 2 * N :].bitcast(U8)
 
         nc.vector.memset(tab_s[:TAB_ROWS_AT, :].bitcast(I32), 0)
         nc.vector.memset(tab2_s[:].bitcast(I32), 0)
-        for plane in (v_planes, v2_plane):
-            nc.gpsimd.memset(plane[:].bitcast(I32), 0)
+        for plane in v_planes:
+            nc.gpsimd.memset(plane[:].rearrange("p a j -> p (a j)").bitcast(I32), 0)
+        for plane in (v2_plane[:].bitcast(I32), wb[:, R:], en[:, 2 * N :]):
+            nc.gpsimd.memset(plane, 0)
         nc.sync.dma_start(list1[:], offs)
         nc.sync.dma_start(out=tab_s[TAB_ROWS_AT:, :].bitcast(I32), in_=tab_scales.rearrange("a q t -> q a t").bitcast(I32))
         nc.sync.dma_start(out=tab_w[:], in_=words(tab_words[0]))
-        raw00 = load_wa("wa00", 0, 0, 0, PASS)
-        raw10 = load_wa("wa10", 1, 0, 0, PASS)
-        nc.sync.dma_start(list2[:], offs2)
-        nc.sync.dma_start(out=tab2_s[TAB2_ROWS_AT : TAB2_ROWS_AT + 64 : 4, :].bitcast(I32), in_=tab2_scales[0].bitcast(I32))
+
+        def gather_tab_scales(c0, c1, picked):
+            nc.vector.tensor_copy(picked[:], tab_s[:].indirect(entries(list1, c0, c1)))
+            return picked
+
+        def carry_tab_scales(g, picked):
+            for q in range(4):
+                row = TAB_ROWS_AT + 8 * q
+                nc.sync.dma_start(
+                    out=v_planes[g][QUADRANT * q : QUADRANT * q + 4].rearrange("p a j -> p (a j)").bitcast(I32),
+                    in_=picked[row : row + 8, :].bitcast(I32),
+                )
 
         v_w = {}
         v2_w = {}
+        wa_q = {}
 
         def gather_tab(c, both):
             nc.vector.tensor_copy(both[:], tab_w[:].bitcast(U32).indirect(entries(list1, c, c + 1)))
             return both
 
-        def part_tab(c, both, parted):
-            nc.vector.tensor_copy(parted[:].bitcast(U16), both[:].bitcast(U16).rearrange("p (j d) -> p d j", d=2))
-            for a in range(2):
-                v_w[c, a] = parted[:, a, :]
+        def part_tab(c, both, make):
+            v_w[c] = make("parted%d" % c, [P, 2, 2 * CHUNK], U8)
+            nc.vector.tensor_copy(v_w[c][:].bitcast(U16), both[:].bitcast(U16).rearrange("p (j d) -> p d j", d=2))
 
         def gather_tab2_scales(c0, c1, picked):
             nc.vector.tensor_copy(picked[:], tab2_s[:].indirect(entries(list2, c0, c1)))
@@ -133,99 +144,105 @@ def tile_list_kg_mul_gelu_kernel(
             v2_w[c] = picked
             nc.vector.tensor_copy(picked[:], tab2_w[:].bitcast(U32).indirect(entries(list2, c, c + 1)))
 
-        def round_wa(copy, grouped, raw):
-            copy(grouped.rearrange("p (u v) m j -> p u m j v", v=2), raw.rearrange("p j (m u v) -> p u m j v", u=2, v=2))
+        def pair_views(grouped, raw, u):
+            return grouped.rearrange("p v m j -> p m j v"), raw.rearrange("p j (m u v) -> p u m j v", u=2, v=2)[:, u]
 
-        def round_pair(a, u, raw):
-            grouped = held("pair%d%d" % (a, u), [P, 2, P, PACK], BF16)
-            nc.scalar.copy(grouped[:].rearrange("p v m j -> p m j v"), raw.rearrange("p j (m u v) -> p u m j v", u=2, v=2)[:, u])
-            return grouped
+        def round_on_scalar(grouped, raw, u):
+            nc.scalar.copy(*pair_views(grouped, raw, u))
 
-        def quantize_wa(a, r0, grouped):
-            span = slice(r0, r0 + P * grouped.shape[1])
-            nc.vector.quantize_mx(
-                out=wa_w[:, a, span].bitcast(FP8X4), scales=wa_s[:, a, span], in_=grouped[:].rearrange("p t m j -> p (t m j)")
+        def round_on_vector(grouped, raw):
+            nc.vector.tensor_copy(
+                grouped.rearrange("p (u v) m j -> p u m j v", v=2), raw.rearrange("p j (m u v) -> p u m j v", u=2, v=2)
             )
+
+        def quantize_wa(a, h, u0, grouped):
+            slices = grouped.shape[1]
+            codes = held("wa_w%d%d%d" % (a, h, u0), [P, slices * P], U32)
+            plane = held("wa_s%d%d%d" % (a, h, u0), [P, slices * P], U8)
+            nc.vector.quantize_mx(out=codes[:].bitcast(FP8X4), scales=plane[:], in_=grouped[:].rearrange("p t m j -> p (t m j)"))
+            for i in range(slices):
+                wa_q[a, h, 2 * u0 + i] = (codes[:, P * i : P * (i + 1)], plane[:, P * i : P * (i + 1)])
 
         banks = [psum.tile([P, CHUNK], F32, name="bank%d" % i) for i in range(BANKS)]
-        emptied = [(i, "scalar") for i in range(BANKS)]
-        tied = set()
+        emptied = list(range(BANKS))
         ha = {}
         hb = {}
-        rounded = {}
+        copied = {}
         hq = {}
 
-        def free_for_hb():
-            untied = [entry for entry in emptied if entry[0] not in tied]
-            return untied + [entry for entry in emptied if entry[1] == "scalar"] + emptied
+        def take():
+            return emptied.pop(0)
 
-        def free_for_wide():
-            usable = [entry for entry in emptied if entry[0] in tied or not hb]
-            return [entry for entry in usable[:-1] if entry[1] == "vector"] + usable
+        def ha_passes(bank, h, u, k, a):
+            c = k // 2
+            g = max(c - 1, 0)
+            at = BLOCK * k - CHUNK * RUNS[g][0]
+            for v in range(2):
+                codes, plane = wa_q[a, h, 2 * u + v]
+                nc.tensor.matmul_mx(
+                    out=banks[bank][:, BLOCK * v : BLOCK * (v + 1)],
+                    lhsT=codes.bitcast(FP8X4),
+                    lhsT_scale=plane,
+                    rhs=v_w[c][:, a, 2 * BLOCK * (k % 2) : 2 * BLOCK * (k % 2 + 1)].bitcast(FP4X4),
+                    rhs_scale=v_planes[g][:, a, at : at + BLOCK],
+                    start=(a == 0 and v == 0),
+                    stop=(a == 1 and v == 1),
+                )
 
-        def take(free):
-            emptied.remove(free[0])
-            return free[0][0]
+        def copy_ha(bank, h, u, k):
+            c = k // 2
+            if (h, c) not in ha:
+                ha[h, c] = tenant("ha%d%d" % (h, c), "ha", [P, 2, CHUNK, 2], F32)
+            nc.scalar.copy(ha[h, c][:, u, BLOCK * (k % 2) : BLOCK * (k % 2 + 1), :], banks[bank][:].rearrange("p (v j) -> p j v", v=2))
+            emptied.append(bank)
 
-        def ha_pass(bank, h, c, t, a):
-            nc.tensor.matmul_mx(
-                out=banks[bank][:],
-                lhsT=wa_w[:, a, r_cols(h, t)].bitcast(FP8X4),
-                lhsT_scale=wa_s[:, a, r_cols(h, t)],
-                rhs=v_w[c, a].bitcast(FP4X4),
-                rhs_scale=v_planes[:, J * a + CHUNK * c : J * a + CHUNK * (c + 1)],
-                start=(a == 0),
-                stop=(a == 1),
-            )
+        def make_ha(h, u, k):
+            bank = take()
+            ha_passes(bank, h, u, k, 0)
+            ha_passes(bank, h, u, k, 1)
+            copy_ha(bank, h, u, k)
 
-        def copy_ha(bank, h, c, t):
-            nc.scalar.copy(ha[h, c][:, t, :], banks[bank][:])
-            emptied.append((bank, "scalar"))
-
-        def make_ha(h, c, t):
-            if t == 0:
-                ha[h, c] = tenant("ha%d%d" % (h, c), "ha", [P, PACK, CHUNK], F32)
-            bank = take(free_for_wide())
-            ha_pass(bank, h, c, t, 0)
-            ha_pass(bank, h, c, t, 1)
-            copy_ha(bank, h, c, t)
-
-        def make_hb(c, h, u):
-            hb[c, h, u] = take(free_for_hb())
+        def make_hb(c, h, w):
+            hb[c, h, w] = take()
             for t in range(PACK):
                 nc.tensor.matmul_mx(
-                    out=banks[hb[c, h, u]][:, UNIT * t : UNIT * (t + 1)],
-                    lhsT=wb_sorted_w[:, r_cols(h, t)].bitcast(FP8X4),
-                    lhsT_scale=wb_sorted_s[WB_ROW + 4 * h :, r_cols(0, t)],
-                    rhs=v2_w[c][:, UNIT * u : UNIT * (u + 1)].bitcast(FP8X4),
-                    rhs_scale=v2_plane[:, CHUNK * c + UNIT * u : CHUNK * c + UNIT * (u + 1)],
+                    out=banks[hb[c, h, w]][:, UNIT * t : UNIT * (t + 1)],
+                    lhsT=wb_sorted_w[:, PASS * h + P * t : PASS * h + P * (t + 1)].bitcast(FP8X4),
+                    lhsT_scale=wb_sorted_s[WB_ROW + 4 * h :, P * t : P * (t + 1)],
+                    rhs=v2_w[c][:, UNIT * w : UNIT * (w + 1)].bitcast(FP8X4),
+                    rhs_scale=v2_plane[:, CHUNK * c + UNIT * w : CHUNK * c + UNIT * (w + 1)],
                     start=True,
                     stop=True,
                 )
 
-        def make_h(c, h, u):
-            if u == 0:
-                rounded[c, h] = ring.tile([P, CHUNK, PACK], BF16, name="rounded", bufs=ROUNDED_TILES, align_bytes=64)
-            within = slice(UNIT * u, UNIT * (u + 1))
-            bank = hb[c, h, u]
-            nc.vector.tensor_tensor(
-                rounded[c, h][:, within, :].rearrange("p (g i) t -> p g t i", i=4),
-                banks[bank][:].rearrange("p (t g i) -> p g t i", t=PACK, i=4),
-                ha[h, c][:, :, within].rearrange("p t (g i) -> p g t i", i=4),
-                MULT,
-            )
-            emptied.append((bank, "vector"))
-            tied.add(bank)
+        def shared(c, h, w):
+            return 2 * c + h >= SHARED_FROM and w == (UNITS - 1) * (1 - h)
+
+        def copy_hb(c, h, w):
+            copied[c, h] = ring.tile([P, UNIT, PACK], F32, name="copied", bufs=2)
+            nc.scalar.copy(copied[c, h][:], banks[hb[c, h, w]][:].rearrange("p (t j) -> p j t", t=PACK))
+            emptied.append(hb[c, h, w])
+
+        def make_h(c, h, w):
+            slot = (UNITS - 1) * h + w
+            product = rounded[:, UNIT * slot : UNIT * (slot + 1), :].rearrange("p j (u v) -> p j u v", u=2)
+            factor = ha[h, c][:, :, UNIT * w : UNIT * (w + 1), :].rearrange("p u j v -> p j u v")
+            if shared(c, h, w):
+                nc.gpsimd.tensor_tensor(product, copied[c, h][:].rearrange("p j (u v) -> p j u v", u=2), factor, MULT)
+            else:
+                nc.vector.tensor_tensor(product, banks[hb[c, h, w]][:].rearrange("p (u v j) -> p j u v", u=2, v=2), factor, MULT)
+                emptied.append(hb[c, h, w])
 
         def quantize_h(c, h):
+            half = rounded[:, (CHUNK - UNIT) * h : (CHUNK - UNIT) * h + CHUNK, :]
             h_w = ring.tile([P, CHUNK], U32, name="h_w", bufs=H_TILES, align_bytes=64)
             h_s = ring.tile([P, CHUNK], U8, name="h_s", bufs=H_TILES, align_bytes=64)
-            nc.vector.quantize_mx(out=h_w[:].bitcast(FP8X4), scales=h_s[:], in_=rounded[c, h][:].rearrange("p j t -> p (j t)"))
+            nc.vector.quantize_mx(out=h_w[:].bitcast(FP8X4), scales=h_s[:], in_=half.rearrange("p j t -> p (j t)"))
             hq[c, h] = (h_w, h_s)
 
         def make_out(c, n):
-            bank = take(free_for_wide())
-            result = ring.tile([P, CHUNK], F32, name="result", bufs=RESULT_TILES)
+            bank = take()
+            result = placed("result", [P, CHUNK], F32, bufs=RESULT_TILES)
             for h in range(2):
                 nc.tensor.matmul_mx(
                     out=banks[bank][:],
@@ -238,57 +255,52 @@ def tile_list_kg_mul_gelu_kernel(
                 )
             nc.scalar.activation(result[:], banks[bank][:], GELU, bias=bias[:, n : n + 1])
             nc.sync.dma_start(out=out[P * n : P * (n + 1), cols(c, c + 1)], in_=result[:])
-            emptied.append((bank, "scalar"))
+            emptied.append(bank)
 
-        def out_banks(c):
-            return [(make_out, (c, n)) for n in range(N // P)]
-
-        nc.vector.tensor_copy(picked_s[:], tab_s[:].indirect(list1[:]))
-        for q in range(4):
-            row = TAB_ROWS_AT + 8 * q
-            nc.sync.dma_start(
-                out=v_planes[QUADRANT * q : QUADRANT * q + 4, :].bitcast(I32), in_=picked_s[row : row + 8, :].bitcast(I32)
-            )
-        raw01 = [load_wa("wa01_%d" % w, 0, 1, PASS // 2 * w, PASS // 2 * (w + 1)) for w in range(2)]
-
-        pairs = [[round_pair(a, u, raw[:]) for u in range(2)] for a, raw in enumerate((raw00, raw10))]
-        parted = [held("parted%d" % c, [P, 2, 2 * CHUNK], U8) for c in range(CHUNKS)]
-        both0 = gather_tab(0, placed("both0", [P, CHUNK], U32))
-        both1 = gather_tab(1, held("both1", [P, CHUNK], U32))
-        part_tab(0, both0, parted[0])
-        raw11 = load_wa("wa11", 1, 1, 0, PASS)
-        part_tab(1, both1, parted[1])
-        quantize_wa(0, 0, pairs[0][0])
-        quantize_wa(0, 2 * P, pairs[0][1])
-        both2 = gather_tab(2, placed("both2", [P, CHUNK], U32))
-        quantize_wa(1, 0, pairs[1][0])
-        part_tab(2, both2, parted[2])
-        quantize_wa(1, 2 * P, pairs[1][1])
-
-        wb = placed("wb", [P, R + PASS // 4], I32)
-        wb_w = wb[:, :R]
-        wb_s = wb[:, R:].bitcast(U8)
+        raw00 = load_wa(placed("wa00", [P, PACK, PASS], F32), 0, 0)
+        picked = gather_tab_scales(0, 3, held("picked", [P, 3 * CHUNK], U8))
+        carry_tab_scales(0, picked[:, cols(0, 2)])
+        raw10 = load_wa(placed("wa10", [P, PACK, PASS], F32), 1, 0)
+        carry_tab_scales(1, picked[:, cols(2, 3)])
+        raw01 = load_wa(held("wa01", [P, PACK, PASS], F32), 0, 1)
+        raw11 = load_wa(placed("wa11", [P, PACK, PASS], F32), 1, 1)
+        nc.sync.dma_start(list2[:], offs2)
+        nc.sync.dma_start(out=tab2_s[TAB2_ROWS_AT : TAB2_ROWS_AT + 64 : 4, :].bitcast(I32), in_=tab2_scales[0].bitcast(I32))
         nc.sync.dma_start(out=wb_w, in_=words(wb_words[0]))
-        nc.gpsimd.memset(wb_s.bitcast(I32), 0)
         for q in range(4):
             row = QUADRANT * q + WB_ROW
             nc.sync.dma_start(
                 out=wb[row : row + 8, R:], in_=wb_scales[0, 4 * q : 4 * q + 4, :].rearrange("s (h c) -> h s c", h=2).bitcast(I32)
             )
-        tab2_w = placed("tab2_w", [P, T], I32)
         nc.sync.dma_start(out=tab2_w[:], in_=words(tab2_words[0]))
 
-        both3 = gather_tab(3, placed("both3", [P, CHUNK], U32))
-        gather_tab2_scales(0, 1, placed("picked2_0", [P, CHUNK], U8))
-        part_tab(3, both3, parted[3])
-
+        pair = [P, 2, P, PACK]
+        pairs = {(0, 0): placed("pair00", pair, BF16), (0, 1): held("pair01", pair, BF16)}
+        pairs[1, 0] = placed("pair10", pair, BF16)
+        pairs[1, 1] = held("pair11", pair, BF16)
+        for a, raw in enumerate((raw00, raw10)):
+            for u in range(2):
+                round_on_scalar(pairs[a, u][:], raw[:], u)
+        both0 = gather_tab(0, held("both0", [P, CHUNK], U32))
+        both1 = gather_tab(1, held("both1", [P, CHUNK], U32))
+        part_tab(0, both0, held)
+        part_tab(1, both1, held)
+        quantize_wa(0, 0, 0, pairs[0, 0])
+        both2 = gather_tab(2, placed("both2", [P, CHUNK], U32))
+        quantize_wa(0, 0, 1, pairs[0, 1])
+        part_tab(2, both2, held)
+        quantize_wa(1, 0, 0, pairs[1, 0])
+        quantize_wa(1, 0, 1, pairs[1, 1])
         grouped01 = held("grouped01", [P, PACK, P, PACK], BF16)
-        for w, copy in enumerate((nc.scalar.copy, nc.vector.tensor_copy)):
-            round_wa(copy, grouped01[:, :, P // 2 * w : P // 2 * (w + 1), :], raw01[w][:])
         grouped11 = placed("grouped11", [P, PACK, P, PACK], BF16)
-        round_wa(nc.vector.tensor_copy, grouped11[:], raw11[:])
-        quantize_wa(0, PASS, grouped01)
-        quantize_wa(1, PASS, grouped11)
+        round_on_vector(grouped01[:], raw01[:])
+        quantize_wa(0, 1, 0, grouped01)
+        round_on_vector(grouped11[:], raw11[:])
+        quantize_wa(1, 1, 0, grouped11)
+        gather_tab2_scales(0, 1, placed("picked2_0", [P, CHUNK], U8))
+        gather_tab2_scales(1, 2, placed("picked2_1", [P, CHUNK], U8))
+        both3 = gather_tab(3, placed("both3", [P, CHUNK], U32))
+        carry_tab_scales(2, gather_tab_scales(3, CHUNKS, placed("picked3", [P, CHUNK], U8))[:])
 
         wb_sorted_w = placed("wb_sorted_w", [P, R], I32)
         wb_sorted_s = placed("wb_sorted_s", [P, PASS], U8)
@@ -298,65 +310,67 @@ def tile_list_kg_mul_gelu_kernel(
             nc.gpsimd.tensor_copy(
                 wb_sorted_w[:, half].rearrange("p (t m) -> p t m", t=PACK), wb_w[:, half].rearrange("p (m t) -> p t m", t=PACK)
             )
-        gather_tab2(0, held("v2_w0", [P, CHUNK], U32))
-        gather_tab2_scales(1, 3, placed("picked2_1", [P, 2 * CHUNK], U8))
 
-        en = placed("en", [P, 2 * N + N // 4], I32)
-        en_w = en[:, : 2 * N].rearrange("p (a n) -> p a n", a=2)
-        en_s = en[:, 2 * N :].bitcast(U8)
         nc.sync.dma_start(out=en_w, in_=en_words.rearrange("a p n i -> p a (n i)").bitcast(I32))
-        nc.gpsimd.memset(en_s.bitcast(I32), 0)
         for q in range(4):
             nc.sync.dma_start(
                 out=en[QUADRANT * q : QUADRANT * q + 2 * EN_ROW, 2 * N :], in_=en_scales[:, 4 * q : 4 * q + 4, :].bitcast(I32)
             )
-        bias = placed("bias", [P, N // P], F32)
+        bias = held("bias", [P, N // P], F32)
         with nc.allow_non_contiguous_dma(reason="one bias value for each partition and output tile"):
             nc.sync.dma_start(out=bias[:], in_=b.rearrange("(c p) -> p c", p=P))
-        gather_tab2(1, held("v2_w1", [P, CHUNK], U32))
 
-        ha_first = placed("ha_first", [P, 2, PACK, CHUNK], F32)
-        ha[0, 0] = ha_first[:, 0]
-        ha[0, 1] = ha_first[:, 1]
-        opened = [(take(free_for_wide()), 0, c, 2 * u + v) for u in range(2) for c in range(2) for v in range(2)]
+        gather_tab2(0, held("v2_w0", [P, CHUNK], U32))
+        part_tab(3, both3, placed)
+        gather_tab2(1, held("v2_w1", [P, CHUNK], U32))
+        rounded = placed("rounded", [P, 2 * CHUNK - UNIT, PACK], BF16)
+
+        opened = [(take(), 0, u, k) for u in range(2) for k in range(4)]
         for group in opened:
-            ha_pass(*group, 0)
+            ha_passes(*group, 0)
         for group in opened:
-            ha_pass(*group, 1)
+            ha_passes(*group, 1)
             copy_ha(*group)
 
-        wide = [(make_ha, (h, c, t)) for h in range(2) for c in range(CHUNKS) for t in range(PACK)][BANKS:]
+        wide = [(make_ha, (h, u, k)) for ks in (range(6), range(6, 8)) for h in range(2) for k in ks for u in range(2)][BANKS:]
 
         def fill(count):
             for step in range(count):
-                if wide and free_for_wide():
+                if wide:
                     make, args = wide.pop(0)
                     make(*args)
 
         fill(ALONE - BANKS)
-        units = [(c, h, u) for c in range(CHUNKS) for h in range(2) for u in range(UNITS)]
+        units = [(c, h, (w + h) % UNITS) for c in range(CHUNKS) for h in range(2) for w in range(UNITS)]
+        given = {(c, h): (c, h, w) for c, h, w in units if shared(c, h, w)}
+        units = [unit for unit in units if not shared(*unit)]
         for unit in units[:LEAD]:
             make_hb(*unit)
-        for i, (c, h, u) in enumerate(units):
-            gathers = 1 <= c < CHUNKS - 1
-            make_h(c, h, u)
+        since = {}
+        for i, (c, h, w) in enumerate(units):
+            first = i == 0 or units[i - 1][:2] != (c, h)
+            make_h(c, h, w)
             if i + LEAD < len(units):
-                make_hb(*units[i + LEAD])
-            if u == 0 and i > 0:
-                fill(1)
+                ahead = units[i + LEAD]
+                if ahead[:2] in given and given[ahead[:2]] not in hb:
+                    make_hb(*given[ahead[:2]])
+                    copy_hb(*given[ahead[:2]])
+                    fill(1)
+                make_hb(*ahead)
+            if first and i > 0:
                 quantize_h(*units[i - 1][:2])
-                if h == 0 and c == 1:
-                    gather_tab2_scales(3, CHUNKS, tenant("ha10", "picked2_3", [P, CHUNK], U8))
                 if h == 0:
-                    wide.extend(out_banks(c - 1))
-                elif c == 1:
-                    gather_tab2(2, placed("v2_w2", [P, CHUNK], U32))
-                elif c == 2:
-                    gather_tab2(3, tenant("ha02", "v2_w3", [P, CHUNK], U32))
-            if h == 1 and u % 2 == 0:
-                fill(2 if gathers else 1)
-            if u % 2 == 1:
-                fill(1)
+                    since[i + DELAY] = c - 1
+            if i in since:
+                wide.extend((make_out, (since[i], n)) for n in range(N // P))
+            if first and (c, h) in given:
+                make_h(*given[c, h])
+            if first and h == 0 and 1 <= c < CHUNKS - 1:
+                gather_tab2(c + 1, tenant("ha1%d" % (c - 1), "v2_w%d" % (c + 1), [P, CHUNK], U32))
+            if first and h == 1 and c < CHUNKS - 2:
+                gather_tab2_scales(c + 2, c + 3, tenant("ha0%d" % c, "picked2_%d" % (c + 2), [P, CHUNK], U8))
+            fill(2 if first and c in EXTRA else 1)
         quantize_h(CHUNKS - 1, 1)
-        wide.extend(out_banks(CHUNKS - 1))
+        fill(len(wide))
+        wide.extend((make_out, (CHUNKS - 1, n)) for n in range(N // P))
         fill(len(wide))

@@ -32,21 +32,25 @@ TAB2_ROWS_AT = 32
 WB_ROW = 4
 EN_ROW = 4
 LEAD = 2
-RUNS = ((0, 2), (2, 3), (3, 4))
+RUNS = ((0, 2), (2, 4))
 ALONE = 24
 DELAY = 1
 EXTRA = (1, 2)
 SHARED_FROM = 1
-H_TILES = 6
-RESULT_TILES = 8
+H_TILES = 8
+HA_AT = 70
+RESULTS_AT = ((0, 8), (54, 62), (70, 86), (102, 110))
 
 PLACES = {
-    "tab_w": 0, "result": 0,
+    "tab_w": 0,
+    "wa01": 54, "both0": 62, "both1": 64, "pair01": 66, "pair11": 68,
+    "v2_w2": 78, "picked2_3": 93.5, "v2_w3": 94,
     "wa00": 16, "wa11": 16,
-    "wa10": 24, "tab_s": 32, "picked2_0": 17.5, "parted3": 16, "both3": 18, "picked3": 20, "picked2_1": 21, "rounded": 26,
-    "pair00": 38, "both2": 38,
-    "pair10": 40,
-    "grouped11": 43, "wb_sorted_w": 39.5, "wb_sorted_s": 44,
+    "wa10": 24, "tab_s": 32, "rounded": 26,
+    "pair00": 38, "both2": 38, "pair10": 46, "both3": 46,
+    "late010": 40, "late011": 42, "late110": 44, "late111": 52,
+    "picked2_0": 17.5, "picked2_1": 18, "parted3": 16,
+    "wb_sorted_w": 48.5, "wb_sorted_s": 53,
 }
 
 
@@ -62,9 +66,6 @@ def tile_list_kg_mul_gelu_kernel(
 
         def held(name, shape, dtype):
             return keep.tile(shape, dtype, name=name, align_bytes=64)
-
-        def tenant(tag, name, shape, dtype):
-            return keep.tile(shape, dtype, name=name, tag=tag, align_bytes=64)
 
         def placed(name, shape, dtype, bufs=1):
             return head.tile(shape, dtype, name=name, offset=int(1024 * PLACES[name]), align_bytes=64, bufs=bufs)
@@ -134,6 +135,9 @@ def tile_list_kg_mul_gelu_kernel(
 
         def gather_tab2_scales(c0, c1, picked):
             nc.vector.tensor_copy(picked[:], tab2_s[:].indirect(entries(list2, c0, c1)))
+            return picked
+
+        def carry_tab2_scales(c0, c1, picked):
             for s in range(4):
                 nc.sync.dma_start(
                     out=v2_plane[s::QUADRANT, cols(c0, c1)].bitcast(I32),
@@ -150,10 +154,10 @@ def tile_list_kg_mul_gelu_kernel(
         def round_on_scalar(grouped, raw, u):
             nc.scalar.copy(*pair_views(grouped, raw, u))
 
-        def round_on_vector(grouped, raw):
-            nc.vector.tensor_copy(
-                grouped.rearrange("p (u v) m j -> p u m j v", v=2), raw.rearrange("p j (m u v) -> p u m j v", u=2, v=2)
-            )
+        def round_on_vector(a, u, raw):
+            grouped = placed("late%d1%d" % (a, u), [P, 2, P, PACK], BF16)
+            nc.vector.tensor_copy(*pair_views(grouped[:], raw, u))
+            return grouped
 
         def quantize_wa(a, h, u0, grouped):
             slices = grouped.shape[1]
@@ -175,7 +179,7 @@ def tile_list_kg_mul_gelu_kernel(
 
         def ha_passes(bank, h, u, k, a):
             c = k // 2
-            g = max(c - 1, 0)
+            g = c // 2
             at = BLOCK * k - CHUNK * RUNS[g][0]
             for v in range(2):
                 codes, plane = wa_q[a, h, 2 * u + v]
@@ -192,7 +196,7 @@ def tile_list_kg_mul_gelu_kernel(
         def copy_ha(bank, h, u, k):
             c = k // 2
             if (h, c) not in ha:
-                ha[h, c] = tenant("ha%d%d" % (h, c), "ha", [P, 2, CHUNK, 2], F32)
+                ha[h, c] = head.tile([P, 2, CHUNK, 2], F32, name="ha%d%d" % (h, c), offset=1024 * (HA_AT + 8 * (2 * c + h)), align_bytes=64)
             nc.scalar.copy(ha[h, c][:, u, BLOCK * (k % 2) : BLOCK * (k % 2 + 1), :], banks[bank][:].rearrange("p (v j) -> p j v", v=2))
             emptied.append(bank)
 
@@ -242,7 +246,7 @@ def tile_list_kg_mul_gelu_kernel(
 
         def make_out(c, n):
             bank = take()
-            result = placed("result", [P, CHUNK], F32, bufs=RESULT_TILES)
+            result = head.tile([P, CHUNK], F32, name="result%d%d" % (c, n), offset=1024 * (RESULTS_AT[c][n // 4] + 2 * (n % 4)), align_bytes=64)
             for h in range(2):
                 nc.tensor.matmul_mx(
                     out=banks[bank][:],
@@ -258,12 +262,29 @@ def tile_list_kg_mul_gelu_kernel(
             emptied.append(bank)
 
         raw00 = load_wa(placed("wa00", [P, PACK, PASS], F32), 0, 0)
-        picked = gather_tab_scales(0, 3, held("picked", [P, 3 * CHUNK], U8))
+        picked = gather_tab_scales(0, CHUNKS, held("picked", [P, J], U8))
         carry_tab_scales(0, picked[:, cols(0, 2)])
         raw10 = load_wa(placed("wa10", [P, PACK, PASS], F32), 1, 0)
-        carry_tab_scales(1, picked[:, cols(2, 3)])
-        raw01 = load_wa(held("wa01", [P, PACK, PASS], F32), 0, 1)
+        carry_tab_scales(1, picked[:, cols(2, 4)])
+        raw01 = load_wa(placed("wa01", [P, PACK, PASS], F32), 0, 1)
         raw11 = load_wa(placed("wa11", [P, PACK, PASS], F32), 1, 1)
+
+        pair = [P, 2, P, PACK]
+        pairs = {(0, 0): placed("pair00", pair, BF16), (0, 1): placed("pair01", pair, BF16)}
+        pairs[1, 0] = placed("pair10", pair, BF16)
+        pairs[1, 1] = placed("pair11", pair, BF16)
+        for a, raw in enumerate((raw00, raw10)):
+            for u in range(2):
+                round_on_scalar(pairs[a, u][:], raw[:], u)
+        both0 = gather_tab(0, placed("both0", [P, CHUNK], U32))
+        both1 = gather_tab(1, placed("both1", [P, CHUNK], U32))
+        part_tab(0, both0, held)
+        part_tab(1, both1, held)
+        quantize_wa(0, 0, 0, pairs[0, 0])
+        both2 = gather_tab(2, placed("both2", [P, CHUNK], U32))
+        quantize_wa(0, 0, 1, pairs[0, 1])
+        part_tab(2, both2, held)
+        quantize_wa(1, 0, 0, pairs[1, 0])
         nc.sync.dma_start(list2[:], offs2)
         nc.sync.dma_start(out=tab2_s[TAB2_ROWS_AT : TAB2_ROWS_AT + 64 : 4, :].bitcast(I32), in_=tab2_scales[0].bitcast(I32))
         nc.sync.dma_start(out=wb_w, in_=words(wb_words[0]))
@@ -274,33 +295,17 @@ def tile_list_kg_mul_gelu_kernel(
             )
         nc.sync.dma_start(out=tab2_w[:], in_=words(tab2_words[0]))
 
-        pair = [P, 2, P, PACK]
-        pairs = {(0, 0): placed("pair00", pair, BF16), (0, 1): held("pair01", pair, BF16)}
-        pairs[1, 0] = placed("pair10", pair, BF16)
-        pairs[1, 1] = held("pair11", pair, BF16)
-        for a, raw in enumerate((raw00, raw10)):
-            for u in range(2):
-                round_on_scalar(pairs[a, u][:], raw[:], u)
-        both0 = gather_tab(0, held("both0", [P, CHUNK], U32))
-        both1 = gather_tab(1, held("both1", [P, CHUNK], U32))
-        part_tab(0, both0, held)
-        part_tab(1, both1, held)
-        quantize_wa(0, 0, 0, pairs[0, 0])
-        both2 = gather_tab(2, placed("both2", [P, CHUNK], U32))
-        quantize_wa(0, 0, 1, pairs[0, 1])
-        part_tab(2, both2, held)
-        quantize_wa(1, 0, 0, pairs[1, 0])
-        quantize_wa(1, 0, 1, pairs[1, 1])
-        grouped01 = held("grouped01", [P, PACK, P, PACK], BF16)
-        grouped11 = placed("grouped11", [P, PACK, P, PACK], BF16)
-        round_on_vector(grouped01[:], raw01[:])
-        quantize_wa(0, 1, 0, grouped01)
-        round_on_vector(grouped11[:], raw11[:])
-        quantize_wa(1, 1, 0, grouped11)
-        gather_tab2_scales(0, 1, placed("picked2_0", [P, CHUNK], U8))
-        gather_tab2_scales(1, 2, placed("picked2_1", [P, CHUNK], U8))
         both3 = gather_tab(3, placed("both3", [P, CHUNK], U32))
-        carry_tab_scales(2, gather_tab_scales(3, CHUNKS, placed("picked3", [P, CHUNK], U8))[:])
+        quantize_wa(1, 0, 1, pairs[1, 1])
+        late = {(0, u): round_on_vector(0, u, raw01[:]) for u in range(2)}
+        quantize_wa(0, 1, 0, late[0, 0])
+        late[1, 0] = round_on_vector(1, 0, raw11[:])
+        quantize_wa(0, 1, 1, late[0, 1])
+        quantize_wa(1, 1, 0, late[1, 0])
+        late[1, 1] = round_on_vector(1, 1, raw11[:])
+        carry_tab2_scales(0, 1, gather_tab2_scales(0, 1, placed("picked2_0", [P, CHUNK], U8)))
+        quantize_wa(1, 1, 1, late[1, 1])
+        picked2_1 = gather_tab2_scales(1, 3, placed("picked2_1", [P, 2 * CHUNK], U8))
 
         wb_sorted_w = placed("wb_sorted_w", [P, R], I32)
         wb_sorted_s = placed("wb_sorted_s", [P, PASS], U8)
@@ -312,6 +317,7 @@ def tile_list_kg_mul_gelu_kernel(
             )
 
         nc.sync.dma_start(out=en_w, in_=en_words.rearrange("a p n i -> p a (n i)").bitcast(I32))
+        carry_tab2_scales(1, 3, picked2_1)
         for q in range(4):
             nc.sync.dma_start(
                 out=en[QUADRANT * q : QUADRANT * q + 2 * EN_ROW, 2 * N :], in_=en_scales[:, 4 * q : 4 * q + 4, :].bitcast(I32)
@@ -332,7 +338,9 @@ def tile_list_kg_mul_gelu_kernel(
             ha_passes(*group, 1)
             copy_ha(*group)
 
-        wide = [(make_ha, (h, u, k)) for ks in (range(6), range(6, 8)) for h in range(2) for k in ks for u in range(2)][BANKS:]
+        wide = [(make_ha, (0, u, k)) for u in range(2) for k in range(4, 6)]
+        wide.extend((make_ha, (1, u, k)) for u in range(2) for k in range(6))
+        wide.extend((make_ha, (h, u, k)) for h in range(2) for u in range(2) for k in range(6, 8))
 
         def fill(count):
             for step in range(count):
@@ -366,9 +374,10 @@ def tile_list_kg_mul_gelu_kernel(
             if first and (c, h) in given:
                 make_h(*given[c, h])
             if first and h == 0 and 1 <= c < CHUNKS - 1:
-                gather_tab2(c + 1, tenant("ha1%d" % (c - 1), "v2_w%d" % (c + 1), [P, CHUNK], U32))
-            if first and h == 1 and c < CHUNKS - 2:
-                gather_tab2_scales(c + 2, c + 3, tenant("ha0%d" % c, "picked2_%d" % (c + 2), [P, CHUNK], U8))
+                gather_tab2(c + 1, placed("v2_w%d" % (c + 1), [P, CHUNK], U32))
+            if first and (c, h) == (1, 1):
+                picked2 = placed("picked2_3", [P, CHUNK], U8)
+                carry_tab2_scales(c + 2, c + 3, gather_tab2_scales(c + 2, c + 3, picked2))
             fill(2 if first and c in EXTRA else 1)
         quantize_h(CHUNKS - 1, 1)
         fill(len(wide))

@@ -23,7 +23,6 @@ PASS = P * PACK
 QUADRANT = 32
 CHUNK = 512
 CHUNKS = J // CHUNK
-BLOCK = 256
 UNIT = 128
 UNITS = CHUNK // UNIT
 BANKS = 8
@@ -177,34 +176,31 @@ def tile_list_kg_mul_gelu_kernel(
         def take():
             return emptied.pop(0)
 
-        def ha_passes(bank, h, u, k, a):
-            c = k // 2
+        def ha_pass(bank, h, t, c, a):
             g = c // 2
-            at = BLOCK * k - CHUNK * RUNS[g][0]
-            for v in range(2):
-                codes, plane = wa_q[a, h, 2 * u + v]
-                nc.tensor.matmul_mx(
-                    out=banks[bank][:, BLOCK * v : BLOCK * (v + 1)],
-                    lhsT=codes.bitcast(FP8X4),
-                    lhsT_scale=plane,
-                    rhs=v_w[c][:, a, 2 * BLOCK * (k % 2) : 2 * BLOCK * (k % 2 + 1)].bitcast(FP4X4),
-                    rhs_scale=v_planes[g][:, a, at : at + BLOCK],
-                    start=(a == 0 and v == 0),
-                    stop=(a == 1 and v == 1),
-                )
+            at = CHUNK * (c - RUNS[g][0])
+            codes, plane = wa_q[a, h, t]
+            nc.tensor.matmul_mx(
+                out=banks[bank][:],
+                lhsT=codes.bitcast(FP8X4),
+                lhsT_scale=plane,
+                rhs=v_w[c][:, a, :].bitcast(FP4X4),
+                rhs_scale=v_planes[g][:, a, at : at + CHUNK],
+                start=(a == 0),
+                stop=(a == 1),
+            )
 
-        def copy_ha(bank, h, u, k):
-            c = k // 2
+        def copy_ha(bank, h, t, c):
             if (h, c) not in ha:
-                ha[h, c] = head.tile([P, 2, CHUNK, 2], F32, name="ha%d%d" % (h, c), offset=1024 * (HA_AT + 8 * (2 * c + h)), align_bytes=64)
-            nc.scalar.copy(ha[h, c][:, u, BLOCK * (k % 2) : BLOCK * (k % 2 + 1), :], banks[bank][:].rearrange("p (v j) -> p j v", v=2))
+                ha[h, c] = head.tile([P, PACK, CHUNK], F32, name="ha%d%d" % (h, c), offset=1024 * (HA_AT + 8 * (2 * c + h)), align_bytes=64)
+            nc.scalar.copy(ha[h, c][:, t, :], banks[bank][:])
             emptied.append(bank)
 
-        def make_ha(h, u, k):
+        def make_ha(h, t, c):
             bank = take()
-            ha_passes(bank, h, u, k, 0)
-            ha_passes(bank, h, u, k, 1)
-            copy_ha(bank, h, u, k)
+            ha_pass(bank, h, t, c, 0)
+            ha_pass(bank, h, t, c, 1)
+            copy_ha(bank, h, t, c)
 
         def make_hb(c, h, w):
             hb[c, h, w] = take()
@@ -229,12 +225,17 @@ def tile_list_kg_mul_gelu_kernel(
 
         def make_h(c, h, w):
             slot = (UNITS - 1) * h + w
-            product = rounded[:, UNIT * slot : UNIT * (slot + 1), :].rearrange("p j (u v) -> p j u v", u=2)
-            factor = ha[h, c][:, :, UNIT * w : UNIT * (w + 1), :].rearrange("p u j v -> p j u v")
+            product = rounded[:, UNIT * slot : UNIT * (slot + 1), :]
+            factor = ha[h, c][:, :, UNIT * w : UNIT * (w + 1)]
             if shared(c, h, w):
-                nc.gpsimd.tensor_tensor(product, copied[c, h][:].rearrange("p j (u v) -> p j u v", u=2), factor, MULT)
+                nc.gpsimd.tensor_tensor(product, copied[c, h][:], factor.rearrange("p t j -> p j t"), MULT)
             else:
-                nc.vector.tensor_tensor(product, banks[hb[c, h, w]][:].rearrange("p (u v j) -> p j u v", u=2, v=2), factor, MULT)
+                nc.vector.tensor_tensor(
+                    product.rearrange("p (g i) t -> p g t i", i=4),
+                    banks[hb[c, h, w]][:].rearrange("p (t g i) -> p g t i", t=PACK, i=4),
+                    factor.rearrange("p t (g i) -> p g t i", i=4),
+                    MULT,
+                )
                 emptied.append(hb[c, h, w])
 
         def quantize_h(c, h):
@@ -331,16 +332,16 @@ def tile_list_kg_mul_gelu_kernel(
         gather_tab2(1, held("v2_w1", [P, CHUNK], U32))
         rounded = placed("rounded", [P, 2 * CHUNK - UNIT, PACK], BF16)
 
-        opened = [(take(), 0, u, k) for u in range(2) for k in range(4)]
+        opened = [(take(), 0, 2 * u + v, c) for u in range(2) for c in range(2) for v in range(2)]
         for group in opened:
-            ha_passes(*group, 0)
+            ha_pass(*group, 0)
         for group in opened:
-            ha_passes(*group, 1)
+            ha_pass(*group, 1)
             copy_ha(*group)
 
-        wide = [(make_ha, (0, u, k)) for u in range(2) for k in range(4, 6)]
-        wide.extend((make_ha, (1, u, k)) for u in range(2) for k in range(6))
-        wide.extend((make_ha, (h, u, k)) for h in range(2) for u in range(2) for k in range(6, 8))
+        wide = [(make_ha, (0, t, 2)) for t in range(PACK)]
+        wide.extend((make_ha, (1, 2 * u + v, c)) for u in range(2) for c in range(3) for v in range(2))
+        wide.extend((make_ha, (h, t, 3)) for h in range(2) for t in range(PACK))
 
         def fill(count):
             for step in range(count):

@@ -46,10 +46,10 @@ PLACES = {
     "v2_w2": 78, "picked2_3": 93.5, "v2_w3": 94,
     "wa00": 16, "wa11": 16,
     "wa10": 24, "tab_s": 32, "rounded": 26,
-    "pair00": 38, "both2": 38, "pair10": 46, "both3": 46,
-    "late010": 40, "late011": 42, "late110": 44, "late111": 52,
-    "picked2_0": 17.5, "picked2_1": 18, "parted3": 16,
-    "wb_sorted_w": 48.5, "wb_sorted_s": 53,
+    "pair00": 38, "both2": 38, "pair10": 50, "both3": 50,
+    "late010": 40, "late011": 42, "late110": 44, "late111": 44,
+    "picked2_0": 17.5, "parted3": 16,
+    "wb_sorted_w": 45.5, "wb_sorted_s": 45,
 }
 
 
@@ -186,8 +186,8 @@ def tile_list_kg_mul_gelu_kernel(
                 lhsT_scale=plane,
                 rhs=v_w[c][:, a, :].bitcast(FP4X4),
                 rhs_scale=v_planes[g][:, a, at : at + CHUNK],
-                start=(a == 0),
-                stop=(a == 1),
+                start=(a == h),
+                stop=(a != h),
             )
 
         def copy_ha(bank, h, t, c):
@@ -198,8 +198,8 @@ def tile_list_kg_mul_gelu_kernel(
 
         def make_ha(h, t, c):
             bank = take()
-            ha_pass(bank, h, t, c, 0)
-            ha_pass(bank, h, t, c, 1)
+            ha_pass(bank, h, t, c, h)
+            ha_pass(bank, h, t, c, 1 - h)
             copy_ha(bank, h, t, c)
 
         def make_hb(c, h, w):
@@ -248,15 +248,15 @@ def tile_list_kg_mul_gelu_kernel(
         def make_out(c, n):
             bank = take()
             result = head.tile([P, CHUNK], F32, name="result%d%d" % (c, n), offset=1024 * (RESULTS_AT[c][n // 4] + 2 * (n % 4)), align_bytes=64)
-            for h in range(2):
+            for h in (1, 0):
                 nc.tensor.matmul_mx(
                     out=banks[bank][:],
                     lhsT=en_w[:, h, P * n : P * (n + 1)].bitcast(FP8X4),
                     lhsT_scale=en_s[EN_ROW * h :, P * n : P * (n + 1)],
                     rhs=hq[c, h][0][:].bitcast(FP8X4),
                     rhs_scale=hq[c, h][1][:],
-                    start=(h == 0),
-                    stop=(h == 1),
+                    start=(h == 1),
+                    stop=(h == 0),
                 )
             nc.scalar.activation(result[:], banks[bank][:], GELU, bias=bias[:, n : n + 1])
             nc.sync.dma_start(out=out[P * n : P * (n + 1), cols(c, c + 1)], in_=result[:])
@@ -300,13 +300,12 @@ def tile_list_kg_mul_gelu_kernel(
         quantize_wa(1, 0, 1, pairs[1, 1])
         late = {(0, u): round_on_vector(0, u, raw01[:]) for u in range(2)}
         quantize_wa(0, 1, 0, late[0, 0])
-        late[1, 0] = round_on_vector(1, 0, raw11[:])
         quantize_wa(0, 1, 1, late[0, 1])
+        late[1, 0] = round_on_vector(1, 0, raw11[:])
         quantize_wa(1, 1, 0, late[1, 0])
         late[1, 1] = round_on_vector(1, 1, raw11[:])
-        carry_tab2_scales(0, 1, gather_tab2_scales(0, 1, placed("picked2_0", [P, CHUNK], U8)))
         quantize_wa(1, 1, 1, late[1, 1])
-        picked2_1 = gather_tab2_scales(1, 3, placed("picked2_1", [P, 2 * CHUNK], U8))
+        picked2_0 = gather_tab2_scales(0, 3, placed("picked2_0", [P, 3 * CHUNK], U8))
 
         wb_sorted_w = placed("wb_sorted_w", [P, R], I32)
         wb_sorted_s = placed("wb_sorted_s", [P, PASS], U8)
@@ -318,7 +317,7 @@ def tile_list_kg_mul_gelu_kernel(
             )
 
         nc.sync.dma_start(out=en_w, in_=en_words.rearrange("a p n i -> p a (n i)").bitcast(I32))
-        carry_tab2_scales(1, 3, picked2_1)
+        carry_tab2_scales(0, 3, picked2_0)
         for q in range(4):
             nc.sync.dma_start(
                 out=en[QUADRANT * q : QUADRANT * q + 2 * EN_ROW, 2 * N :], in_=en_scales[:, 4 * q : 4 * q + 4, :].bitcast(I32)

@@ -48,7 +48,7 @@ PLACES = {
     "wa10": 24, "tab_s": 32, "rounded": 26,
     "pair00": 38, "both2": 38, "pair10": 50, "both3": 50,
     "late010": 40, "late011": 42, "late110": 44, "late111": 44,
-    "picked2_0": 17.5, "parted3": 16,
+    "picked2_0": 17.5, "picked2_1": 18, "parted3": 16,
     "wb_sorted_w": 45.5, "wb_sorted_s": 45,
 }
 
@@ -305,7 +305,8 @@ def tile_list_kg_mul_gelu_kernel(
         quantize_wa(1, 1, 0, late[1, 0])
         late[1, 1] = round_on_vector(1, 1, raw11[:])
         quantize_wa(1, 1, 1, late[1, 1])
-        picked2_0 = gather_tab2_scales(0, 3, placed("picked2_0", [P, 3 * CHUNK], U8))
+        carry_tab2_scales(0, 1, gather_tab2_scales(0, 1, placed("picked2_0", [P, CHUNK], U8)))
+        picked2_1 = gather_tab2_scales(1, 3, placed("picked2_1", [P, 2 * CHUNK], U8))
 
         wb_sorted_w = placed("wb_sorted_w", [P, R], I32)
         wb_sorted_s = placed("wb_sorted_s", [P, PASS], U8)
@@ -317,7 +318,7 @@ def tile_list_kg_mul_gelu_kernel(
             )
 
         nc.sync.dma_start(out=en_w, in_=en_words.rearrange("a p n i -> p a (n i)").bitcast(I32))
-        carry_tab2_scales(0, 3, picked2_0)
+        carry_tab2_scales(1, 3, picked2_1)
         for q in range(4):
             nc.sync.dma_start(
                 out=en[QUADRANT * q : QUADRANT * q + 2 * EN_ROW, 2 * N :], in_=en_scales[:, 4 * q : 4 * q + 4, :].bitcast(I32)

@@ -104,6 +104,9 @@ def tile_list_kg_mul_gelu_kernel(
             nc.gpsimd.memset(plane[:].rearrange("p a j -> p (a j)").bitcast(I32), 0)
         for plane in (v2_plane[:].bitcast(I32), wb[:, R:], en[:, 2 * N :]):
             nc.gpsimd.memset(plane, 0)
+        column = held("column", [P, 2], F32)
+        nc.vector.memset(column[:, 0:1], 0.0)
+        nc.scalar.activation(column[:, 1:2], column[:, 0:1], GELU)
         nc.sync.dma_start(list1[:], offs)
         nc.sync.dma_start(out=tab_s[TAB_ROWS_AT:, :].bitcast(I32), in_=tab_scales.rearrange("a q t -> q a t").bitcast(I32))
         nc.sync.dma_start(out=tab_w[:], in_=words(tab_words[0]))

from contextlib import ExitStack

import concourse.mybir as mybir

K, L, R, N, T, J = 1024, 512, 1024, 1024, 4096, 2048
FLOPS = 2 * J * (K * R + L * R + R * N)

F32 = mybir.dt.float32
BF16 = mybir.dt.bfloat16
I32 = mybir.dt.int32
U32 = mybir.dt.uint32
U16 = mybir.dt.uint16
U8 = mybir.dt.uint8
FP8X4 = mybir.dt.float8_e4m3fn_x4
FP4X4 = mybir.dt.float4_e2m1fn_x4
MULT = mybir.AluOpType.mult
ADD = mybir.AluOpType.add
GELU = mybir.ActivationFunctionType.Gelu_apprx_tanh

P = 128
PACK = 4
PASS = P * PACK
QUADRANT = 32
CHUNK = 512
CHUNKS = J // CHUNK
UNIT = 128
UNITS = CHUNK // UNIT
BANKS = 8
TAB_ROWS_AT = 96
TAB2_ROWS_AT = 32
WB_ROW = 4
EN_ROW = 4
LEAD = 2
RUNS = ((0, 2), (2, 4))
ALONE = 24
DELAY = 1
EXTRA = (1, 2)
SHARED_FROM = 1
H_TILES = 8
HA_AT = 70
RESULTS_AT = ((0, 8), (54, 62), (70, 86), (102, 110))

PLACES = {
    "tab_w": 0,
    "wa01": 54, "both0": 62, "both1": 64, "pair01": 66, "pair11": 68,
    "v2_w2": 78, "picked2_3": 93.5, "v2_w3": 94,
    "wa00": 16, "wa11": 16,
    "wa10": 24, "tab_s": 32, "rounded": 26,
    "pair00": 38, "both2": 38, "pair10": 50, "both3": 50,
    "late010": 40, "late011": 42, "late110": 44, "late111": 44,
    "picked2_0": 17.5, "picked2_1": 18, "parted3": 16,
    "wb_sorted_w": 45.5, "wb_sorted_s": 45,
}


def tile_list_kg_mul_gelu_kernel(
    tc, tab_words, tab_scales, tab2_words, tab2_scales, wa, wb_words, wb_scales, en_words, en_scales, b, offs, offs2, out
):
    nc = tc.nc
    with ExitStack() as ctx:
        keep = ctx.enter_context(tc.tile_pool(name="keep", bufs=1))
        head = ctx.enter_context(tc.tile_pool(name="head", bufs=1))
        ring = ctx.enter_context(tc.tile_pool(name="ring", bufs=2))
        psum = ctx.enter_context(tc.psum_pool(name="psum", bufs=1))

        def held(name, shape, dtype):
            return keep.tile(shape, dtype, name=name, align_bytes=64)

        def placed(name, shape, dtype, bufs=1):
            return head.tile(shape, dtype, name=name, offset=int(1024 * PLACES[name]), align_bytes=64, bufs=bufs)

        def words(dram):
            return dram.rearrange("p n i -> p (n i)").bitcast(I32)

        def load_wa(raw, a, h):
            rows = wa[PASS * a : PASS * (a + 1), PASS * h : PASS * (h + 1)]
            nc.sync.dma_start(out=raw[:], in_=rows.rearrange("(p j) c -> p j c", j=PACK))
            return raw

        def cols(c0, c1):
            return slice(CHUNK * c0, CHUNK * c1)

        def entries(lst, c0, c1):
            return lst[:, CHUNK // 16 * c0 : CHUNK // 16 * c1]

        list1 = keep.tile([P, J // 16], U16, name="list1")
        list2 = keep.tile([P, J // 16], U16, name="list2")
        tab_w = placed("tab_w", [P, T], I32)
        tab_s = placed("tab_s", [P, T], U8)
        tab2_s = held("tab2_s", [P, T], U8)
        tab2_w = held("tab2_w", [P, T], I32)
        v2_plane = held("v2_plane", [P, J], U8)
        v_planes = [held("v_planes%d" % g, [P, 2, CHUNK * (c1 - c0)], U8) for g, (c0, c1) in enumerate(RUNS)]
        wb = held("wb", [P, R + PASS // 4], I32)
        en = held("en", [P, 2 * N + N // 4], I32)
        wb_w = wb[:, :R]
        wb_s = wb[:, R:].bitcast(U8)
        en_w = en[:, : 2 * N].rearrange("p (a n) -> p a n", a=2)
        en_s = en[:, 2 * N :].bitcast(U8)

        nc.vector.memset(tab_s[:TAB_ROWS_AT, :].bitcast(I32), 0)
        nc.vector.memset(tab2_s[:].bitcast(I32), 0)
        for plane in v_planes:
            nc.gpsimd.memset(plane[:].rearrange("p a j -> p (a j)").bitcast(I32), 0)
        for plane in (v2_plane[:].bitcast(I32), wb[:, R:], en[:, 2 * N :]):
            nc.gpsimd.memset(plane, 0)
        column = held("column", [P, 2], F32)
        nc.vector.memset(column[:, 0:1], 0.0)
        nc.scalar.activation(column[:, 1:2], column[:, 0:1], GELU)
        nc.sync.dma_start(list1[:], offs)
        nc.sync.dma_start(out=tab_s[TAB_ROWS_AT:, :].bitcast(I32), in_=tab_scales.rearrange("a q t -> q a t").bitcast(I32))
        nc.sync.dma_start(out=tab_w[:], in_=words(tab_words[0]))

        def gather_tab_scales(c0, c1, picked):
            nc.vector.tensor_copy(picked[:], tab_s[:].indirect(entries(list1, c0, c1)))
            return picked

        def carry_tab_scales(g, picked):
            for q in range(4):
                row = TAB_ROWS_AT + 8 * q
                nc.sync.dma_start(
                    out=v_planes[g][QUADRANT * q : QUADRANT * q + 4].rearrange("p a j -> p (a j)").bitcast(I32),
                    in_=picked[row : row + 8, :].bitcast(I32),
                )

        v_w = {}
        v2_w = {}
        wa_q = {}

        def gather_tab(c, both):
            nc.vector.tensor_copy(both[:], tab_w[:].bitcast(U32).indirect(entries(list1, c, c + 1)))
            return both

        def part_tab(c, both, make):
            v_w[c] = make("parted%d" % c, [P, 2, 2 * CHUNK], U8)
            nc.vector.tensor_copy(v_w[c][:].bitcast(U16), both[:].bitcast(U16).rearrange("p (j d) -> p d j", d=2))

        def gather_tab2_scales(c0, c1, picked):
            nc.vector.tensor_copy(picked[:], tab2_s[:].indirect(entries(list2, c0, c1)))
            return picked

        def carry_tab2_scales(c0, c1, picked):
            for s in range(4):
                nc.sync.dma_start(
                    out=v2_plane[s::QUADRANT, cols(c0, c1)].bitcast(I32),
                    in_=picked[TAB2_ROWS_AT + 4 * s : TAB2_ROWS_AT + 64 : 16, :].bitcast(I32),
                )

        def gather_tab2(c, picked):
            v2_w[c] = picked
            nc.vector.tensor_copy(picked[:], tab2_w[:].bitcast(U32).indirect(entries(list2, c, c + 1)))

        def pair_views(grouped, raw, u):
            return grouped.rearrange("p v m j -> p m j v"), raw.rearrange("p j (m u v) -> p u m j v", u=2, v=2)[:, u]

        def round_on_scalar(grouped, raw, u):
            nc.scalar.copy(*pair_views(grouped, raw, u))

        def round_on_vector(a, u, raw):
            grouped = placed("late%d1%d" % (a, u), [P, 2, P, PACK], BF16)
            nc.vector.tensor_copy(*pair_views(grouped[:], raw, u))
            return grouped

        def quantize_wa(a, h, u0, grouped):
            slices = grouped.shape[1]
            codes = held("wa_w%d%d%d" % (a, h, u0), [P, slices * P], U32)
            plane = held("wa_s%d%d%d" % (a, h, u0), [P, slices * P], U8)
            nc.vector.quantize_mx(out=codes[:].bitcast(FP8X4), scales=plane[:], in_=grouped[:].rearrange("p t m j -> p (t m j)"))
            for i in range(slices):
                wa_q[a, h, 2 * u0 + i] = (codes[:, P * i : P * (i + 1)], plane[:, P * i : P * (i + 1)])

        banks = [psum.tile([P, CHUNK], F32, name="bank%d" % i) for i in range(BANKS)]
        emptied = list(range(BANKS))
        ha = {}
        hb = {}
        copied = {}
        hq = {}

        def take():
            return emptied.pop(0)

        def ha_pass(bank, h, t, c, a):
            g = c // 2
            at = CHUNK * (c - RUNS[g][0])
            codes, plane = wa_q[a, h, t]
            nc.tensor.matmul_mx(
                out=banks[bank][:],
                lhsT=codes.bitcast(FP8X4),
                lhsT_scale=plane,
                rhs=v_w[c][:, a, :].bitcast(FP4X4),
                rhs_scale=v_planes[g][:, a, at : at + CHUNK],
                start=(a == h),
                stop=(a != h),
            )

        def copy_ha(bank, h, t, c):
            if (h, c) not in ha:
                ha[h, c] = head.tile([P, PACK, CHUNK], F32, name="ha%d%d" % (h, c), offset=1024 * (HA_AT + 8 * (2 * c + h)), align_bytes=64)
            nc.scalar.copy(ha[h, c][:, t, :], banks[bank][:])
            emptied.append(bank)

        def make_ha(h, t, c):
            bank = take()
            ha_pass(bank, h, t, c, h)
            ha_pass(bank, h, t, c, 1 - h)
            copy_ha(bank, h, t, c)

        def make_hb(c, h, w):
            hb[c, h, w] = take()
            for t in range(PACK):
                nc.tensor.matmul_mx(
                    out=banks[hb[c, h, w]][:, UNIT * t : UNIT * (t + 1)],
                    lhsT=wb_sorted_w[:, PASS * h + P * t : PASS * h + P * (t + 1)].bitcast(FP8X4),
                    lhsT_scale=wb_sorted_s[WB_ROW + 4 * h :, P * t : P * (t + 1)],
                    rhs=v2_w[c][:, UNIT * w : UNIT * (w + 1)].bitcast(FP8X4),
                    rhs_scale=v2_plane[:, CHUNK * c + UNIT * w : CHUNK * c + UNIT * (w + 1)],
                    start=True,
                    stop=True,
                )

        def shared(c, h, w):
            return 2 * c + h >= SHARED_FROM and w == (UNITS - 1) * (1 - h)

        def copy_hb(c, h, w):
            copied[c, h] = ring.tile([P, UNIT, PACK], F32, name="copied", bufs=2)
            nc.scalar.copy(copied[c, h][:], banks[hb[c, h, w]][:].rearrange("p (t j) -> p j t", t=PACK))
            emptied.append(hb[c, h, w])

        def make_h(c, h, w):
            slot = (UNITS - 1) * h + w
            product = rounded[:, UNIT * slot : UNIT * (slot + 1), :]
            factor = ha[h, c][:, :, UNIT * w : UNIT * (w + 1)]
            if shared(c, h, w):
                nc.gpsimd.tensor_tensor(product, copied[c, h][:], factor.rearrange("p t j -> p j t"), MULT)
            else:
                nc.vector.tensor_tensor(
                    product.rearrange("p (g i) t -> p g t i", i=4),
                    banks[hb[c, h, w]][:].rearrange("p (t g i) -> p g t i", t=PACK, i=4),
                    factor.rearrange("p t (g i) -> p g t i", i=4),
                    MULT,
                )
                emptied.append(hb[c, h, w])

        def quantize_h(c, h):
            half = rounded[:, (CHUNK - UNIT) * h : (CHUNK - UNIT) * h + CHUNK, :]
            h_w = ring.tile([P, CHUNK], U32, name="h_w", bufs=H_TILES, align_bytes=64)
            h_s = ring.tile([P, CHUNK], U8, name="h_s", bufs=H_TILES, align_bytes=64)
            nc.vector.quantize_mx(out=h_w[:].bitcast(FP8X4), scales=h_s[:], in_=half.rearrange("p j t -> p (j t)"))
            hq[c, h] = (h_w, h_s)

        def make_out(c, n):
            bank = take()
            result = head.tile([P, CHUNK], F32, name="result%d%d" % (c, n), offset=1024 * (RESULTS_AT[c][n // 4] + 2 * (n % 4)), align_bytes=64)
            for h in (1, 0):
                nc.tensor.matmul_mx(
                    out=banks[bank][:],
                    lhsT=en_w[:, h, P * n : P * (n + 1)].bitcast(FP8X4),
                    lhsT_scale=en_s[EN_ROW * h :, P * n : P * (n + 1)],
                    rhs=hq[c, h][0][:].bitcast(FP8X4),
                    rhs_scale=hq[c, h][1][:],
                    start=(h == 1),
                    stop=(h == 0),
                )
            nc.scalar.activation(result[:], banks[bank][:], GELU, bias=bias[:, n : n + 1])
            nc.sync.dma_start(out=out[P * n : P * (n + 1), cols(c, c + 1)], in_=result[:])
            emptied.append(bank)

        raw00 = load_wa(placed("wa00", [P, PACK, PASS], F32), 0, 0)
        picked = gather_tab_scales(0, CHUNKS, held("picked", [P, J], U8))
        carry_tab_scales(0, picked[:, cols(0, 2)])
        raw10 = load_wa(placed("wa10", [P, PACK, PASS], F32), 1, 0)
        carry_tab_scales(1, picked[:, cols(2, 4)])
        raw01 = load_wa(placed("wa01", [P, PACK, PASS], F32), 0, 1)
        raw11 = load_wa(placed("wa11", [P, PACK, PASS], F32), 1, 1)

        pair = [P, 2, P, PACK]
        pairs = {(0, 0): placed("pair00", pair, BF16), (0, 1): placed("pair01", pair, BF16)}
        pairs[1, 0] = placed("pair10", pair, BF16)
        pairs[1, 1] = placed("pair11", pair, BF16)
        for a, raw in enumerate((raw00, raw10)):
            for u in range(2):
                round_on_scalar(pairs[a, u][:], raw[:], u)
        both0 = gather_tab(0, placed("both0", [P, CHUNK], U32))
        both1 = gather_tab(1, placed("both1", [P, CHUNK], U32))
        part_tab(0, both0, held)
        part_tab(1, both1, held)
        quantize_wa(0, 0, 0, pairs[0, 0])
        both2 = gather_tab(2, placed("both2", [P, CHUNK], U32))
        quantize_wa(0, 0, 1, pairs[0, 1])
        part_tab(2, both2, held)
        quantize_wa(1, 0, 0, pairs[1, 0])
        nc.sync.dma_start(list2[:], offs2)
        nc.sync.dma_start(out=tab2_s[TAB2_ROWS_AT : TAB2_ROWS_AT + 64 : 4, :].bitcast(I32), in_=tab2_scales[0].bitcast(I32))
        nc.sync.dma_start(out=wb_w, in_=words(wb_words[0]))
        for q in range(4):
            row = QUADRANT * q + WB_ROW
            nc.sync.dma_start(
                out=wb[row : row + 8, R:], in_=wb_scales[0, 4 * q : 4 * q + 4, :].rearrange("s (h c) -> h s c", h=2).bitcast(I32)
            )
        nc.sync.dma_start(out=tab2_w[:], in_=words(tab2_words[0]))

        both3 = gather_tab(3, placed("both3", [P, CHUNK], U32))
        quantize_wa(1, 0, 1, pairs[1, 1])
        late = {(0, u): round_on_vector(0, u, raw01[:]) for u in range(2)}
        quantize_wa(0, 1, 0, late[0, 0])
        quantize_wa(0, 1, 1, late[0, 1])
        late[1, 0] = round_on_vector(1, 0, raw11[:])
        quantize_wa(1, 1, 0, late[1, 0])
        late[1, 1] = round_on_vector(1, 1, raw11[:])
        quantize_wa(1, 1, 1, late[1, 1])
        carry_tab2_scales(0, 1, gather_tab2_scales(0, 1, placed("picked2_0", [P, CHUNK], U8)))
        picked2_1 = gather_tab2_scales(1, 3, placed("picked2_1", [P, 2 * CHUNK], U8))

        wb_sorted_w = placed("wb_sorted_w", [P, R], I32)
        wb_sorted_s = placed("wb_sorted_s", [P, PASS], U8)
        nc.gpsimd.tensor_copy(wb_sorted_s[:].rearrange("p (t m) -> p t m", t=PACK), wb_s.rearrange("p (m t) -> p t m", t=PACK))
        for h in range(2):
            half = slice(PASS * h, PASS * (h + 1))
            nc.gpsimd.tensor_copy(
                wb_sorted_w[:, half].rearrange("p (t m) -> p t m", t=PACK), wb_w[:, half].rearrange("p (m t) -> p t m", t=PACK)
            )

        nc.sync.dma_start(out=en_w, in_=en_words.rearrange("a p n i -> p a (n i)").bitcast(I32))
        carry_tab2_scales(1, 3, picked2_1)
        for q in range(4):
            nc.sync.dma_start(
                out=en[QUADRANT * q : QUADRANT * q + 2 * EN_ROW, 2 * N :], in_=en_scales[:, 4 * q : 4 * q + 4, :].bitcast(I32)
            )
        bias = held("bias", [P, N // P], F32)
        with nc.allow_non_contiguous_dma(reason="one bias value for each partition and output tile"):
            nc.sync.dma_start(out=bias[:], in_=b.rearrange("(c p) -> p c", p=P))

        gather_tab2(0, held("v2_w0", [P, CHUNK], U32))
        part_tab(3, both3, placed)
        gather_tab2(1, held("v2_w1", [P, CHUNK], U32))
        rounded = placed("rounded", [P, 2 * CHUNK - UNIT, PACK], BF16)

        opened = [(take(), 0, 2 * u + v, c) for u in range(2) for c in range(2) for v in range(2)]
        for group in opened:
            ha_pass(*group, 0)
        for group in opened:
            ha_pass(*group, 1)
            copy_ha(*group)

        wide = [(make_ha, (0, t, 2)) for t in range(PACK)]
        wide.extend((make_ha, (1, 2 * u + v, c)) for u in range(2) for c in range(3) for v in range(2))
        wide.extend((make_ha, (h, t, 3)) for h in range(2) for t in range(PACK))

        def fill(count):
            for step in range(count):
                if wide:
                    make, args = wide.pop(0)
                    make(*args)

        fill(ALONE - BANKS)
        units = [(c, h, (w + h) % UNITS) for c in range(CHUNKS) for h in range(2) for w in range(UNITS)]
        given = {(c, h): (c, h, w) for c, h, w in units if shared(c, h, w)}
        units = [unit for unit in units if not shared(*unit)]
        for unit in units[:LEAD]:
            make_hb(*unit)
        since = {}
        for i, (c, h, w) in enumerate(units):
            first = i == 0 or units[i - 1][:2] != (c, h)
            make_h(c, h, w)
            if i + LEAD < len(units):
                ahead = units[i + LEAD]
                if ahead[:2] in given and given[ahead[:2]] not in hb:
                    make_hb(*given[ahead[:2]])
                    copy_hb(*given[ahead[:2]])
                    fill(1)
                make_hb(*ahead)
            if first and i > 0:
                quantize_h(*units[i - 1][:2])
                if h == 0:
                    since[i + DELAY] = c - 1
            if i in since:
                wide.extend((make_out, (since[i], n)) for n in range(N // P))
            if first and (c, h) in given:
                make_h(*given[c, h])
            if first and h == 0 and 1 <= c < CHUNKS - 1:
                gather_tab2(c + 1, placed("v2_w%d" % (c + 1), [P, CHUNK], U32))
            if first and (c, h) == (1, 1):
                picked2 = placed("picked2_3", [P, CHUNK], U8)
                carry_tab2_scales(c + 2, c + 3, gather_tab2_scales(c + 2, c + 3, picked2))
            fill(2 if first and c in EXTRA else 1)
        quantize_h(CHUNKS - 1, 1)
        fill(len(wide))
        wide.extend((make_out, (CHUNKS - 1, n)) for n in range(N // P))
        fill(len(wide))
